import numpy as np
import ml_dtypes


def mxq(x, axis, fmt="e4m3"):
    dtype, down = {"e4m3": (ml_dtypes.float8_e4m3fn, 7), "e5m2": (ml_dtypes.float8_e5m2, 14)}[fmt]
    v = np.moveaxis(np.asarray(x, np.float32).astype(ml_dtypes.bfloat16).astype(np.float64), axis, -1)
    blocks = v.reshape(v.shape[:-1] + (-1, 32))
    amax = np.abs(blocks).max(-1, keepdims=True)
    byte = np.maximum(np.where(amax > 0, np.frexp(amax)[1] - 1 + 127, 0) - down, 1)
    scale = np.exp2(byte - 127.0)
    codes = (blocks / scale).astype(np.float32).astype(dtype).astype(np.float64)
    return np.moveaxis((codes * scale).reshape(v.shape), -1, axis)


WIDE = False


def mx_kscale(k):
    if not WIDE:
        return np.ones(k)
    levels = np.array([10, -10, 5, -5, 0])
    if k % 512:
        return np.exp2(np.random.permutation(np.resize(levels, k // 32))).repeat(32)
    a = np.empty((k // 512, 16))
    for p in range(k // 512):
        a[p, :8] = np.random.permutation(np.resize(levels, 8))
        for g in range(8):
            far = levels[np.abs(levels - a[p, g]) >= 10]
            a[p, g + 8] = far[np.random.randint(len(far))]
    return np.exp2(a.ravel()).repeat(32)


def f64(x):
    return np.asarray(x).astype(np.float64)


def striped(idx):
    return np.tile(idx.reshape(-1, 16).T, (8, 1)).astype(np.uint16)


def unstriped(offs):
    return offs[:16].T.reshape(-1).astype(np.int64)


E2M1 = np.array([0.0, 0.5, 1.0, 1.5, 2.0, 3.0, 4.0, 6.0, -0.0, -0.5, -1.0, -1.5, -2.0, -3.0, -4.0, -6.0])


def pack_weight(w, fmt):
    k, n = w.shape
    w = f64(np.asarray(w, np.float32).astype(ml_dtypes.bfloat16)).reshape(k // 32, 32, n)
    amax = np.abs(w).max(1)
    if fmt == "e4m3":
        byte = np.frexp(amax)[1] - 1 + 127 - 7
    else:
        mant, ex = np.frexp(amax / 6.0)
        byte = np.where(mant > 0.5, ex, ex - 1) + 127
    byte = np.clip(np.where(amax > 0, byte, 1), 1, 254)
    scaled = (w * np.exp2(127.0 - byte)[:, None, :]).reshape(k, n).astype(np.float32)
    by_word = np.ascontiguousarray(scaled.reshape(k // 512, 128, 4, n).transpose(0, 1, 3, 2))
    if fmt == "e4m3":
        words = by_word.astype(ml_dtypes.float8_e4m3fn).view(np.uint8)
    else:
        c = by_word.astype(ml_dtypes.float4_e2m1fn).view(np.uint8) & 0xF
        words = (c[..., 0::2] | (c[..., 1::2] << 4)).reshape(k // 512, 128, 2 * n)
    return np.ascontiguousarray(words), np.ascontiguousarray(byte.astype(np.uint8).reshape(k // 512, 16, n))


def unpack_weight(words, scales, fmt):
    g, _, n = scales.shape
    words = np.ascontiguousarray(words).reshape(g, 128, n, -1)
    if fmt == "e4m3":
        vals = words.view(ml_dtypes.float8_e4m3fn).astype(np.float64)
    else:
        nib = np.empty((g, 128, n, 4), np.uint8)
        nib[..., 0::2] = words & 0xF
        nib[..., 1::2] = words >> 4
        vals = E2M1[nib]
    vals = vals * np.repeat(np.exp2(scales.astype(np.float64) - 127.0), 8, axis=1)[..., None]
    return vals.transpose(0, 1, 3, 2).reshape(g * 512, n)


def gelu(v):
    return 0.5 * v * (1.0 + np.tanh(np.sqrt(2.0 / np.pi) * (v + 0.044715 * v**3)))


K, T, S, H, N = 1024, 2048, 1024, 1024, 512

def setup_inputs():
    n = np.random.standard_normal
    s = mx_kscale(K)[:, None]
    u = mx_kscale(H)[:, None]
    tab_words, tab_scales = pack_weight(n((K, T)) * s, "e4m3")
    offs = striped(np.random.permutation(T)[:S])
    wa = (n((K, H)) / np.sqrt(K) / s).astype(np.float32)
    wb_words, wb_scales = pack_weight(n((K, H)) / np.sqrt(K) / s * u.T, "e2m1")
    wo = (n((H, N)) / np.sqrt(H) / u).astype(np.float32)
    gT = np.exp(0.3 * n((H, T))).astype(np.float32)
    return {"tab_words": tab_words, "tab_scales": tab_scales, "offs": offs,
            "wa": wa, "wb_words": wb_words, "wb_scales": wb_scales,
            "wo": wo, "gT": gT}

def reference(tab_words, tab_scales, offs, wa, wb_words, wb_scales, wo, gT):
    v = unpack_weight(tab_words, tab_scales, "e4m3")[:, unstriped(offs)]
    g = f64(gT)[:, unstriped(offs)]
    qa = mxq(f64(wa), 0, "e4m3")
    qb = unpack_weight(wb_words, wb_scales, "e2m1")
    A = qa.T @ v
    B = qb.T @ v
    h = np.log(1.0 + np.exp(A)) * B * g
    qh = mxq(h, 0, "e4m3")
    qo = mxq(f64(wo), 0, "e4m3")
    return qo.T @ qh

@@ -1,0 +1,305 @@
+from contextlib import ExitStack
+
+import concourse.mybir as mybir
+
+K, T, S, H, N = 1024, 2048, 1024, 1024, 512
+FLOPS = 2 * (2 * K * H * S + H * N * S)
+
+F32 = mybir.dt.float32
+BF16 = mybir.dt.bfloat16
+I32 = mybir.dt.int32
+U32 = mybir.dt.uint32
+U16 = mybir.dt.uint16
+U8 = mybir.dt.uint8
+E4M3 = mybir.dt.float8_e4m3fn_x4
+E2M1 = mybir.dt.float4_e2m1fn_x4
+MULT = mybir.AluOpType.mult
+MAX = mybir.AluOpType.max
+SIGMOID = mybir.ActivationFunctionType.Sigmoid
+LN = mybir.ActivationFunctionType.Ln
+
+P = 128
+PACK = 4
+PASS = P * PACK
+HALF = 512
+BLOCK = 128
+FLOOR = 1e-12
+
+
+def tile_list_softplus_step_input_kernel(
+    tc, tab_words, tab_scales, offs, wa, wb_words, wb_scales, wo, gT, out
+):
+    nc = tc.nc
+    with ExitStack() as ctx:
+        lists = ctx.enter_context(tc.tile_pool(name="lists", bufs=1))
+        keep = ctx.enter_context(tc.tile_pool(name="keep", bufs=1))
+        ring = ctx.enter_context(tc.tile_pool(name="ring", bufs=2))
+        psum = ctx.enter_context(tc.psum_pool(name="psum", bufs=1))
+
+        def held(shape, dtype, name):
+            return keep.tile(shape, dtype, name=name, align_bytes=64)
+
+        offsets = lists.tile([P, S // 16], U16, name="offsets")
+        nc.sync.dma_start(offsets[:], offs)
+
+        def half_offsets(half):
+            return offsets[:, half * (HALF // 16) : (half + 1) * (HALF // 16)]
+
+        tab_planes = held([P, T], U8, "tab_planes")
+        moved_plane = held([P, S], U8, "moved_plane")
+        wb_planes = held([P, 2, H], U8, "wb_planes")
+        nc.vector.memset(tab_planes[:].bitcast(I32), 0)
+        nc.vector.memset(wb_planes[:].rearrange("p a c -> p (a c)").bitcast(I32), 0)
+        nc.vector.memset(moved_plane[:].bitcast(I32), 0)
+        warm = held([P, 1], F32, "warm")
+        nc.vector.memset(warm[:], 0.0)
+        nc.scalar.activation(warm[:], warm[:], SIGMOID, scale=-1.0)
+
+        def load_rows(src, slot):
+            raw = held([P, PACK, HALF], F32, slot)
+            nc.sync.dma_start(raw[:], src.rearrange("(p j) c -> p j c", j=PACK))
+            return raw
+
+        def load_wa(b, a):
+            return load_rows(wa[a * PASS : (a + 1) * PASS, b * PASS : (b + 1) * PASS], "raw%d%d" % (b, a))
+
+        for q in range(4):
+            nc.gpsimd.dma_start(
+                tab_planes[32 * q : 32 * q + 8, :].bitcast(I32),
+                tab_scales[:, 4 * q : 4 * q + 4, :].bitcast(I32),
+            )
+        for q in range(4):
+            nc.gpsimd.dma_start(
+                wb_planes[32 * q : 32 * q + 4, :, :].bitcast(I32),
+                wb_scales[:, 4 * q : 4 * q + 4, :].rearrange("a r c -> r a c").bitcast(I32),
+            )
+        table = []
+        for a in range(2):
+            words = held([P, T], I32, "table%d" % a)
+            nc.sync.dma_start(words[:], tab_words[a].rearrange("p t i -> p (t i)").bitcast(I32))
+            table.append(words)
+        wa_raw = {}
+        for a in range(2):
+            wa_raw[0, a] = load_wa(0, a)
+        wb_raw = held([P, 2, H // 2], I32, "wb_raw")
+        nc.sync.dma_start(wb_raw[:], wb_words.rearrange("a p w -> p a w").bitcast(I32))
+        for a in range(2):
+            wa_raw[1, a] = load_wa(1, a)
+        g_rows = gT.rearrange("(b m t e) n -> b t e m n", m=P // 4, t=PACK, e=4)
+        wo_rows = wo.rearrange("(b m t e) n -> b e m t n", m=P // 4, t=PACK, e=4)
+        factors = {}
+
+        def load_factors(b):
+            for t in range(PACK):
+                rows = held([P, T], F32, "factors%d%d" % (b, t))
+                for e in range(4):
+                    nc.sync.dma_start(rows[e:P:4, :], g_rows[b, t, e])
+                factors[b, t] = rows
+
+        load_factors(0)
+        wo_raw = []
+        for b in range(2):
+            raw = held([P, PACK, N], F32, "wo_raw%d" % b)
+            for e in range(4):
+                nc.sync.dma_start(raw[e:P:4, :, :], wo_rows[b, e])
+            wo_raw.append(raw)
+        load_factors(1)
+
+        picked = {}
+        for a in range(2):
+            for half in range(2):
+                words = held([P, HALF], U32, "picked%d%d" % (a, half))
+                nc.vector.tensor_copy(words[:], table[a][:].bitcast(U32).indirect(half_offsets(half)))
+                picked[a, half] = words
+        picked_planes = held([P, S], U8, "table0")
+        nc.vector.tensor_copy(picked_planes[:], tab_planes[:].indirect(offsets[:]))
+        for q in range(4):
+            nc.gpsimd.dma_start(
+                moved_plane[32 * q : 32 * q + 4, :].bitcast(I32),
+                picked_planes[32 * q + 4 : 32 * q + 8, :].bitcast(I32),
+            )
+
+        wa_codes, wa_planes = {}, {}
+        rounded_slots = [["rounded00", "rounded01"], ["rounded01", "raw10"]]
+
+        def quantise(rounded, name):
+            width = rounded.shape[1] // PACK
+            codes = held([P, width], U32, name + "_codes")
+            plane = held([P, width], U8, name + "_plane")
+            nc.vector.quantize_mx(out=codes[:].bitcast(E4M3), scales=plane[:], in_=rounded)
+            return codes, plane
+
+        def prepare_wa(b, a, copies):
+            rounded = held([P, PACK * PASS], BF16, rounded_slots[b][a])
+            dealt = rounded[:].rearrange("p (t m e j) -> p m t j e", t=PACK, e=4, j=PACK)
+            source = wa_raw[b, a][:].rearrange("p j (m t e) -> p m t j e", t=PACK, e=4)
+            share = (P // 4) // len(copies)
+            for n, copy in enumerate(copies):
+                copy(dealt[:, n * share : (n + 1) * share], source[:, n * share : (n + 1) * share])
+            wa_codes[b, a], wa_planes[b, a] = quantise(rounded[:], "wa%d%d" % (b, a))
+
+        prepare_wa(0, 0, [nc.scalar.copy])
+        prepare_wa(0, 1, [nc.scalar.copy, nc.vector.tensor_copy])
+
+        wb_dealt = []
+
+        def deal_wb():
+            codes = held([P, 4, PACK, P // 4, 2], I32, "raw11")
+            planes = held([P, 4, PACK, P], U8, "rounded01")
+            nc.vector.tensor_copy(
+                codes[:],
+                wb_raw[:].rearrange("p a (b m t w) -> p (a b) t m w", b=2, t=PACK, w=2),
+            )
+            nc.vector.tensor_copy(
+                planes[:].bitcast(I32),
+                wb_planes[:].bitcast(I32).rearrange("p a (b m t) -> p (a b) t m", b=2, t=PACK),
+            )
+            wb_dealt.extend([codes, planes])
+
+        def steps_before_guard(b, half):
+            cols = slice(half * HALF, (half + 1) * HALF)
+            banks = [psum.tile([P, HALF], F32, name="sum_bank", bufs=6) for t in range(PACK)]
+            order = [(t, a) for t in range(PACK) for a in range(2)]
+            if (b, half) == (0, 0):
+                order = [(t, a) for a in range(2) for t in range(PACK)]
+            for t, a in order:
+                nc.tensor.matmul_mx(
+                    out=banks[t][:],
+                    lhsT=wa_codes[b, a][:, t * P : (t + 1) * P].bitcast(E4M3),
+                    lhsT_scale=wa_planes[b, a][:, t * P : (t + 1) * P],
+                    rhs=picked[a, half][:].bitcast(E4M3),
+                    rhs_scale=picked_planes[4 * a : P, cols],
+                    start=(a == 0),
+                    stop=(a == 1),
+                )
+            logs = ring.tile([P, 2, PACK, HALF // 2], F32, name="logs", bufs=2)
+            for t in range(PACK):
+                nc.scalar.activation(
+                    logs[:, :, t, :], banks[t][:].rearrange("p (u n) -> p u n", u=2), SIGMOID, scale=-1.0
+                )
+            for u in range(2):
+                nc.scalar.activation(logs[:, u], logs[:, u], LN, bias=FLOOR)
+            return banks, logs
+
+        phases = [(b, half) for b in range(2) for half in range(2)]
+        pending = steps_before_guard(*phases[0])
+
+        for a in range(2):
+            prepare_wa(1, a, [nc.vector.tensor_copy])
+        deal_wb()
+
+        wo_quantised = []
+
+        def round_wo(b):
+            raw = wo_raw[b]
+            rounded = held([P, PACK * N], BF16, "picked%d0" % b)
+            for piece in range(4):
+                cols = slice(piece * P, (piece + 1) * P)
+                nc.scalar.copy(
+                    rounded[:].rearrange("p (n j) -> p n j", j=PACK)[:, cols, :].rearrange(
+                        "p (c i) j -> p c j i", i=2
+                    ),
+                    raw[:, :, cols].rearrange("p j (c i) -> p c j i", i=2),
+                )
+            wo_quantised.append(quantise(rounded[:], "wo%d" % b))
+
+        h_quantised = {}
+        out_rows = out.rearrange("(c p) s -> p c s", p=P)
+
+        def project(half, block):
+            bank = psum.tile([P, N // P, BLOCK], F32, name="sum_bank", bufs=6)
+            for c in range(N // P):
+                for b in range(2):
+                    w_codes, w_plane = wo_quantised[b]
+                    h_codes, h_plane = h_quantised[b, half, block]
+                    nc.tensor.matmul_mx(
+                        out=bank[:, c, :],
+                        lhsT=w_codes[:, c * P : (c + 1) * P].bitcast(E4M3),
+                        lhsT_scale=w_plane[:, c * P : (c + 1) * P],
+                        rhs=h_codes.bitcast(E4M3),
+                        rhs_scale=h_plane,
+                        start=(b == 0),
+                        stop=(b == 1),
+                    )
+            result = ring.tile([P, N // P, BLOCK], F32, name="result", bufs=4)
+            nc.scalar.copy(result[:], bank[:])
+            first = half * HALF + block * BLOCK
+            nc.sync.dma_start(out_rows[:, :, first : first + BLOCK], result[:])
+
+        for index, (b, half) in enumerate(phases):
+            banks, logs = pending
+            steps = keep.tile([P, PACK, HALF], F32, name="work%d" % (index % 2))
+            if index == 0:
+                for u in range(2):
+                    cols = slice(u * (HALF // 2), (u + 1) * (HALF // 2))
+                    for t in range(PACK):
+                        nc.vector.scalar_tensor_tensor(
+                            steps[:, t, cols], logs[:, u, t, :], -1.0, banks[t][:, cols], MULT, MAX
+                        )
+            else:
+                for t in range(PACK):
+                    nc.vector.scalar_tensor_tensor(
+                        steps[:, t, :].rearrange("p (u n) -> p u n", u=2),
+                        logs[:, :, t, :],
+                        -1.0,
+                        banks[t][:].rearrange("p (u n) -> p u n", u=2),
+                        MULT,
+                        MAX,
+                    )
+            if index + 1 < len(phases):
+                pending = steps_before_guard(*phases[index + 1])
+            if index == 3:
+                round_wo(0)
+                round_wo(1)
+                for block in range(HALF // BLOCK):
+                    project(0, block)
+
+            scaled = keep.tile([P, PACK, HALF], F32, name="work%d" % ((index + 1) % 2))
+
+            def scale_steps(t, first, count):
+                entries = offsets[:, (half * HALF + first) // 16 : (half * HALF + first + count) // 16]
+                nc.vector.tensor_tensor(
+                    scaled[:, t, first : first + count],
+                    factors[b, t][:].indirect(entries),
+                    steps[:, t, first : first + count],
+                    MULT,
+                )
+
+            for t in range(2):
+                scale_steps(t, 0, HALF)
+            h_rounded = ring.tile([P, HALF, PACK], BF16, name="h_rounded", bufs=2, align_bytes=64)
+            for block in range(HALF // BLOCK):
+                if block % 2 == 0:
+                    for t in range(2, PACK):
+                        scale_steps(t, block * BLOCK, 2 * BLOCK)
+                cols = slice(block * BLOCK, (block + 1) * BLOCK)
+                list_cols = slice(half * HALF + block * BLOCK, half * HALF + (block + 1) * BLOCK)
+                bank = psum.tile([P, PACK, BLOCK], F32, name="b_bank", bufs=2)
+                for t in range(PACK):
+                    for a in range(2):
+                        nc.tensor.matmul_mx(
+                            out=bank[:, t, :],
+                            lhsT=wb_dealt[0][:, 2 * a + b, t].rearrange("p m w -> p (m w)").bitcast(U8).bitcast(E2M1),
+                            lhsT_scale=wb_dealt[1][:, 2 * a + b, t, :],
+                            rhs=picked[a, half][:, cols].bitcast(E4M3),
+                            rhs_scale=(picked_planes, moved_plane)[a][:, list_cols],
+                            start=(a == 0),
+                            stop=(a == 1),
+                        )
+                nc.vector.tensor_tensor(
+                    h_rounded[:, cols, :].rearrange("p (c i) t -> p c t i", i=2),
+                    bank[:].rearrange("p t (c i) -> p c t i", i=2),
+                    scaled[:, :, cols].rearrange("p t (c i) -> p c t i", i=2),
+                    MULT,
+                )
+                if index == 3:
+                    codes, plane = quantise(
+                        h_rounded[:, cols, :].rearrange("p n t -> p (n t)"), "h%d%d%d" % (b, half, block)
+                    )
+                    h_quantised[b, half, block] = (codes[:], plane[:])
+                    project(1, block)
+            if index < 3:
+                codes, plane = quantise(h_rounded[:].rearrange("p n t -> p (n t)"), "h%d%d" % (b, half))
+                for block in range(HALF // BLOCK):
+                    cols = slice(block * BLOCK, (block + 1) * BLOCK)
+                    h_quantised[b, half, block] = (codes[:, cols], plane[:, cols])

@@ -55,13 +55,16 @@ def tile_list_softplus_step_input_kernel(
         nc.vector.memset(warm[:], 0.0)
         nc.scalar.activation(warm[:], warm[:], SIGMOID, scale=-1.0)
 
-        def load_rows(src, slot):
-            raw = held([P, PACK, HALF], F32, slot)
-            nc.sync.dma_start(raw[:], src.rearrange("(p j) c -> p j c", j=PACK))
-            return raw
-
-        def load_wa(b, a):
-            return load_rows(wa[a * PASS : (a + 1) * PASS, b * PASS : (b + 1) * PASS], "raw%d%d" % (b, a))
+        def load_wa(b, a, pieces):
+            width = PASS // pieces
+            tiles = []
+            for n in range(pieces):
+                raw = held([P, PACK, width], F32, "raw%d%d%d" % (b, a, n))
+                first = b * PASS + n * width
+                rows = wa[a * PASS : (a + 1) * PASS, first : first + width]
+                nc.sync.dma_start(raw[:], rows.rearrange("(p j) c -> p j c", j=PACK))
+                tiles.append(raw)
+            return tiles
 
         for q in range(4):
             nc.gpsimd.dma_start(
@@ -80,11 +83,10 @@ def tile_list_softplus_step_input_kernel(
             table.append(words)
         wa_raw = {}
         for a in range(2):
-            wa_raw[0, a] = load_wa(0, a)
+            wa_raw[0, a] = load_wa(0, a, 2)
         wb_raw = held([P, 2, H // 2], I32, "wb_raw")
         nc.sync.dma_start(wb_raw[:], wb_words.rearrange("a p w -> p a w").bitcast(I32))
-        for a in range(2):
-            wa_raw[1, a] = load_wa(1, a)
+        wa_raw[1, 0] = load_wa(1, 0, 1)
         g_rows = gT.rearrange("(b m t e) n -> b t e m n", m=P // 4, t=PACK, e=4)
         wo_rows = wo.rearrange("(b m t e) n -> b e m t n", m=P // 4, t=PACK, e=4)
         factors = {}
@@ -97,6 +99,7 @@ def tile_list_softplus_step_input_kernel(
                 factors[b, t] = rows
 
         load_factors(0)
+        wa_raw[1, 1] = load_wa(1, 1, 2)
         wo_raw = []
         for b in range(2):
             raw = held([P, PACK, N], F32, "wo_raw%d" % b)
@@ -120,31 +123,33 @@ def tile_list_softplus_step_input_kernel(
             )
 
         wa_codes, wa_planes = {}, {}
-        rounded_slots = [["rounded00", "rounded01"], ["rounded01", "raw10"]]
 
-        def quantise(rounded, name):
+        def quantise(rounded, name, slot=None):
             width = rounded.shape[1] // PACK
-            codes = held([P, width], U32, name + "_codes")
+            codes = held([P, width], U32, slot or name + "_codes")
             plane = held([P, width], U8, name + "_plane")
             nc.vector.quantize_mx(out=codes[:].bitcast(E4M3), scales=plane[:], in_=rounded)
             return codes, plane
 
-        def prepare_wa(b, a, copies):
-            rounded = held([P, PACK * PASS], BF16, rounded_slots[b][a])
+        def round_wa(b, a, copy, slot):
+            rounded = held([P, PACK * PASS], BF16, slot)
             dealt = rounded[:].rearrange("p (t m e j) -> p m t j e", t=PACK, e=4, j=PACK)
-            source = wa_raw[b, a][:].rearrange("p j (m t e) -> p m t j e", t=PACK, e=4)
-            share = (P // 4) // len(copies)
-            for n, copy in enumerate(copies):
-                copy(dealt[:, n * share : (n + 1) * share], source[:, n * share : (n + 1) * share])
+            share = (P // 4) // len(wa_raw[b, a])
+            for n, raw in enumerate(wa_raw[b, a]):
+                copy(dealt[:, n * share : (n + 1) * share], raw[:].rearrange("p j (m t e) -> p m t j e", t=PACK, e=4))
+            return rounded
+
+        def prepare_wa(b, a, copy, slot):
+            rounded = round_wa(b, a, copy, slot)
             wa_codes[b, a], wa_planes[b, a] = quantise(rounded[:], "wa%d%d" % (b, a))
 
-        prepare_wa(0, 0, [nc.scalar.copy])
-        prepare_wa(0, 1, [nc.scalar.copy, nc.vector.tensor_copy])
+        for a in range(2):
+            prepare_wa(0, a, nc.scalar.copy, "rounded0%d" % a)
 
         wb_dealt = []
 
         def deal_wb():
-            codes = held([P, 4, PACK, P // 4, 2], I32, "raw11")
+            codes = held([P, 4, PACK, P // 4, 2], I32, "raw100")
             planes = held([P, 4, PACK, P], U8, "rounded01")
             nc.vector.tensor_copy(
                 codes[:],
@@ -158,7 +163,7 @@ def tile_list_softplus_step_input_kernel(
 
         def steps_before_guard(b, half):
             cols = slice(half * HALF, (half + 1) * HALF)
-            banks = [psum.tile([P, HALF], F32, name="sum_bank", bufs=6) for t in range(PACK)]
+            banks = [psum.tile([P, HALF], F32, name="sum_bank", bufs=5) for t in range(PACK)]
             order = [(t, a) for t in range(PACK) for a in range(2)]
             if (b, half) == (0, 0):
                 order = [(t, a) for a in range(2) for t in range(PACK)]
@@ -184,9 +189,10 @@ def tile_list_softplus_step_input_kernel(
         phases = [(b, half) for b in range(2) for half in range(2)]
         pending = steps_before_guard(*phases[0])
 
-        for a in range(2):
-            prepare_wa(1, a, [nc.vector.tensor_copy])
+        prepare_wa(1, 0, nc.vector.tensor_copy, "rounded01")
         deal_wb()
+        first_factors = held([P, S], F32, "first_factors")
+        nc.vector.tensor_copy(first_factors[:], factors[0, 0][:].indirect(offsets[:]))
 
         wo_quantised = []
 
@@ -206,25 +212,42 @@ def tile_list_softplus_step_input_kernel(
         h_quantised = {}
         out_rows = out.rearrange("(c p) s -> p c s", p=P)
 
-        def project(half, block):
-            bank = psum.tile([P, N // P, BLOCK], F32, name="sum_bank", bufs=6)
-            for c in range(N // P):
-                for b in range(2):
-                    w_codes, w_plane = wo_quantised[b]
-                    h_codes, h_plane = h_quantised[b, half, block]
-                    nc.tensor.matmul_mx(
-                        out=bank[:, c, :],
-                        lhsT=w_codes[:, c * P : (c + 1) * P].bitcast(E4M3),
-                        lhsT_scale=w_plane[:, c * P : (c + 1) * P],
-                        rhs=h_codes.bitcast(E4M3),
-                        rhs_scale=h_plane,
-                        start=(b == 0),
-                        stop=(b == 1),
-                    )
-            result = ring.tile([P, N // P, BLOCK], F32, name="result", bufs=4)
-            nc.scalar.copy(result[:], bank[:])
+        def project_pass(target, c, b, half, block):
+            w_codes, w_plane = wo_quantised[b]
+            h_codes, h_plane = h_quantised[b, half, block]
+            nc.tensor.matmul_mx(
+                out=target,
+                lhsT=w_codes[:, c * P : (c + 1) * P].bitcast(E4M3),
+                lhsT_scale=w_plane[:, c * P : (c + 1) * P],
+                rhs=h_codes.bitcast(E4M3),
+                rhs_scale=h_plane,
+                start=(b == 0),
+                stop=(b == 1),
+            )
+
+        def store(result, half, block):
             first = half * HALF + block * BLOCK
             nc.sync.dma_start(out_rows[:, :, first : first + BLOCK], result[:])
+
+        def project(half, block):
+            bank = psum.tile([P, N // P, BLOCK], F32, name="sum_bank", bufs=5)
+            for c in range(N // P):
+                for b in range(2):
+                    project_pass(bank[:, c, :], c, b, half, block)
+            result = ring.tile([P, N // P, BLOCK], F32, name="result", bufs=4)
+            nc.scalar.copy(result[:], bank[:])
+            store(result, half, block)
+
+        def project_last(half, block):
+            banks = [psum.tile([P, BLOCK], F32, name="sum_bank", bufs=5) for c in range(N // P)]
+            for b in range(2):
+                for c in range(N // P):
+                    project_pass(banks[c][:], c, b, half, block)
+            result = ring.tile([P, N // P, BLOCK], F32, name="result", bufs=4)
+            for c in range(N // P):
+                copy = nc.vector.tensor_copy if c % 2 else nc.scalar.copy
+                copy(result[:, c, :], banks[c][:])
+            store(result, half, block)
 
         for index, (b, half) in enumerate(phases):
             banks, logs = pending
@@ -246,8 +269,12 @@ def tile_list_softplus_step_input_kernel(
                         MULT,
                         MAX,
                     )
+            if index == 1:
+                wa_codes[1, 1], wa_planes[1, 1] = quantise(last_rounded[:], "wa11", "h_first")
             if index + 1 < len(phases):
                 pending = steps_before_guard(*phases[index + 1])
+            if index == 0:
+                last_rounded = round_wa(1, 1, nc.scalar.copy, "rounded00")
             if index == 3:
                 round_wo(0)
                 round_wo(1)
@@ -257,24 +284,27 @@ def tile_list_softplus_step_input_kernel(
             scaled = keep.tile([P, PACK, HALF], F32, name="work%d" % ((index + 1) % 2))
 
             def scale_steps(t, first, count):
-                entries = offsets[:, (half * HALF + first) // 16 : (half * HALF + first + count) // 16]
+                start = half * HALF + first
+                if (b, t) == (0, 0):
+                    looked_up = first_factors[:, start : start + count]
+                else:
+                    looked_up = factors[b, t][:].indirect(offsets[:, start // 16 : (start + count) // 16])
                 nc.vector.tensor_tensor(
                     scaled[:, t, first : first + count],
-                    factors[b, t][:].indirect(entries),
+                    looked_up,
                     steps[:, t, first : first + count],
                     MULT,
                 )
 
-            for t in range(2):
-                scale_steps(t, 0, HALF)
-            h_rounded = ring.tile([P, HALF, PACK], BF16, name="h_rounded", bufs=2, align_bytes=64)
-            for block in range(HALF // BLOCK):
-                if block % 2 == 0:
-                    for t in range(2, PACK):
-                        scale_steps(t, block * BLOCK, 2 * BLOCK)
+            if index == 0:
+                h_rounded = held([P, HALF, PACK], BF16, "h_first")
+            else:
+                h_rounded = ring.tile([P, HALF, PACK], BF16, name="h_rounded", bufs=2, align_bytes=64)
+
+            def finish(block):
                 cols = slice(block * BLOCK, (block + 1) * BLOCK)
                 list_cols = slice(half * HALF + block * BLOCK, half * HALF + (block + 1) * BLOCK)
-                bank = psum.tile([P, PACK, BLOCK], F32, name="b_bank", bufs=2)
+                bank = psum.tile([P, PACK, BLOCK], F32, name="b_bank", bufs=3)
                 for t in range(PACK):
                     for a in range(2):
                         nc.tensor.matmul_mx(
@@ -292,14 +322,34 @@ def tile_list_softplus_step_input_kernel(
                     scaled[:, :, cols].rearrange("p t (c i) -> p c t i", i=2),
                     MULT,
                 )
-                if index == 3:
-                    codes, plane = quantise(
-                        h_rounded[:, cols, :].rearrange("p n t -> p (n t)"), "h%d%d%d" % (b, half, block)
-                    )
-                    h_quantised[b, half, block] = (codes[:], plane[:])
-                    project(1, block)
+
+            def quantise_h(first, count):
+                cols = slice(first * BLOCK, (first + count) * BLOCK)
+                codes, plane = quantise(
+                    h_rounded[:, cols, :].rearrange("p n t -> p (n t)"), "h%d%d%d" % (b, half, first)
+                )
+                for n in range(count):
+                    part = slice(n * BLOCK, (n + 1) * BLOCK)
+                    h_quantised[b, half, first + n] = (codes[:, part], plane[:, part])
+
+            scale_steps(0, 0, HALF)
+            scale_steps(1, 0, HALF)
+            scale_steps(2, 0, HALF // 2)
+            scale_steps(3, 0, HALF // 2)
+            scale_steps(2, HALF // 2, HALF // 2)
+            finish(0)
+            scale_steps(3, HALF // 2, HALF // 2)
+            finish(1)
+            finish(2)
             if index < 3:
-                codes, plane = quantise(h_rounded[:].rearrange("p n t -> p (n t)"), "h%d%d" % (b, half))
-                for block in range(HALF // BLOCK):
-                    cols = slice(block * BLOCK, (block + 1) * BLOCK)
-                    h_quantised[b, half, block] = (codes[:, cols], plane[:, cols])
+                finish(3)
+                quantise_h(0, 2)
+                quantise_h(2, 2)
+            else:
+                quantise_h(0, 2)
+                finish(3)
+                quantise_h(2, 1)
+                quantise_h(3, 1)
+                for block in range(HALF // BLOCK - 1):
+                    project(1, block)
+                project_last(1, HALF // BLOCK - 1)

@@ -84,18 +84,17 @@ def tile_list_softplus_step_input_kernel(
         wa_raw = {}
         for a in range(2):
             wa_raw[0, a] = load_wa(0, a, 2)
-        wb_raw = held([P, 2, H // 2], I32, "wb_raw")
-        nc.sync.dma_start(wb_raw[:], wb_words.rearrange("a p w -> p a w").bitcast(I32))
+        wb_raw = held([P, 2, 2 * H], U8, "wb_raw")
+        nc.sync.dma_start(wb_raw[:].bitcast(I32), wb_words.rearrange("a p w -> p a w").bitcast(I32))
         wa_raw[1, 0] = load_wa(1, 0, 1)
-        g_rows = gT.rearrange("(b m t e) n -> b t e m n", m=P // 4, t=PACK, e=4)
-        wo_rows = wo.rearrange("(b m t e) n -> b e m t n", m=P // 4, t=PACK, e=4)
+        g_rows = gT.rearrange("(b p t) n -> b t p n", p=P, t=PACK)
+        wo_rows = wo.rearrange("(b p t) n -> b p t n", p=P, t=PACK)
         factors = {}
 
         def load_factors(b):
             for t in range(PACK):
                 rows = held([P, T], F32, "factors%d%d" % (b, t))
-                for e in range(4):
-                    nc.sync.dma_start(rows[e:P:4, :], g_rows[b, t, e])
+                nc.sync.dma_start(rows[:], g_rows[b, t])
                 factors[b, t] = rows
 
         load_factors(0)
@@ -103,8 +102,7 @@ def tile_list_softplus_step_input_kernel(
         wo_raw = []
         for b in range(2):
             raw = held([P, PACK, N], F32, "wo_raw%d" % b)
-            for e in range(4):
-                nc.sync.dma_start(raw[e:P:4, :, :], wo_rows[b, e])
+            nc.sync.dma_start(raw[:], wo_rows[b])
             wo_raw.append(raw)
         load_factors(1)
 
@@ -133,10 +131,10 @@ def tile_list_softplus_step_input_kernel(
 
         def round_wa(b, a, copy, slot):
             rounded = held([P, PACK * PASS], BF16, slot)
-            dealt = rounded[:].rearrange("p (t m e j) -> p m t j e", t=PACK, e=4, j=PACK)
-            share = (P // 4) // len(wa_raw[b, a])
+            dealt = rounded[:].rearrange("p (u e m j) -> p u m j e", u=2, e=2, j=PACK)
+            share = P // len(wa_raw[b, a])
             for n, raw in enumerate(wa_raw[b, a]):
-                copy(dealt[:, n * share : (n + 1) * share], raw[:].rearrange("p j (m t e) -> p m t j e", t=PACK, e=4))
+                copy(dealt[:, :, n * share : (n + 1) * share], raw[:].rearrange("p j (m u e) -> p u m j e", u=2, e=2))
             return rounded
 
         def prepare_wa(b, a, copy, slot):
@@ -149,15 +147,15 @@ def tile_list_softplus_step_input_kernel(
         wb_dealt = []
 
         def deal_wb():
-            codes = held([P, 4, PACK, P // 4, 2], I32, "raw100")
+            codes = held([P, 4, PACK, P, 2], U8, "raw100")
             planes = held([P, 4, PACK, P], U8, "rounded01")
             nc.vector.tensor_copy(
                 codes[:],
-                wb_raw[:].rearrange("p a (b m t w) -> p (a b) t m w", b=2, t=PACK, w=2),
+                wb_raw[:].rearrange("p a (b m t e) -> p (a b) t m e", b=2, t=PACK, e=2),
             )
             nc.vector.tensor_copy(
-                planes[:].bitcast(I32),
-                wb_planes[:].bitcast(I32).rearrange("p a (b m t) -> p (a b) t m", b=2, t=PACK),
+                planes[:],
+                wb_planes[:].rearrange("p a (b m t) -> p (a b) t m", b=2, t=PACK),
             )
             wb_dealt.extend([codes, planes])
 
@@ -191,8 +189,6 @@ def tile_list_softplus_step_input_kernel(
 
         prepare_wa(1, 0, nc.vector.tensor_copy, "rounded01")
         deal_wb()
-        first_factors = held([P, S], F32, "first_factors")
-        nc.vector.tensor_copy(first_factors[:], factors[0, 0][:].indirect(offsets[:]))
 
         wo_quantised = []
 
@@ -285,10 +281,7 @@ def tile_list_softplus_step_input_kernel(
 
             def scale_steps(t, first, count):
                 start = half * HALF + first
-                if (b, t) == (0, 0):
-                    looked_up = first_factors[:, start : start + count]
-                else:
-                    looked_up = factors[b, t][:].indirect(offsets[:, start // 16 : (start + count) // 16])
+                looked_up = factors[b, t][:].indirect(offsets[:, start // 16 : (start + count) // 16])
                 nc.vector.tensor_tensor(
                     scaled[:, t, first : first + count],
                     looked_up,
@@ -309,7 +302,7 @@ def tile_list_softplus_step_input_kernel(
                     for a in range(2):
                         nc.tensor.matmul_mx(
                             out=bank[:, t, :],
-                            lhsT=wb_dealt[0][:, 2 * a + b, t].rearrange("p m w -> p (m w)").bitcast(U8).bitcast(E2M1),
+                            lhsT=wb_dealt[0][:, 2 * a + b, t].rearrange("p m e -> p (m e)").bitcast(E2M1),
                             lhsT_scale=wb_dealt[1][:, 2 * a + b, t, :],
                             rhs=picked[a, half][:, cols].bitcast(E4M3),
                             rhs_scale=(picked_planes, moved_plane)[a][:, list_cols],

@@ -23,7 +23,9 @@ PACK = 4
 PASS = P * PACK
 HALF = 512
 BLOCK = 128
+RUN = 4
 FLOOR = 1e-12
+BATCHES = ((0, 1, 2), (3, 4, 5), (6, 7))
 
 
 def tile_list_softplus_step_input_kernel(
@@ -39,21 +41,25 @@ def tile_list_softplus_step_input_kernel(
         def held(shape, dtype, name):
             return keep.tile(shape, dtype, name=name, align_bytes=64)
 
+        def bank_tile(number, shape):
+            return psum.tile(shape, F32, name="bank%d" % number)
+
         offsets = lists.tile([P, S // 16], U16, name="offsets")
         nc.sync.dma_start(offsets[:], offs)
 
-        def half_offsets(half):
-            return offsets[:, half * (HALF // 16) : (half + 1) * (HALF // 16)]
+        def list_part(first, count):
+            return offsets[:, first // 16 : (first + count) // 16]
 
         tab_planes = held([P, T], U8, "tab_planes")
-        moved_plane = held([P, S], U8, "moved_plane")
         wb_planes = held([P, 2, H], U8, "wb_planes")
+        moved_plane = held([P, S], U8, "moved_plane")
         nc.vector.memset(tab_planes[:].bitcast(I32), 0)
         nc.vector.memset(wb_planes[:].rearrange("p a c -> p (a c)").bitcast(I32), 0)
         nc.vector.memset(moved_plane[:].bitcast(I32), 0)
-        warm = held([P, 1], F32, "warm")
-        nc.vector.memset(warm[:], 0.0)
-        nc.scalar.activation(warm[:], warm[:], SIGMOID, scale=-1.0)
+        def load_table(a):
+            words = held([P, T], I32, "table%d" % a)
+            nc.sync.dma_start(words[:], tab_words[a].rearrange("p t i -> p (t i)").bitcast(I32))
+            return words
 
         def load_wa(b, a, pieces):
             width = PASS // pieces
@@ -66,283 +72,288 @@ def tile_list_softplus_step_input_kernel(
                 tiles.append(raw)
             return tiles
 
+        table = [load_table(0)]
         for q in range(4):
-            nc.gpsimd.dma_start(
+            nc.sync.dma_start(
                 tab_planes[32 * q : 32 * q + 8, :].bitcast(I32),
                 tab_scales[:, 4 * q : 4 * q + 4, :].bitcast(I32),
             )
+        wa_raw = {(0, a): load_wa(0, a, 2) for a in range(2)}
+        table.append(load_table(1))
+        for a in range(2):
+            wa_raw[1, a] = load_wa(1, a, 1)
+        wb_raw = held([P, 2, H // 2], I32, "wb_raw")
+        nc.sync.dma_start(wb_raw[:], wb_words.rearrange("a p w -> p a w").bitcast(I32))
         for q in range(4):
-            nc.gpsimd.dma_start(
+            nc.sync.dma_start(
                 wb_planes[32 * q : 32 * q + 4, :, :].bitcast(I32),
                 wb_scales[:, 4 * q : 4 * q + 4, :].rearrange("a r c -> r a c").bitcast(I32),
             )
-        table = []
-        for a in range(2):
-            words = held([P, T], I32, "table%d" % a)
-            nc.sync.dma_start(words[:], tab_words[a].rearrange("p t i -> p (t i)").bitcast(I32))
-            table.append(words)
-        wa_raw = {}
-        for a in range(2):
-            wa_raw[0, a] = load_wa(0, a, 2)
-        wb_raw = held([P, 2, 2 * H], U8, "wb_raw")
-        nc.sync.dma_start(wb_raw[:].bitcast(I32), wb_words.rearrange("a p w -> p a w").bitcast(I32))
-        wa_raw[1, 0] = load_wa(1, 0, 1)
-        g_rows = gT.rearrange("(b p t) n -> b t p n", p=P, t=PACK)
-        wo_rows = wo.rearrange("(b p t) n -> b p t n", p=P, t=PACK)
-        factors = {}
+        g_rows = gT.rearrange("(b m t e) n -> b t m e n", b=2, t=PACK, e=RUN)
+        wo_rows = wo.rearrange("(b m t e) n -> b t m e n", b=2, t=PACK, e=RUN)
+        factors = []
 
-        def load_factors(b):
-            for t in range(PACK):
-                rows = held([P, T], F32, "factors%d%d" % (b, t))
-                nc.sync.dma_start(rows[:], g_rows[b, t])
-                factors[b, t] = rows
+        def load_factors(s):
+            rows = held([P, T], F32, "factors%d" % s)
+            nc.sync.dma_start(rows[:], g_rows[s // PACK, s % PACK])
+            factors.append(rows)
 
-        load_factors(0)
-        wa_raw[1, 1] = load_wa(1, 1, 2)
-        wo_raw = []
-        for b in range(2):
-            raw = held([P, PACK, N], F32, "wo_raw%d" % b)
-            nc.sync.dma_start(raw[:], wo_rows[b])
-            wo_raw.append(raw)
-        load_factors(1)
+        for s in range(3):
+            load_factors(s)
 
-        picked = {}
-        for a in range(2):
-            for half in range(2):
-                words = held([P, HALF], U32, "picked%d%d" % (a, half))
-                nc.vector.tensor_copy(words[:], table[a][:].bitcast(U32).indirect(half_offsets(half)))
-                picked[a, half] = words
-        picked_planes = held([P, S], U8, "table0")
-        nc.vector.tensor_copy(picked_planes[:], tab_planes[:].indirect(offsets[:]))
-        for q in range(4):
-            nc.gpsimd.dma_start(
-                moved_plane[32 * q : 32 * q + 4, :].bitcast(I32),
-                picked_planes[32 * q + 4 : 32 * q + 8, :].bitcast(I32),
-            )
+        picked = [held([P, S], U32, "picked%d" % a) for a in range(2)]
+        picked_planes = held([P, S], U8, "picked_planes")
 
-        wa_codes, wa_planes = {}, {}
-
-        def quantise(rounded, name, slot=None):
+        def quantise(rounded, name):
             width = rounded.shape[1] // PACK
-            codes = held([P, width], U32, slot or name + "_codes")
+            codes = held([P, width], U32, name + "_codes")
             plane = held([P, width], U8, name + "_plane")
             nc.vector.quantize_mx(out=codes[:].bitcast(E4M3), scales=plane[:], in_=rounded)
             return codes, plane
 
         def round_wa(b, a, copy, slot):
             rounded = held([P, PACK * PASS], BF16, slot)
-            dealt = rounded[:].rearrange("p (u e m j) -> p u m j e", u=2, e=2, j=PACK)
-            share = P // len(wa_raw[b, a])
+            dealt = rounded[:].rearrange("p (t m e j) -> p m t j e", t=PACK, e=RUN, j=PACK)
+            share = (P // RUN) // len(wa_raw[b, a])
             for n, raw in enumerate(wa_raw[b, a]):
-                copy(dealt[:, :, n * share : (n + 1) * share], raw[:].rearrange("p j (m u e) -> p u m j e", u=2, e=2))
+                copy(
+                    dealt[:, n * share : (n + 1) * share],
+                    raw[:].rearrange("p j (m t e) -> p m t j e", t=PACK, e=RUN),
+                )
             return rounded
 
-        def prepare_wa(b, a, copy, slot):
-            rounded = round_wa(b, a, copy, slot)
-            wa_codes[b, a], wa_planes[b, a] = quantise(rounded[:], "wa%d%d" % (b, a))
-
+        wa_quantised = {}
+        nc.vector.tensor_copy(picked[0][:], table[0][:].bitcast(U32).indirect(offsets[:]))
+        nc.vector.tensor_copy(picked_planes[:], tab_planes[:].indirect(offsets[:]))
         for a in range(2):
-            prepare_wa(0, a, nc.scalar.copy, "rounded0%d" % a)
-
-        wb_dealt = []
-
-        def deal_wb():
-            codes = held([P, 4, PACK, P, 2], U8, "raw100")
-            planes = held([P, 4, PACK, P], U8, "rounded01")
+            rounded = round_wa(0, a, nc.scalar.copy, "rounded0%d" % a)
+            wa_quantised[0, a] = quantise(rounded[:], "wa0%d" % a)
+        for half in range(2):
             nc.vector.tensor_copy(
-                codes[:],
-                wb_raw[:].rearrange("p a (b m t e) -> p (a b) t m e", b=2, t=PACK, e=2),
+                picked[1][:, half * HALF : (half + 1) * HALF],
+                table[1][:].bitcast(U32).indirect(list_part(half * HALF, HALF)),
             )
-            nc.vector.tensor_copy(
-                planes[:],
-                wb_planes[:].rearrange("p a (b m t) -> p (a b) t m", b=2, t=PACK),
-            )
-            wb_dealt.extend([codes, planes])
 
-        def steps_before_guard(b, half):
-            cols = slice(half * HALF, (half + 1) * HALF)
-            banks = [psum.tile([P, HALF], F32, name="sum_bank", bufs=5) for t in range(PACK)]
-            order = [(t, a) for t in range(PACK) for a in range(2)]
-            if (b, half) == (0, 0):
-                order = [(t, a) for a in range(2) for t in range(PACK)]
-            for t, a in order:
+        for q in range(4):
+            nc.sync.dma_start(
+                moved_plane[32 * q : 32 * q + 4, :].bitcast(I32),
+                picked_planes[32 * q + 4 : 32 * q + 8, :].bitcast(I32),
+            )
+        for s in range(3, 2 * PACK):
+            load_factors(s)
+        wo_raw = []
+        for b in range(2):
+            raw = held([P, PACK, N], F32, "raw1%d0" % b)
+            for t in range(PACK):
+                nc.sync.dma_start(raw[:, t, :], wo_rows[b, t])
+            wo_raw.append(raw)
+
+        work = held([P, 2 * PACK * S], F32, "work")
+
+        def units_of(batch):
+            return [(s, half) for half in range(2) for s in batch]
+
+        def log_parts(batch):
+            count = 2 * len(batch)
+            rows = count - 2
+            region = work[:, batch[0] * S : (batch[-1] + 1) * S].rearrange("p (r c) -> p r c", r=rows)
+            strip = HALF // rows
+            places = [region[:, r : r + 1, 0:HALF] for r in range(rows)]
+            for n in range(2):
+                places.append(region[:, :, HALF + n * strip : HALF + (n + 1) * strip])
+            return region, places
+
+        def shaped(view, place):
+            return view.rearrange("p (r c) -> p r c", r=place.shape[1])
+
+        def logs_of(batch, first_pass_ahead):
+            units = units_of(batch)
+            banks = [bank_tile(n, [P, HALF]) for n in range(len(units))]
+            order = [(n, a) for n in range(len(units)) for a in range(2)]
+            if first_pass_ahead:
+                order = [(n, a) for a in range(2) for n in range(len(units))]
+            for n, a in order:
+                s, half = units[n]
+                codes, plane = wa_quantised[s // PACK, a]
+                channels = slice(s % PACK * P, (s % PACK + 1) * P)
+                cols = slice(half * HALF, (half + 1) * HALF)
                 nc.tensor.matmul_mx(
-                    out=banks[t][:],
-                    lhsT=wa_codes[b, a][:, t * P : (t + 1) * P].bitcast(E4M3),
-                    lhsT_scale=wa_planes[b, a][:, t * P : (t + 1) * P],
-                    rhs=picked[a, half][:].bitcast(E4M3),
+                    out=banks[n][:],
+                    lhsT=codes[:, channels].bitcast(E4M3),
+                    lhsT_scale=plane[:, channels],
+                    rhs=picked[a][:, cols].bitcast(E4M3),
                     rhs_scale=picked_planes[4 * a : P, cols],
                     start=(a == 0),
                     stop=(a == 1),
                 )
-            logs = ring.tile([P, 2, PACK, HALF // 2], F32, name="logs", bufs=2)
-            for t in range(PACK):
-                nc.scalar.activation(
-                    logs[:, :, t, :], banks[t][:].rearrange("p (u n) -> p u n", u=2), SIGMOID, scale=-1.0
+            region, places = log_parts(batch)
+            for bank, place in zip(banks, places):
+                nc.scalar.activation(place, shaped(bank[:], place), SIGMOID, scale=-1.0)
+            for r in range(region.shape[1]):
+                nc.scalar.activation(region[:, r, :], region[:, r, :], LN, bias=FLOOR)
+            return banks, places
+
+        def guard(batch, banks, places):
+            steps = ring.tile([P, 3, S], F32, name="steps", bufs=2)
+            for (s, half), bank, place in zip(units_of(batch), banks, places):
+                target = steps[:, s - batch[0], half * HALF : (half + 1) * HALF]
+                nc.vector.scalar_tensor_tensor(
+                    shaped(target, place), place, -1.0, shaped(bank[:], place), MULT, MAX
                 )
-            for u in range(2):
-                nc.scalar.activation(logs[:, u], logs[:, u], LN, bias=FLOOR)
-            return banks, logs
+            return steps
 
-        phases = [(b, half) for b in range(2) for half in range(2)]
-        pending = steps_before_guard(*phases[0])
-
-        prepare_wa(1, 0, nc.vector.tensor_copy, "rounded01")
-        deal_wb()
-
-        wo_quantised = []
-
-        def round_wo(b):
-            raw = wo_raw[b]
-            rounded = held([P, PACK * N], BF16, "picked%d0" % b)
-            for piece in range(4):
-                cols = slice(piece * P, (piece + 1) * P)
-                nc.scalar.copy(
-                    rounded[:].rearrange("p (n j) -> p n j", j=PACK)[:, cols, :].rearrange(
-                        "p (c i) j -> p c j i", i=2
-                    ),
-                    raw[:, :, cols].rearrange("p j (c i) -> p c j i", i=2),
-                )
-            wo_quantised.append(quantise(rounded[:], "wo%d" % b))
-
-        h_quantised = {}
-        out_rows = out.rearrange("(c p) s -> p c s", p=P)
-
-        def project_pass(target, c, b, half, block):
-            w_codes, w_plane = wo_quantised[b]
-            h_codes, h_plane = h_quantised[b, half, block]
-            nc.tensor.matmul_mx(
-                out=target,
-                lhsT=w_codes[:, c * P : (c + 1) * P].bitcast(E4M3),
-                lhsT_scale=w_plane[:, c * P : (c + 1) * P],
-                rhs=h_codes.bitcast(E4M3),
-                rhs_scale=h_plane,
-                start=(b == 0),
-                stop=(b == 1),
+        def scale_steps(batch, steps, s, first, count):
+            nc.vector.tensor_tensor(
+                work[:, s * S + first : s * S + first + count],
+                factors[s][:].indirect(list_part(first, count)),
+                steps[:, s - batch[0], first : first + count],
+                MULT,
             )
 
-        def store(result, half, block):
-            first = half * HALF + block * BLOCK
-            nc.sync.dma_start(out_rows[:, :, first : first + BLOCK], result[:])
+        pending = logs_of(BATCHES[0], True)
 
-        def project(half, block):
-            bank = psum.tile([P, N // P, BLOCK], F32, name="sum_bank", bufs=5)
-            for c in range(N // P):
-                for b in range(2):
-                    project_pass(bank[:, c, :], c, b, half, block)
-            result = ring.tile([P, N // P, BLOCK], F32, name="result", bufs=4)
-            nc.scalar.copy(result[:], bank[:])
-            store(result, half, block)
+        rounded = round_wa(1, 0, nc.vector.tensor_copy, "tab_planes")
+        wa_quantised[1, 0] = quantise(rounded[:], "wa10")
+        rounded = round_wa(1, 1, nc.vector.tensor_copy, "table1")
+        wb_codes = held([P, 4, PACK, P // RUN, 2], I32, "wb_codes")
+        nc.vector.tensor_copy(
+            wb_codes[:], wb_raw[:].rearrange("p a (b m t w) -> p (a b) t m w", b=2, t=PACK, w=2)
+        )
+        wa_quantised[1, 1] = quantise(rounded[:], "wa11")
+        wb_dealt_planes = held([P, 4, PACK, P // RUN], I32, "wb_dealt_planes")
+        nc.vector.tensor_copy(
+            wb_dealt_planes[:],
+            wb_planes[:].bitcast(I32).rearrange("p a (b m t) -> p (a b) t m", b=2, t=PACK),
+        )
 
-        def project_last(half, block):
-            banks = [psum.tile([P, BLOCK], F32, name="sum_bank", bufs=5) for c in range(N // P)]
-            for b in range(2):
-                for c in range(N // P):
-                    project_pass(banks[c][:], c, b, half, block)
-            result = ring.tile([P, N // P, BLOCK], F32, name="result", bufs=4)
-            for c in range(N // P):
-                copy = nc.vector.tensor_copy if c % 2 else nc.scalar.copy
-                copy(result[:, c, :], banks[c][:])
-            store(result, half, block)
+        h_rounded = [held([P, S, PACK], BF16, slot) for slot in ("table0", "factors0")]
+        h_codes = [held([P, S], U32, "h_codes%d" % b) for b in range(2)]
+        h_planes = [held([P, S], U8, "h_planes%d" % b) for b in range(2)]
+        scaled = work[:].rearrange("p (s n) -> p s n", n=S)
 
-        for index, (b, half) in enumerate(phases):
-            banks, logs = pending
-            steps = keep.tile([P, PACK, HALF], F32, name="work%d" % (index % 2))
-            if index == 0:
-                for u in range(2):
-                    cols = slice(u * (HALF // 2), (u + 1) * (HALF // 2))
-                    for t in range(PACK):
-                        nc.vector.scalar_tensor_tensor(
-                            steps[:, t, cols], logs[:, u, t, :], -1.0, banks[t][:, cols], MULT, MAX
-                        )
-            else:
-                for t in range(PACK):
-                    nc.vector.scalar_tensor_tensor(
-                        steps[:, t, :].rearrange("p (u n) -> p u n", u=2),
-                        logs[:, :, t, :],
-                        -1.0,
-                        banks[t][:].rearrange("p (u n) -> p u n", u=2),
-                        MULT,
-                        MAX,
+        def inputs_of(b, block, number):
+            cols = slice(block * BLOCK, (block + 1) * BLOCK)
+            bank = bank_tile(number, [P, PACK, BLOCK])
+            for t in range(PACK):
+                for a in range(2):
+                    nc.tensor.matmul_mx(
+                        out=bank[:, t, :],
+                        lhsT=wb_codes[:, 2 * a + b, t].rearrange("p m w -> p (m w)").bitcast(E2M1),
+                        lhsT_scale=wb_dealt_planes[:, 2 * a + b, t].bitcast(U8),
+                        rhs=picked[a][:, cols].bitcast(E4M3),
+                        rhs_scale=(picked_planes, moved_plane)[a][:, cols],
+                        start=(a == 0),
+                        stop=(a == 1),
                     )
-            if index == 1:
-                wa_codes[1, 1], wa_planes[1, 1] = quantise(last_rounded[:], "wa11", "h_first")
-            if index + 1 < len(phases):
-                pending = steps_before_guard(*phases[index + 1])
-            if index == 0:
-                last_rounded = round_wa(1, 1, nc.scalar.copy, "rounded00")
-            if index == 3:
-                round_wo(0)
-                round_wo(1)
-                for block in range(HALF // BLOCK):
-                    project(0, block)
+            return bank
 
-            scaled = keep.tile([P, PACK, HALF], F32, name="work%d" % ((index + 1) % 2))
+        def finish(b, block, bank):
+            cols = slice(block * BLOCK, (block + 1) * BLOCK)
+            nc.vector.tensor_tensor(
+                h_rounded[b][:, cols, :].rearrange("p (c i) t -> p c t i", i=4),
+                bank[:].rearrange("p t (c i) -> p c t i", i=4),
+                scaled[:, b * PACK : (b + 1) * PACK, cols].rearrange("p t (c i) -> p c t i", i=4),
+                MULT,
+            )
 
-            def scale_steps(t, first, count):
-                start = half * HALF + first
-                looked_up = factors[b, t][:].indirect(offsets[:, start // 16 : (start + count) // 16])
-                nc.vector.tensor_tensor(
-                    scaled[:, t, first : first + count],
-                    looked_up,
-                    steps[:, t, first : first + count],
-                    MULT,
-                )
+        def quantise_h(b, first, count):
+            cols = slice(first * BLOCK, (first + count) * BLOCK)
+            nc.vector.quantize_mx(
+                out=h_codes[b][:, cols].bitcast(E4M3),
+                scales=h_planes[b][:, cols],
+                in_=h_rounded[b][:, cols, :].rearrange("p n t -> p (n t)"),
+            )
 
-            if index == 0:
-                h_rounded = held([P, HALF, PACK], BF16, "h_first")
+        batch = BATCHES[0]
+        steps = guard(batch, *pending)
+        pending = logs_of(BATCHES[1], False)
+        scale_steps(batch, steps, 0, 0, HALF)
+        scale_steps(batch, steps, 0, HALF, HALF)
+        scale_steps(batch, steps, 1, 0, S)
+        scale_steps(batch, steps, 2, 0, S)
+        spare = (6, 7, 4, 5)
+        batch = BATCHES[1]
+        steps = guard(batch, *pending)
+        pending = logs_of(BATCHES[2], False)
+        scale_steps(batch, steps, 3, 0, HALF)
+        scale_steps(batch, steps, 3, HALF, HALF)
+        rest = [(s, half) for half in range(2) for s in (4, 5)]
+        for block in range(S // BLOCK):
+            finish(0, block, inputs_of(0, block, spare[block % 4]))
+            if block % 2 == 1:
+                s, half = rest[block // 2]
+                scale_steps(batch, steps, s, half * HALF, HALF)
+            if block == 4:
+                quantise_h(0, 0, 4)
+        quantise_h(0, 4, 4)
+        wo_quantised = []
+        wo_rounded = []
+        for b in range(2):
+            rounded = held([P, N, PACK], BF16, "rounded0%d" % b)
+            nc.scalar.copy(
+                rounded[:].rearrange("p (c i) t -> p c t i", i=4),
+                wo_raw[b][:].rearrange("p t (c i) -> p c t i", i=4),
+            )
+            wo_rounded.append(rounded)
+
+        batch = BATCHES[2]
+        steps = guard(batch, *pending)
+        for s in batch:
+            scale_steps(batch, steps, s, 0, HALF)
+        for b in range(2):
+            wo_quantised.append(quantise(wo_rounded[b][:].rearrange("p n t -> p (n t)"), "wo%d" % b))
+
+        def project(target, c, b, cols, start, stop):
+            codes, plane = wo_quantised[b]
+            nc.tensor.matmul_mx(
+                out=target,
+                lhsT=codes[:, c * P : (c + 1) * P].bitcast(E4M3),
+                lhsT_scale=plane[:, c * P : (c + 1) * P],
+                rhs=h_codes[b][:, cols].bitcast(E4M3),
+                rhs_scale=h_planes[b][:, cols],
+                start=start,
+                stop=stop,
+            )
+
+        late = [inputs_of(1, block, spare[block]) for block in range(4)]
+        late += [inputs_of(1, block, block - 4) for block in range(4, 8)]
+        for block in range(4):
+            finish(1, block, late[block])
+            if block % 2 == 1:
+                scale_steps(batch, steps, batch[block // 2], HALF, HALF)
+        quantise_h(1, 0, 4)
+        for c in range(N // P):
+            bank = bank_tile(spare[c], [P, HALF])
+            for b in range(2):
+                project(bank[:], c, b, slice(0, HALF), b == 0, b == 1)
+            result = held([P, HALF], F32, "factors%d" % (1 + c))
+            nc.scalar.copy(result[:], bank[:])
+            nc.sync.dma_start(out[c * P : (c + 1) * P, 0:HALF], result[:])
+
+        out_rows = out.rearrange("(c p) s -> p c s", p=P)
+
+        def project_block(block):
+            cols = slice(block * BLOCK, (block + 1) * BLOCK)
+            result = held([P, N // P, BLOCK], F32, "raw0%d%d" % (block // 2 % 2, block % 2))
+            if block < 7:
+                bank = bank_tile(block - 4, [P, N // P, BLOCK])
+                for b in range(2):
+                    for c in range(N // P):
+                        project(bank[:, c, :], c, b, cols, (b, c) == (0, 0), (b, c) == (1, N // P - 1))
+                nc.scalar.copy(result[:], bank[:])
             else:
-                h_rounded = ring.tile([P, HALF, PACK], BF16, name="h_rounded", bufs=2, align_bytes=64)
+                for pair, copy in enumerate((nc.scalar.copy, nc.vector.tensor_copy)):
+                    bank = bank_tile(spare[pair], [P, 2, BLOCK])
+                    for b in range(2):
+                        for c in range(2):
+                            project(bank[:, c, :], 2 * pair + c, b, cols, (b, c) == (0, 0), (b, c) == (1, 1))
+                    copy(result[:, 2 * pair : 2 * pair + 2, :], bank[:])
+            nc.sync.dma_start(out_rows[:, :, cols], result[:])
 
-            def finish(block):
-                cols = slice(block * BLOCK, (block + 1) * BLOCK)
-                list_cols = slice(half * HALF + block * BLOCK, half * HALF + (block + 1) * BLOCK)
-                bank = psum.tile([P, PACK, BLOCK], F32, name="b_bank", bufs=3)
-                for t in range(PACK):
-                    for a in range(2):
-                        nc.tensor.matmul_mx(
-                            out=bank[:, t, :],
-                            lhsT=wb_dealt[0][:, 2 * a + b, t].rearrange("p m e -> p (m e)").bitcast(E2M1),
-                            lhsT_scale=wb_dealt[1][:, 2 * a + b, t, :],
-                            rhs=picked[a, half][:, cols].bitcast(E4M3),
-                            rhs_scale=(picked_planes, moved_plane)[a][:, list_cols],
-                            start=(a == 0),
-                            stop=(a == 1),
-                        )
-                nc.vector.tensor_tensor(
-                    h_rounded[:, cols, :].rearrange("p (c i) t -> p c t i", i=2),
-                    bank[:].rearrange("p t (c i) -> p c t i", i=2),
-                    scaled[:, :, cols].rearrange("p t (c i) -> p c t i", i=2),
-                    MULT,
-                )
-
-            def quantise_h(first, count):
-                cols = slice(first * BLOCK, (first + count) * BLOCK)
-                codes, plane = quantise(
-                    h_rounded[:, cols, :].rearrange("p n t -> p (n t)"), "h%d%d%d" % (b, half, first)
-                )
-                for n in range(count):
-                    part = slice(n * BLOCK, (n + 1) * BLOCK)
-                    h_quantised[b, half, first + n] = (codes[:, part], plane[:, part])
-
-            scale_steps(0, 0, HALF)
-            scale_steps(1, 0, HALF)
-            scale_steps(2, 0, HALF // 2)
-            scale_steps(3, 0, HALF // 2)
-            scale_steps(2, HALF // 2, HALF // 2)
-            finish(0)
-            scale_steps(3, HALF // 2, HALF // 2)
-            finish(1)
-            finish(2)
-            if index < 3:
-                finish(3)
-                quantise_h(0, 2)
-                quantise_h(2, 2)
-            else:
-                quantise_h(0, 2)
-                finish(3)
-                quantise_h(2, 1)
-                quantise_h(3, 1)
-                for block in range(HALF // BLOCK - 1):
-                    project(1, block)
-                project_last(1, HALF // BLOCK - 1)
+        for block in range(4, 8):
+            finish(1, block, late[block])
+            if block > 4:
+                quantise_h(1, block - 1, 1)
+                project_block(block - 1)
+        quantise_h(1, 7, 1)
+        project_block(7)

@@ -139,7 +139,7 @@ def tile_list_softplus_step_input_kernel(
                 moved_plane[32 * q : 32 * q + 4, :].bitcast(I32),
                 picked_planes[32 * q + 4 : 32 * q + 8, :].bitcast(I32),
             )
-        for s in range(3, 2 * PACK):
+        for s in range(3, 6):
             load_factors(s)
         wo_raw = []
         for b in range(2):
@@ -147,6 +147,8 @@ def tile_list_softplus_step_input_kernel(
             for t in range(PACK):
                 nc.sync.dma_start(raw[:, t, :], wo_rows[b, t])
             wo_raw.append(raw)
+        for s in range(6, 8):
+            load_factors(s)
 
         work = held([P, 2 * PACK * S], F32, "work")
 
@@ -226,7 +228,7 @@ def tile_list_softplus_step_input_kernel(
             wb_planes[:].bitcast(I32).rearrange("p a (b m t) -> p (a b) t m", b=2, t=PACK),
         )
 
-        h_rounded = [held([P, S, PACK], BF16, slot) for slot in ("table0", "factors0")]
+        h_rounded = [held([P, S, PACK], BF16, "table0")]
         h_codes = [held([P, S], U32, "h_codes%d" % b) for b in range(2)]
         h_planes = [held([P, S], U8, "h_planes%d" % b) for b in range(2)]
         scaled = work[:].rearrange("p (s n) -> p s n", n=S)
@@ -287,21 +289,20 @@ def tile_list_softplus_step_input_kernel(
                 quantise_h(0, 0, 4)
         quantise_h(0, 4, 4)
         wo_quantised = []
-        wo_rounded = []
+        wo_rounded = held([P, 2, N, PACK], BF16, "wa11_codes")
         for b in range(2):
-            rounded = held([P, N, PACK], BF16, "rounded0%d" % b)
             nc.scalar.copy(
-                rounded[:].rearrange("p (c i) t -> p c t i", i=4),
+                wo_rounded[:, b].rearrange("p (c i) t -> p c t i", i=4),
                 wo_raw[b][:].rearrange("p t (c i) -> p c t i", i=4),
             )
-            wo_rounded.append(rounded)
 
         batch = BATCHES[2]
         steps = guard(batch, *pending)
         for s in batch:
             scale_steps(batch, steps, s, 0, HALF)
         for b in range(2):
-            wo_quantised.append(quantise(wo_rounded[b][:].rearrange("p n t -> p (n t)"), "wo%d" % b))
+            wo_quantised.append(quantise(wo_rounded[:, b].rearrange("p n t -> p (n t)"), "wo%d" % b))
+        h_rounded.append(held([P, S, PACK], BF16, "wa11_codes"))
 
         def project(target, c, b, cols, start, stop):
             codes, plane = wo_quantised[b]
@@ -317,43 +318,34 @@ def tile_list_softplus_step_input_kernel(
 
         late = [inputs_of(1, block, spare[block]) for block in range(4)]
         late += [inputs_of(1, block, block - 4) for block in range(4, 8)]
-        for block in range(4):
-            finish(1, block, late[block])
-            if block % 2 == 1:
-                scale_steps(batch, steps, batch[block // 2], HALF, HALF)
-        quantise_h(1, 0, 4)
-        for c in range(N // P):
-            bank = bank_tile(spare[c], [P, HALF])
-            for b in range(2):
-                project(bank[:], c, b, slice(0, HALF), b == 0, b == 1)
-            result = held([P, HALF], F32, "factors%d" % (1 + c))
-            nc.scalar.copy(result[:], bank[:])
-            nc.sync.dma_start(out[c * P : (c + 1) * P, 0:HALF], result[:])
-
         out_rows = out.rearrange("(c p) s -> p c s", p=P)
 
-        def project_block(block):
-            cols = slice(block * BLOCK, (block + 1) * BLOCK)
-            result = held([P, N // P, BLOCK], F32, "raw0%d%d" % (block // 2 % 2, block % 2))
-            if block < 7:
-                bank = bank_tile(block - 4, [P, N // P, BLOCK])
-                for b in range(2):
-                    for c in range(N // P):
-                        project(bank[:, c, :], c, b, cols, (b, c) == (0, 0), (b, c) == (1, N // P - 1))
-                nc.scalar.copy(result[:], bank[:])
-            else:
-                for pair, copy in enumerate((nc.scalar.copy, nc.vector.tensor_copy)):
-                    bank = bank_tile(spare[pair], [P, 2, BLOCK])
-                    for b in range(2):
-                        for c in range(2):
-                            project(bank[:, c, :], 2 * pair + c, b, cols, (b, c) == (0, 0), (b, c) == (1, 1))
-                    copy(result[:, 2 * pair : 2 * pair + 2, :], bank[:])
+        def emit(first, count, numbers, copies, slot):
+            cols = slice(first * BLOCK, (first + count) * BLOCK)
+            share = (N // P) // len(numbers)
+            result = held([P, N // P, count * BLOCK], F32, slot)
+            banks = [bank_tile(number, [P, share, count * BLOCK]) for number in numbers]
+            for b in range(2):
+                for n, bank in enumerate(banks):
+                    for c in range(share):
+                        project(bank[:, c, :], n * share + c, b, cols, (b, c) == (0, 0), (b, c) == (1, share - 1))
+            for n, bank in enumerate(banks):
+                copies[n](result[:, n * share : (n + 1) * share, :], bank[:])
             nc.sync.dma_start(out_rows[:, :, cols], result[:])
 
-        for block in range(4, 8):
+        on_scalar = (nc.scalar.copy, nc.scalar.copy)
+        for pair in range(2):
+            finish(1, 2 * pair, late[2 * pair])
+            finish(1, 2 * pair + 1, late[2 * pair + 1])
+            scale_steps(batch, steps, batch[pair], HALF, HALF)
+            quantise_h(1, 2 * pair, 2)
+            emit(2 * pair, 2, spare[2 * pair : 2 * pair + 2], on_scalar, "raw00%d" % pair)
+        for block in range(4, 7):
             finish(1, block, late[block])
-            if block > 4:
-                quantise_h(1, block - 1, 1)
-                project_block(block - 1)
+        quantise_h(1, 4, 2)
+        emit(4, 2, spare[0:2], on_scalar, "raw010")
+        quantise_h(1, 6, 1)
+        emit(6, 1, spare[2:3], on_scalar, "raw011")
+        finish(1, 7, late[7])
         quantise_h(1, 7, 1)
-        project_block(7)
+        emit(7, 1, (spare[3], 0), (nc.scalar.copy, nc.vector.tensor_copy), "rounded00")

@@ -25,6 +25,7 @@ HALF = 512
 BLOCK = 128
 RUN = 4
 FLOOR = 1e-12
+LEAD = 4
 BATCHES = ((0, 1, 2), (3, 4, 5), (6, 7))
 
 
@@ -61,16 +62,11 @@ def tile_list_softplus_step_input_kernel(
             nc.sync.dma_start(words[:], tab_words[a].rearrange("p t i -> p (t i)").bitcast(I32))
             return words
 
-        def load_wa(b, a, pieces):
-            width = PASS // pieces
-            tiles = []
-            for n in range(pieces):
-                raw = held([P, PACK, width], F32, "raw%d%d%d" % (b, a, n))
-                first = b * PASS + n * width
-                rows = wa[a * PASS : (a + 1) * PASS, first : first + width]
-                nc.sync.dma_start(raw[:], rows.rearrange("(p j) c -> p j c", j=PACK))
-                tiles.append(raw)
-            return tiles
+        def load_wa(b, a):
+            raw = held([P, PACK, PASS], F32, "raw%d%d" % (b, a))
+            rows = wa[a * PASS : (a + 1) * PASS, b * PASS : (b + 1) * PASS]
+            nc.sync.dma_start(raw[:], rows.rearrange("(p j) c -> p j c", j=PACK))
+            return raw
 
         table = [load_table(0)]
         for q in range(4):
@@ -78,17 +74,12 @@ def tile_list_softplus_step_input_kernel(
                 tab_planes[32 * q : 32 * q + 8, :].bitcast(I32),
                 tab_scales[:, 4 * q : 4 * q + 4, :].bitcast(I32),
             )
-        wa_raw = {(0, a): load_wa(0, a, 2) for a in range(2)}
+        wa_raw = {(0, a): load_wa(0, a) for a in range(2)}
         table.append(load_table(1))
         for a in range(2):
-            wa_raw[1, a] = load_wa(1, a, 1)
+            wa_raw[1, a] = load_wa(1, a)
         wb_raw = held([P, 2, H // 2], I32, "wb_raw")
         nc.sync.dma_start(wb_raw[:], wb_words.rearrange("a p w -> p a w").bitcast(I32))
-        for q in range(4):
-            nc.sync.dma_start(
-                wb_planes[32 * q : 32 * q + 4, :, :].bitcast(I32),
-                wb_scales[:, 4 * q : 4 * q + 4, :].rearrange("a r c -> r a c").bitcast(I32),
-            )
         g_rows = gT.rearrange("(b m t e) n -> b t m e n", b=2, t=PACK, e=RUN)
         wo_rows = wo.rearrange("(b m t e) n -> b t m e n", b=2, t=PACK, e=RUN)
         factors = []
@@ -111,22 +102,26 @@ def tile_list_softplus_step_input_kernel(
             nc.vector.quantize_mx(out=codes[:].bitcast(E4M3), scales=plane[:], in_=rounded)
             return codes, plane
 
-        def round_wa(b, a, copy, slot):
+        def round_wa(b, a, copies, slot):
             rounded = held([P, PACK * PASS], BF16, slot)
             dealt = rounded[:].rearrange("p (t m e j) -> p m t j e", t=PACK, e=RUN, j=PACK)
-            share = (P // RUN) // len(wa_raw[b, a])
-            for n, raw in enumerate(wa_raw[b, a]):
-                copy(
-                    dealt[:, n * share : (n + 1) * share],
-                    raw[:].rearrange("p j (m t e) -> p m t j e", t=PACK, e=RUN),
-                )
+            source = wa_raw[b, a][:].rearrange("p j (m t e) -> p m t j e", t=PACK, e=RUN)
+            first = 0
+            for copy, share in copies:
+                copy(dealt[:, first : first + share], source[:, first : first + share])
+                first += share
             return rounded
 
         wa_quantised = {}
         nc.vector.tensor_copy(picked[0][:], table[0][:].bitcast(U32).indirect(offsets[:]))
         nc.vector.tensor_copy(picked_planes[:], tab_planes[:].indirect(offsets[:]))
+        runs = P // RUN
+        shares = (
+            [(nc.scalar.copy, runs)],
+            [(nc.scalar.copy, 12), (nc.vector.tensor_copy, runs - 12)],
+        )
         for a in range(2):
-            rounded = round_wa(0, a, nc.scalar.copy, "rounded0%d" % a)
+            rounded = round_wa(0, a, shares[a], "rounded0%d" % a)
             wa_quantised[0, a] = quantise(rounded[:], "wa0%d" % a)
         for half in range(2):
             nc.vector.tensor_copy(
@@ -134,16 +129,18 @@ def tile_list_softplus_step_input_kernel(
                 table[1][:].bitcast(U32).indirect(list_part(half * HALF, HALF)),
             )
 
-        for q in range(4):
+        for r in range(4):
             nc.sync.dma_start(
-                moved_plane[32 * q : 32 * q + 4, :].bitcast(I32),
-                picked_planes[32 * q + 4 : 32 * q + 8, :].bitcast(I32),
+                wb_planes[r:P:32, :, :].bitcast(I32),
+                wb_scales.rearrange("a (q r) c -> r q a c", r=4)[r].bitcast(I32),
             )
+        for r in range(4):
+            nc.sync.dma_start(moved_plane[r:P:32, :].bitcast(I32), picked_planes[4 + r : P : 32, :].bitcast(I32))
         for s in range(3, 6):
             load_factors(s)
         wo_raw = []
         for b in range(2):
-            raw = held([P, PACK, N], F32, "raw1%d0" % b)
+            raw = held([P, PACK, N], F32, "raw1%d" % b)
             for t in range(PACK):
                 nc.sync.dma_start(raw[:, t, :], wo_rows[b, t])
             wo_raw.append(raw)
@@ -173,7 +170,7 @@ def tile_list_softplus_step_input_kernel(
             banks = [bank_tile(n, [P, HALF]) for n in range(len(units))]
             order = [(n, a) for n in range(len(units)) for a in range(2)]
             if first_pass_ahead:
-                order = [(n, a) for a in range(2) for n in range(len(units))]
+                order = sorted(order, key=lambda na: (na[0] + LEAD * na[1], -na[1]))
             for n, a in order:
                 s, half = units[n]
                 codes, plane = wa_quantised[s // PACK, a]
@@ -204,9 +201,10 @@ def tile_list_softplus_step_input_kernel(
                 )
             return steps
 
-        def scale_steps(batch, steps, s, first, count):
+        def scale_steps(batch, steps, s, first, count, place=None):
+            place = first if place is None else place
             nc.vector.tensor_tensor(
-                work[:, s * S + first : s * S + first + count],
+                work[:, s * S + place : s * S + place + count],
                 factors[s][:].indirect(list_part(first, count)),
                 steps[:, s - batch[0], first : first + count],
                 MULT,
@@ -214,19 +212,14 @@ def tile_list_softplus_step_input_kernel(
 
         pending = logs_of(BATCHES[0], True)
 
-        rounded = round_wa(1, 0, nc.vector.tensor_copy, "tab_planes")
+        rounded = round_wa(1, 0, [(nc.vector.tensor_copy, runs)], "tab_planes")
         wa_quantised[1, 0] = quantise(rounded[:], "wa10")
-        rounded = round_wa(1, 1, nc.vector.tensor_copy, "table1")
+        rounded = round_wa(1, 1, [(nc.vector.tensor_copy, runs)], "table1")
         wb_codes = held([P, 4, PACK, P // RUN, 2], I32, "wb_codes")
         nc.vector.tensor_copy(
             wb_codes[:], wb_raw[:].rearrange("p a (b m t w) -> p (a b) t m w", b=2, t=PACK, w=2)
         )
         wa_quantised[1, 1] = quantise(rounded[:], "wa11")
-        wb_dealt_planes = held([P, 4, PACK, P // RUN], I32, "wb_dealt_planes")
-        nc.vector.tensor_copy(
-            wb_dealt_planes[:],
-            wb_planes[:].bitcast(I32).rearrange("p a (b m t) -> p (a b) t m", b=2, t=PACK),
-        )
 
         h_rounded = [held([P, S, PACK], BF16, "table0")]
         h_codes = [held([P, S], U32, "h_codes%d" % b) for b in range(2)]
@@ -249,12 +242,13 @@ def tile_list_softplus_step_input_kernel(
                     )
             return bank
 
-        def finish(b, block, bank):
+        def finish(b, block, bank, place=None):
             cols = slice(block * BLOCK, (block + 1) * BLOCK)
+            place = block * BLOCK if place is None else place
             nc.vector.tensor_tensor(
                 h_rounded[b][:, cols, :].rearrange("p (c i) t -> p c t i", i=4),
                 bank[:].rearrange("p t (c i) -> p c t i", i=4),
-                scaled[:, b * PACK : (b + 1) * PACK, cols].rearrange("p t (c i) -> p c t i", i=4),
+                scaled[:, b * PACK : (b + 1) * PACK, place : place + BLOCK].rearrange("p t (c i) -> p c t i", i=4),
                 MULT,
             )
 
@@ -273,18 +267,21 @@ def tile_list_softplus_step_input_kernel(
         scale_steps(batch, steps, 0, HALF, HALF)
         scale_steps(batch, steps, 1, 0, S)
         scale_steps(batch, steps, 2, 0, S)
+        wb_dealt_planes = held([P, 4, PACK, P // RUN], I32, "wb_dealt_planes")
+        nc.vector.tensor_copy(
+            wb_dealt_planes[:],
+            wb_planes[:].bitcast(I32).rearrange("p a (b m t) -> p (a b) t m", b=2, t=PACK),
+        )
         spare = (6, 7, 4, 5)
         batch = BATCHES[1]
         steps = guard(batch, *pending)
         pending = logs_of(BATCHES[2], False)
         scale_steps(batch, steps, 3, 0, HALF)
         scale_steps(batch, steps, 3, HALF, HALF)
-        rest = [(s, half) for half in range(2) for s in (4, 5)]
         for block in range(S // BLOCK):
             finish(0, block, inputs_of(0, block, spare[block % 4]))
-            if block % 2 == 1:
-                s, half = rest[block // 2]
-                scale_steps(batch, steps, s, half * HALF, HALF)
+            if block % 4 == 1:
+                scale_steps(batch, steps, 4 + block // 4, 0, HALF)
             if block == 4:
                 quantise_h(0, 0, 4)
         quantise_h(0, 4, 4)
@@ -296,6 +293,7 @@ def tile_list_softplus_step_input_kernel(
                 wo_raw[b][:].rearrange("p t (c i) -> p c t i", i=4),
             )
 
+        earlier = (batch, steps)
         batch = BATCHES[2]
         steps = guard(batch, *pending)
         for s in batch:
@@ -320,7 +318,7 @@ def tile_list_softplus_step_input_kernel(
         late += [inputs_of(1, block, block - 4) for block in range(4, 8)]
         out_rows = out.rearrange("(c p) s -> p c s", p=P)
 
-        def emit(first, count, numbers, copies, slot):
+        def emit(first, count, numbers, copies, slot, apart=False):
             cols = slice(first * BLOCK, (first + count) * BLOCK)
             share = (N // P) // len(numbers)
             result = held([P, N // P, count * BLOCK], F32, slot)
@@ -330,22 +328,33 @@ def tile_list_softplus_step_input_kernel(
                     for c in range(share):
                         project(bank[:, c, :], n * share + c, b, cols, (b, c) == (0, 0), (b, c) == (1, share - 1))
             for n, bank in enumerate(banks):
-                copies[n](result[:, n * share : (n + 1) * share, :], bank[:])
-            nc.sync.dma_start(out_rows[:, :, cols], result[:])
+                rows = slice(n * share, (n + 1) * share)
+                copies[n](result[:, rows, :], bank[:])
+                if apart:
+                    nc.sync.dma_start(out_rows[:, rows, cols], result[:, rows, :])
+            if not apart:
+                nc.sync.dma_start(out_rows[:, :, cols], result[:])
+
+        def scale_four(slices, first, count, place):
+            for s in slices:
+                scale_steps(*(earlier if s in earlier[0] else (batch, steps)), s, first, count, place)
 
         on_scalar = (nc.scalar.copy, nc.scalar.copy)
         for pair in range(2):
             finish(1, 2 * pair, late[2 * pair])
             finish(1, 2 * pair + 1, late[2 * pair + 1])
-            scale_steps(batch, steps, batch[pair], HALF, HALF)
+            scale_four((4 + 2 * pair, 5 + 2 * pair), HALF, 2 * BLOCK, HALF)
             quantise_h(1, 2 * pair, 2)
-            emit(2 * pair, 2, spare[2 * pair : 2 * pair + 2], on_scalar, "raw00%d" % pair)
-        for block in range(4, 7):
-            finish(1, block, late[block])
+            emit(2 * pair, 2, spare[2 * pair : 2 * pair + 2], on_scalar, "raw0%d" % pair)
+        finish(1, 4, late[4])
+        finish(1, 5, late[5])
+        scale_four((4, 5, 6, 7), 6 * BLOCK, BLOCK, HALF)
         quantise_h(1, 4, 2)
-        emit(4, 2, spare[0:2], on_scalar, "raw010")
+        emit(4, 2, spare[0:2], on_scalar, "rounded00")
+        finish(1, 6, late[6], HALF)
+        scale_four((4, 5, 6, 7), 7 * BLOCK, BLOCK, HALF)
         quantise_h(1, 6, 1)
-        emit(6, 1, spare[2:3], on_scalar, "raw011")
-        finish(1, 7, late[7])
+        emit(6, 1, spare[2:3], on_scalar, "rounded01")
+        finish(1, 7, late[7], HALF)
         quantise_h(1, 7, 1)
-        emit(7, 1, (spare[3], 0), (nc.scalar.copy, nc.vector.tensor_copy), "rounded00")
+        emit(7, 1, (spare[3], 0), (nc.scalar.copy, nc.vector.tensor_copy), "table0")

@@ -22,10 +22,12 @@ P = 128
 PACK = 4
 PASS = P * PACK
 HALF = 512
+QUARTER = 256
+STRIP = 64
 BLOCK = 128
 RUN = 4
 FLOOR = 1e-12
-LEAD = 4
+LEAD = 3
 BATCHES = ((0, 1, 2), (3, 4, 5), (6, 7))
 
 
@@ -120,13 +122,13 @@ def tile_list_softplus_step_input_kernel(
             [(nc.scalar.copy, runs)],
             [(nc.scalar.copy, 12), (nc.vector.tensor_copy, runs - 12)],
         )
+        first_rounded = [round_wa(0, a, shares[a], "rounded0%d" % a) for a in range(2)]
         for a in range(2):
-            rounded = round_wa(0, a, shares[a], "rounded0%d" % a)
-            wa_quantised[0, a] = quantise(rounded[:], "wa0%d" % a)
-        for half in range(2):
+            wa_quantised[0, a] = quantise(first_rounded[a][:], "wa0%d" % a)
+        for first, count in ((0, QUARTER), (QUARTER, QUARTER), (HALF, HALF)):
             nc.vector.tensor_copy(
-                picked[1][:, half * HALF : (half + 1) * HALF],
-                table[1][:].bitcast(U32).indirect(list_part(half * HALF, HALF)),
+                picked[1][:, first : first + count],
+                table[1][:].bitcast(U32).indirect(list_part(first, count)),
             )
 
         for r in range(4):
@@ -157,34 +159,78 @@ def tile_list_softplus_step_input_kernel(
             rows = count - 2
             region = work[:, batch[0] * S : (batch[-1] + 1) * S].rearrange("p (r c) -> p r c", r=rows)
             strip = HALF // rows
-            places = [region[:, r : r + 1, 0:HALF] for r in range(rows)]
-            for n in range(2):
-                places.append(region[:, :, HALF + n * strip : HALF + (n + 1) * strip])
+            places = [region[:, r : r + 1, strip : strip + HALF] for r in range(rows)]
+            places.append(region[:, :, 0:strip])
+            places.append(region[:, :, HALF + strip : HALF + 2 * strip])
             return region, places
 
         def shaped(view, place):
             return view.rearrange("p (r c) -> p r c", r=place.shape[1])
 
-        def logs_of(batch, first_pass_ahead):
+        def multiply(target, s, cols, a, start, stop):
+            codes, plane = wa_quantised[s // PACK, a]
+            channels = slice(s % PACK * P, (s % PACK + 1) * P)
+            nc.tensor.matmul_mx(
+                out=target,
+                lhsT=codes[:, channels].bitcast(E4M3),
+                lhsT_scale=plane[:, channels],
+                rhs=picked[a][:, cols].bitcast(E4M3),
+                rhs_scale=picked_planes[4 * a : P, cols],
+                start=start,
+                stop=stop,
+            )
+
+        first_units = (
+            ((1, 2), 0, QUARTER),
+            ((0,), 0, HALF),
+            ((1, 2), QUARTER, QUARTER),
+            ((0,), HALF, HALF),
+            ((1,), HALF, HALF),
+            ((2,), HALF, HALF),
+        )
+        first_rows = (1, 2, 3, 4, 0)
+
+        def first_logs():
+            banks = [bank_tile(n, [P, len(unit[0]), unit[2]]) for n, unit in enumerate(first_units)]
+            order = [(n, turn) for turn in range(2) for n in range(LEAD)]
+            order += [(n, turn) for n in range(LEAD, len(banks)) for turn in range(2)]
+            for n, turn in order:
+                slices, first, count = first_units[n]
+                a = turn if n < LEAD else 1 - turn
+                for k, s in enumerate(slices):
+                    opens, closes = (turn, k) == (0, 0), (turn, k) == (1, len(slices) - 1)
+                    multiply(banks[n][:, k, :], s, slice(first, first + count), a, opens, closes)
+            strips = HALF // STRIP
+            region = work[:, HALF : HALF + strips * (HALF + STRIP)].rearrange("p (r c) -> p r c", r=strips)
+            views = [bank[:] for bank in banks[:-1]] + [banks[-1][:, 0, :].rearrange("p (r c) -> p r c", c=STRIP)]
+            places = [
+                region[:, row, 0:HALF].rearrange("p (r c) -> p r c", r=view.shape[1])
+                for row, view in zip(first_rows, views)
+            ]
+            places.append(region[:, :, HALF:])
+            for view, logs in zip(views, places):
+                nc.scalar.activation(logs, view, SIGMOID, scale=-1.0)
+            parts = [region[:, row, :] for row in first_rows]
+            parts.insert(len(parts) - 1, region[:, len(first_rows) :, HALF:])
+            for part in parts:
+                nc.scalar.activation(part, part, LN, bias=FLOOR)
+            return views, places
+
+        def first_guard(banks, places):
+            steps = ring.tile([P, 3, S], F32, name="steps", bufs=2)
+            for (slices, first, count), bank, logs in zip(first_units, banks, places):
+                target = steps[:, slices[0] : slices[-1] + 1, first : first + count]
+                if len(slices) == 1:
+                    target = shaped(target[:, 0, :], logs)
+                nc.vector.scalar_tensor_tensor(target, logs, -1.0, bank, MULT, MAX)
+            return steps
+
+        def logs_of(batch):
             units = units_of(batch)
             banks = [bank_tile(n, [P, HALF]) for n in range(len(units))]
-            order = [(n, a) for n in range(len(units)) for a in range(2)]
-            if first_pass_ahead:
-                order = sorted(order, key=lambda na: (na[0] + LEAD * na[1], -na[1]))
-            for n, a in order:
-                s, half = units[n]
-                codes, plane = wa_quantised[s // PACK, a]
-                channels = slice(s % PACK * P, (s % PACK + 1) * P)
-                cols = slice(half * HALF, (half + 1) * HALF)
-                nc.tensor.matmul_mx(
-                    out=banks[n][:],
-                    lhsT=codes[:, channels].bitcast(E4M3),
-                    lhsT_scale=plane[:, channels],
-                    rhs=picked[a][:, cols].bitcast(E4M3),
-                    rhs_scale=picked_planes[4 * a : P, cols],
-                    start=(a == 0),
-                    stop=(a == 1),
-                )
+            for (s, half), bank in zip(units, banks):
+                for a in range(2):
+                    multiply(bank[:], s, slice(half * HALF, (half + 1) * HALF), a, a == 0, a == 1)
             region, places = log_parts(batch)
             for bank, place in zip(banks, places):
                 nc.scalar.activation(place, shaped(bank[:], place), SIGMOID, scale=-1.0)
@@ -210,7 +256,7 @@ def tile_list_softplus_step_input_kernel(
                 MULT,
             )
 
-        pending = logs_of(BATCHES[0], True)
+        pending = first_logs()
 
         rounded = round_wa(1, 0, [(nc.vector.tensor_copy, runs)], "tab_planes")
         wa_quantised[1, 0] = quantise(rounded[:], "wa10")
@@ -261,12 +307,10 @@ def tile_list_softplus_step_input_kernel(
             )
 
         batch = BATCHES[0]
-        steps = guard(batch, *pending)
-        pending = logs_of(BATCHES[1], False)
-        scale_steps(batch, steps, 0, 0, HALF)
-        scale_steps(batch, steps, 0, HALF, HALF)
-        scale_steps(batch, steps, 1, 0, S)
-        scale_steps(batch, steps, 2, 0, S)
+        steps = first_guard(*pending)
+        pending = logs_of(BATCHES[1])
+        for s in batch:
+            scale_steps(batch, steps, s, 0, S)
         wb_dealt_planes = held([P, 4, PACK, P // RUN], I32, "wb_dealt_planes")
         nc.vector.tensor_copy(
             wb_dealt_planes[:],
@@ -275,7 +319,7 @@ def tile_list_softplus_step_input_kernel(
         spare = (6, 7, 4, 5)
         batch = BATCHES[1]
         steps = guard(batch, *pending)
-        pending = logs_of(BATCHES[2], False)
+        pending = logs_of(BATCHES[2])
         scale_steps(batch, steps, 3, 0, HALF)
         scale_steps(batch, steps, 3, HALF, HALF)
         for block in range(S // BLOCK):
@@ -352,9 +396,9 @@ def tile_list_softplus_step_input_kernel(
         quantise_h(1, 4, 2)
         emit(4, 2, spare[0:2], on_scalar, "rounded00")
         finish(1, 6, late[6], HALF)
-        scale_four((4, 5, 6, 7), 7 * BLOCK, BLOCK, HALF)
+        scale_four((4, 5, 6, 7), 7 * BLOCK, BLOCK, HALF + BLOCK)
         quantise_h(1, 6, 1)
         emit(6, 1, spare[2:3], on_scalar, "rounded01")
-        finish(1, 7, late[7], HALF)
+        finish(1, 7, late[7], HALF + BLOCK)
         quantise_h(1, 7, 1)
         emit(7, 1, (spare[3], 0), (nc.scalar.copy, nc.vector.tensor_copy), "table0")

@@ -358,8 +358,8 @@ def tile_list_softplus_step_input_kernel(
                 stop=stop,
             )
 
-        late = [inputs_of(1, block, spare[block]) for block in range(4)]
-        late += [inputs_of(1, block, block - 4) for block in range(4, 8)]
+        late_banks = (4, 5, 0, 1, 6, 7)
+        late = {block: inputs_of(1, block, late_banks[block]) for block in (4, 5, 0, 1, 2, 3)}
         out_rows = out.rearrange("(c p) s -> p c s", p=P)
 
         def emit(first, count, numbers, copies, slot, apart=False):
@@ -389,16 +389,18 @@ def tile_list_softplus_step_input_kernel(
             finish(1, 2 * pair + 1, late[2 * pair + 1])
             scale_four((4 + 2 * pair, 5 + 2 * pair), HALF, 2 * BLOCK, HALF)
             quantise_h(1, 2 * pair, 2)
-            emit(2 * pair, 2, spare[2 * pair : 2 * pair + 2], on_scalar, "raw0%d" % pair)
+            emit(2 * pair, 2, ((2, 3), (4, 5))[pair], on_scalar, "raw0%d" % pair)
         finish(1, 4, late[4])
+        late[6] = inputs_of(1, 6, late_banks[4])
         finish(1, 5, late[5])
+        late[7] = inputs_of(1, 7, late_banks[5])
         scale_four((4, 5, 6, 7), 6 * BLOCK, BLOCK, HALF)
         quantise_h(1, 4, 2)
-        emit(4, 2, spare[0:2], on_scalar, "rounded00")
+        emit(4, 2, (0, 1), on_scalar, "rounded00")
         finish(1, 6, late[6], HALF)
         scale_four((4, 5, 6, 7), 7 * BLOCK, BLOCK, HALF + BLOCK)
         quantise_h(1, 6, 1)
-        emit(6, 1, spare[2:3], on_scalar, "rounded01")
+        emit(6, 1, (2,), on_scalar, "rounded01")
         finish(1, 7, late[7], HALF + BLOCK)
         quantise_h(1, 7, 1)
-        emit(7, 1, (spare[3], 0), (nc.scalar.copy, nc.vector.tensor_copy), "table0")
+        emit(7, 1, (3, 4), (nc.scalar.copy, nc.vector.tensor_copy), "table0", True)

@@ -38,7 +38,6 @@ def tile_list_softplus_step_input_kernel(
     with ExitStack() as ctx:
         lists = ctx.enter_context(tc.tile_pool(name="lists", bufs=1))
         keep = ctx.enter_context(tc.tile_pool(name="keep", bufs=1))
-        ring = ctx.enter_context(tc.tile_pool(name="ring", bufs=2))
         psum = ctx.enter_context(tc.psum_pool(name="psum", bufs=1))
 
         def held(shape, dtype, name):
@@ -91,8 +90,7 @@ def tile_list_softplus_step_input_kernel(
             nc.sync.dma_start(rows[:], g_rows[s // PACK, s % PACK])
             factors.append(rows)
 
-        for s in range(3):
-            load_factors(s)
+        load_factors(0)
 
         picked = [held([P, S], U32, "picked%d" % a) for a in range(2)]
         picked_planes = held([P, S], U8, "picked_planes")
@@ -138,7 +136,7 @@ def tile_list_softplus_step_input_kernel(
             )
         for r in range(4):
             nc.sync.dma_start(moved_plane[r:P:32, :].bitcast(I32), picked_planes[4 + r : P : 32, :].bitcast(I32))
-        for s in range(3, 6):
+        for s in range(1, 6):
             load_factors(s)
         wo_raw = []
         for b in range(2):
@@ -154,10 +152,9 @@ def tile_list_softplus_step_input_kernel(
         def units_of(batch):
             return [(s, half) for half in range(2) for s in batch]
 
-        def log_parts(batch):
-            count = 2 * len(batch)
+        def log_parts(span, count):
             rows = count - 2
-            region = work[:, batch[0] * S : (batch[-1] + 1) * S].rearrange("p (r c) -> p r c", r=rows)
+            region = span.rearrange("p (r c) -> p r c", r=rows)
             strip = HALF // rows
             places = [region[:, r : r + 1, strip : strip + HALF] for r in range(rows)]
             places.append(region[:, :, 0:strip])
@@ -217,7 +214,7 @@ def tile_list_softplus_step_input_kernel(
             return views, places
 
         def first_guard(banks, places):
-            steps = ring.tile([P, 3, S], F32, name="steps", bufs=2)
+            steps = held([P, 3, S], F32, "steps")
             for (slices, first, count), bank, logs in zip(first_units, banks, places):
                 target = steps[:, slices[0] : slices[-1] + 1, first : first + count]
                 if len(slices) == 1:
@@ -225,21 +222,25 @@ def tile_list_softplus_step_input_kernel(
                 nc.vector.scalar_tensor_tensor(target, logs, -1.0, bank, MULT, MAX)
             return steps
 
-        def logs_of(batch):
+        def logs_of(batch, numbers, slot=None):
             units = units_of(batch)
-            banks = [bank_tile(n, [P, HALF]) for n in range(len(units))]
+            banks = [bank_tile(number, [P, HALF]) for number in numbers]
             for (s, half), bank in zip(units, banks):
                 for a in range(2):
                     multiply(bank[:], s, slice(half * HALF, (half + 1) * HALF), a, a == 0, a == 1)
-            region, places = log_parts(batch)
-            for bank, place in zip(banks, places):
-                nc.scalar.activation(place, shaped(bank[:], place), SIGMOID, scale=-1.0)
+            region, places = log_parts(work[:, batch[0] * S : (batch[-1] + 1) * S], len(units))
+            before, targets = region, places
+            if slot:
+                gates = held([P, len(units) * HALF], F32, slot)
+                before, targets = log_parts(gates[:], len(units))
+            for bank, target in zip(banks, targets):
+                nc.scalar.activation(target, shaped(bank[:], target), SIGMOID, scale=-1.0)
             for r in range(region.shape[1]):
-                nc.scalar.activation(region[:, r, :], region[:, r, :], LN, bias=FLOOR)
+                nc.scalar.activation(region[:, r, :], before[:, r, :], LN, bias=FLOOR)
             return banks, places
 
-        def guard(batch, banks, places):
-            steps = ring.tile([P, 3, S], F32, name="steps", bufs=2)
+        def guard(batch, banks, places, slot):
+            steps = held([P, 3, S], F32, slot)
             for (s, half), bank, place in zip(units_of(batch), banks, places):
                 target = steps[:, s - batch[0], half * HALF : (half + 1) * HALF]
                 nc.vector.scalar_tensor_tensor(
@@ -298,6 +299,17 @@ def tile_list_softplus_step_input_kernel(
                 MULT,
             )
 
+        def finish_aside(b, block, bank, slot):
+            cols = slice(block * BLOCK, (block + 1) * BLOCK)
+            woven = held([P, BLOCK, PACK], F32, slot)
+            nc.scalar.copy(woven[:], bank[:].rearrange("p t n -> p n t"))
+            return lambda: nc.gpsimd.tensor_tensor(
+                h_rounded[b][:, cols, :],
+                woven[:],
+                scaled[:, b * PACK : (b + 1) * PACK, cols].rearrange("p t n -> p n t"),
+                MULT,
+            )
+
         def quantise_h(b, first, count):
             cols = slice(first * BLOCK, (first + count) * BLOCK)
             nc.vector.quantize_mx(
@@ -308,26 +320,27 @@ def tile_list_softplus_step_input_kernel(
 
         batch = BATCHES[0]
         steps = first_guard(*pending)
-        pending = logs_of(BATCHES[1])
-        for s in batch:
-            scale_steps(batch, steps, s, 0, S)
         wb_dealt_planes = held([P, 4, PACK, P // RUN], I32, "wb_dealt_planes")
         nc.vector.tensor_copy(
             wb_dealt_planes[:],
             wb_planes[:].bitcast(I32).rearrange("p a (b m t) -> p (a b) t m", b=2, t=PACK),
         )
+        pending = logs_of(BATCHES[1], range(6))
+        for s in batch:
+            scale_steps(batch, steps, s, 0, S)
         spare = (6, 7, 4, 5)
         batch = BATCHES[1]
-        steps = guard(batch, *pending)
-        pending = logs_of(BATCHES[2])
-        scale_steps(batch, steps, 3, 0, HALF)
-        scale_steps(batch, steps, 3, HALF, HALF)
-        for block in range(S // BLOCK):
-            finish(0, block, inputs_of(0, block, spare[block % 4]))
-            if block % 4 == 1:
-                scale_steps(batch, steps, 4 + block // 4, 0, HALF)
-            if block == 4:
-                quantise_h(0, 0, 4)
+        steps = guard(batch, *pending, "steps")
+        aside = [finish_aside(0, block, inputs_of(0, block, block - 4), "rounded0%d" % (block % 2)) for block in (4, 5)]
+        pending = logs_of(BATCHES[2], (2, 3, 0, 1), "wa11_codes")
+        scale_steps(batch, steps, 3, 0, S)
+        scale_steps(batch, steps, 4, 0, HALF)
+        for product in aside:
+            product()
+        for block, number in zip((0, 1, 2, 3, 6, 7), (6, 7, 4, 5, 6, 7)):
+            finish(0, block, inputs_of(0, block, number))
+        quantise_h(0, 0, 4)
+        scale_steps(batch, steps, 5, 0, HALF)
         quantise_h(0, 4, 4)
         wo_quantised = []
         wo_rounded = held([P, 2, N, PACK], BF16, "wa11_codes")
@@ -339,7 +352,7 @@ def tile_list_softplus_step_input_kernel(
 
         earlier = (batch, steps)
         batch = BATCHES[2]
-        steps = guard(batch, *pending)
+        steps = guard(batch, *pending, "late_steps")
         for s in batch:
             scale_steps(batch, steps, s, 0, HALF)
         for b in range(2):
@@ -358,8 +371,9 @@ def tile_list_softplus_step_input_kernel(
                 stop=stop,
             )
 
-        late_banks = (4, 5, 0, 1, 6, 7)
-        late = {block: inputs_of(1, block, late_banks[block]) for block in (4, 5, 0, 1, 2, 3)}
+        late_banks = (4, 5, 3, 2, 6, 7)
+        late = {block: inputs_of(1, block, late_banks[block]) for block in (4, 5, 0, 1, 3, 2)}
+        aside = finish_aside(1, 3, late[3], "wb_raw")
         out_rows = out.rearrange("(c p) s -> p c s", p=P)
 
         def emit(first, count, numbers, copies, slot, apart=False):
@@ -384,23 +398,24 @@ def tile_list_softplus_step_input_kernel(
                 scale_steps(*(earlier if s in earlier[0] else (batch, steps)), s, first, count, place)
 
         on_scalar = (nc.scalar.copy, nc.scalar.copy)
+        aside()
+        for block in range(3):
+            finish(1, block, late[block])
         for pair in range(2):
-            finish(1, 2 * pair, late[2 * pair])
-            finish(1, 2 * pair + 1, late[2 * pair + 1])
             scale_four((4 + 2 * pair, 5 + 2 * pair), HALF, 2 * BLOCK, HALF)
             quantise_h(1, 2 * pair, 2)
-            emit(2 * pair, 2, ((2, 3), (4, 5))[pair], on_scalar, "raw0%d" % pair)
+            emit(2 * pair, 2, ((0, 1), (4, 5))[pair], on_scalar, "raw0%d" % pair)
         finish(1, 4, late[4])
         late[6] = inputs_of(1, 6, late_banks[4])
         finish(1, 5, late[5])
         late[7] = inputs_of(1, 7, late_banks[5])
         scale_four((4, 5, 6, 7), 6 * BLOCK, BLOCK, HALF)
         quantise_h(1, 4, 2)
-        emit(4, 2, (0, 1), on_scalar, "rounded00")
+        emit(4, 2, (2, 3), on_scalar, "rounded00")
         finish(1, 6, late[6], HALF)
         scale_four((4, 5, 6, 7), 7 * BLOCK, BLOCK, HALF + BLOCK)
         quantise_h(1, 6, 1)
-        emit(6, 1, (2,), on_scalar, "rounded01")
+        emit(6, 1, (0,), on_scalar, "rounded01")
         finish(1, 7, late[7], HALF + BLOCK)
         quantise_h(1, 7, 1)
-        emit(7, 1, (3, 4), (nc.scalar.copy, nc.vector.tensor_copy), "table0", True)
+        emit(7, 1, (1, 4), (nc.scalar.copy, nc.vector.tensor_copy), "table0", True)

@@ -14,6 +14,7 @@ U8 = mybir.dt.uint8
 E4M3 = mybir.dt.float8_e4m3fn_x4
 E2M1 = mybir.dt.float4_e2m1fn_x4
 MULT = mybir.AluOpType.mult
+ADD = mybir.AluOpType.add
 MAX = mybir.AluOpType.max
 SIGMOID = mybir.ActivationFunctionType.Sigmoid
 LN = mybir.ActivationFunctionType.Ln
@@ -95,9 +96,9 @@ def tile_list_softplus_step_input_kernel(
         picked = [held([P, S], U32, "picked%d" % a) for a in range(2)]
         picked_planes = held([P, S], U8, "picked_planes")
 
-        def quantise(rounded, name):
+        def quantise(rounded, name, slot=None):
             width = rounded.shape[1] // PACK
-            codes = held([P, width], U32, name + "_codes")
+            codes = held([P, width], U32, slot or name + "_codes")
             plane = held([P, width], U8, name + "_plane")
             nc.vector.quantize_mx(out=codes[:].bitcast(E4M3), scales=plane[:], in_=rounded)
             return codes, plane
@@ -136,14 +137,20 @@ def tile_list_softplus_step_input_kernel(
             )
         for r in range(4):
             nc.sync.dma_start(moved_plane[r:P:32, :].bitcast(I32), picked_planes[4 + r : P : 32, :].bitcast(I32))
-        for s in range(1, 6):
+        for s in range(1, 3):
             load_factors(s)
         wo_raw = []
-        for b in range(2):
+
+        def load_wo(b):
             raw = held([P, PACK, N], F32, "raw1%d" % b)
             for t in range(PACK):
                 nc.sync.dma_start(raw[:, t, :], wo_rows[b, t])
             wo_raw.append(raw)
+
+        load_wo(0)
+        for s in range(3, 6):
+            load_factors(s)
+        load_wo(1)
         for s in range(6, 8):
             load_factors(s)
 
@@ -321,7 +328,7 @@ def tile_list_softplus_step_input_kernel(
         batch = BATCHES[0]
         steps = first_guard(*pending)
         wb_dealt_planes = held([P, 4, PACK, P // RUN], I32, "wb_dealt_planes")
-        nc.vector.tensor_copy(
+        nc.gpsimd.tensor_copy(
             wb_dealt_planes[:],
             wb_planes[:].bitcast(I32).rearrange("p a (b m t) -> p (a b) t m", b=2, t=PACK),
         )
@@ -330,33 +337,39 @@ def tile_list_softplus_step_input_kernel(
             scale_steps(batch, steps, s, 0, S)
         spare = (6, 7, 4, 5)
         batch = BATCHES[1]
+        wo_rounded = [held([P, N, PACK], BF16, "factors2")]
+        nc.gpsimd.tensor_scalar(wo_rounded[0][:], wo_raw[0][:].rearrange("p t n -> p n t"), 1.0, 0.0, MULT, ADD)
         steps = guard(batch, *pending, "steps")
         aside = [finish_aside(0, block, inputs_of(0, block, block - 4), "rounded0%d" % (block % 2)) for block in (4, 5)]
         pending = logs_of(BATCHES[2], (2, 3, 0, 1), "wa11_codes")
-        scale_steps(batch, steps, 3, 0, S)
+        scale_steps(batch, steps, 3, 0, HALF)
         scale_steps(batch, steps, 4, 0, HALF)
+        scale_steps(batch, steps, 3, HALF, HALF)
         for product in aside:
             product()
-        for block, number in zip((0, 1, 2, 3, 6, 7), (6, 7, 4, 5, 6, 7)):
+        for block, number in zip((0, 1, 2, 3, 6), (6, 7, 4, 5, 6)):
             finish(0, block, inputs_of(0, block, number))
         quantise_h(0, 0, 4)
         scale_steps(batch, steps, 5, 0, HALF)
-        quantise_h(0, 4, 4)
+        for s in (4, 5):
+            scale_steps(batch, steps, s, HALF, QUARTER)
+        finish_aside(0, 7, inputs_of(0, 7, 6), "rounded00")()
         wo_quantised = []
-        wo_rounded = held([P, 2, N, PACK], BF16, "wa11_codes")
-        for b in range(2):
-            nc.scalar.copy(
-                wo_rounded[:, b].rearrange("p (c i) t -> p c t i", i=4),
-                wo_raw[b][:].rearrange("p t (c i) -> p c t i", i=4),
-            )
+        wo_rounded.append(held([P, N, PACK], BF16, "wa11_codes"))
+        nc.scalar.copy(
+            wo_rounded[1][:].rearrange("p (c i) t -> p c t i", i=4),
+            wo_raw[1][:].rearrange("p t (c i) -> p c t i", i=4),
+        )
 
         earlier = (batch, steps)
         batch = BATCHES[2]
         steps = guard(batch, *pending, "late_steps")
+        quantise_h(0, 4, 4)
         for s in batch:
             scale_steps(batch, steps, s, 0, HALF)
         for b in range(2):
-            wo_quantised.append(quantise(wo_rounded[:, b].rearrange("p n t -> p (n t)"), "wo%d" % b))
+            rounded = wo_rounded[b][:].rearrange("p n t -> p (n t)")
+            wo_quantised.append(quantise(rounded, "wo%d" % b, ("rounded01", None)[b]))
         h_rounded.append(held([P, S, PACK], BF16, "wa11_codes"))
 
         def project(target, c, b, cols, start, stop):
@@ -371,7 +384,7 @@ def tile_list_softplus_step_input_kernel(
                 stop=stop,
             )
 
-        late_banks = (4, 5, 3, 2, 6, 7)
+        late_banks = (4, 5, 3, 2, 7, 6)
         late = {block: inputs_of(1, block, late_banks[block]) for block in (4, 5, 0, 1, 3, 2)}
         aside = finish_aside(1, 3, late[3], "wb_raw")
         out_rows = out.rearrange("(c p) s -> p c s", p=P)
@@ -402,7 +415,7 @@ def tile_list_softplus_step_input_kernel(
         for block in range(3):
             finish(1, block, late[block])
         for pair in range(2):
-            scale_four((4 + 2 * pair, 5 + 2 * pair), HALF, 2 * BLOCK, HALF)
+            scale_four((6 + pair,), HALF, QUARTER, HALF)
             quantise_h(1, 2 * pair, 2)
             emit(2 * pair, 2, ((0, 1), (4, 5))[pair], on_scalar, "raw0%d" % pair)
         finish(1, 4, late[4])
@@ -415,7 +428,7 @@ def tile_list_softplus_step_input_kernel(
         finish(1, 6, late[6], HALF)
         scale_four((4, 5, 6, 7), 7 * BLOCK, BLOCK, HALF + BLOCK)
         quantise_h(1, 6, 1)
-        emit(6, 1, (0,), on_scalar, "rounded01")
+        emit(6, 1, (0,), on_scalar, "factors3")
         finish(1, 7, late[7], HALF + BLOCK)
         quantise_h(1, 7, 1)
         emit(7, 1, (1, 4), (nc.scalar.copy, nc.vector.tensor_copy), "table0", True)

@@ -22,14 +22,17 @@ LN = mybir.ActivationFunctionType.Ln
 P = 128
 PACK = 4
 PASS = P * PACK
+QUADRANT = 32
+ROWS = 4
+RUN = 4
+LINE = 4
 HALF = 512
 QUARTER = 256
-STRIP = 64
 BLOCK = 128
-RUN = 4
 FLOOR = 1e-12
-LEAD = 3
 BATCHES = ((0, 1, 2), (3, 4, 5), (6, 7))
+LEAD = 4
+STRIP = 64
 
 
 def tile_list_softplus_step_input_kernel(
@@ -41,8 +44,8 @@ def tile_list_softplus_step_input_kernel(
         keep = ctx.enter_context(tc.tile_pool(name="keep", bufs=1))
         psum = ctx.enter_context(tc.psum_pool(name="psum", bufs=1))
 
-        def held(shape, dtype, name):
-            return keep.tile(shape, dtype, name=name, align_bytes=64)
+        def held(shape, dtype, slot):
+            return keep.tile(shape, dtype, name=slot, align_bytes=64)
 
         def bank_tile(number, shape):
             return psum.tile(shape, F32, name="bank%d" % number)
@@ -59,6 +62,7 @@ def tile_list_softplus_step_input_kernel(
         nc.vector.memset(tab_planes[:].bitcast(I32), 0)
         nc.vector.memset(wb_planes[:].rearrange("p a c -> p (a c)").bitcast(I32), 0)
         nc.vector.memset(moved_plane[:].bitcast(I32), 0)
+
         def load_table(a):
             words = held([P, T], I32, "table%d" % a)
             nc.sync.dma_start(words[:], tab_words[a].rearrange("p t i -> p (t i)").bitcast(I32))
@@ -71,10 +75,10 @@ def tile_list_softplus_step_input_kernel(
             return raw
 
         table = [load_table(0)]
-        for q in range(4):
+        for q in range(P // QUADRANT):
             nc.sync.dma_start(
-                tab_planes[32 * q : 32 * q + 8, :].bitcast(I32),
-                tab_scales[:, 4 * q : 4 * q + 4, :].bitcast(I32),
+                tab_planes[QUADRANT * q : QUADRANT * q + 2 * ROWS, :].bitcast(I32),
+                tab_scales[:, ROWS * q : ROWS * (q + 1), :].bitcast(I32),
             )
         wa_raw = {(0, a): load_wa(0, a) for a in range(2)}
         table.append(load_table(1))
@@ -82,6 +86,11 @@ def tile_list_softplus_step_input_kernel(
             wa_raw[1, a] = load_wa(1, a)
         wb_raw = held([P, 2, H // 2], I32, "wb_raw")
         nc.sync.dma_start(wb_raw[:], wb_words.rearrange("a p w -> p a w").bitcast(I32))
+        for r in range(ROWS):
+            nc.sync.dma_start(
+                wb_planes[r:P:QUADRANT, :, :].bitcast(I32),
+                wb_scales.rearrange("a (q r) c -> r q a c", r=ROWS)[r].bitcast(I32),
+            )
         g_rows = gT.rearrange("(b m t e) n -> b t m e n", b=2, t=PACK, e=RUN)
         wo_rows = wo.rearrange("(b m t e) n -> b t m e n", b=2, t=PACK, e=RUN)
         factors = []
@@ -95,6 +104,7 @@ def tile_list_softplus_step_input_kernel(
 
         picked = [held([P, S], U32, "picked%d" % a) for a in range(2)]
         picked_planes = held([P, S], U8, "picked_planes")
+        wa_quantised = {}
 
         def quantise(rounded, name, slot=None):
             width = rounded.shape[1] // PACK
@@ -103,41 +113,38 @@ def tile_list_softplus_step_input_kernel(
             nc.vector.quantize_mx(out=codes[:].bitcast(E4M3), scales=plane[:], in_=rounded)
             return codes, plane
 
-        def round_wa(b, a, copies, slot):
-            rounded = held([P, PACK * PASS], BF16, slot)
-            dealt = rounded[:].rearrange("p (t m e j) -> p m t j e", t=PACK, e=RUN, j=PACK)
+        def round_wa(b, a, first, count, copy, slot):
+            rounded = held([P, count * PASS], BF16, slot)
+            dealt = rounded[:].rearrange("p (t m e j) -> p m t j e", t=count, e=RUN, j=PACK)
             source = wa_raw[b, a][:].rearrange("p j (m t e) -> p m t j e", t=PACK, e=RUN)
-            first = 0
-            for copy, share in copies:
-                copy(dealt[:, first : first + share], source[:, first : first + share])
-                first += share
+            copy(dealt, source[:, :, first : first + count])
             return rounded
 
-        wa_quantised = {}
+        def quantise_wa(b, a, first, rounded):
+            codes, plane = quantise(rounded[:], "wa%d%d%d" % (b, a, first))
+            for t in range(rounded.shape[1] // PASS):
+                cols = slice(t * P, (t + 1) * P)
+                wa_quantised[PACK * b + first + t, a] = (codes[:, cols], plane[:, cols])
+
         nc.vector.tensor_copy(picked[0][:], table[0][:].bitcast(U32).indirect(offsets[:]))
         nc.vector.tensor_copy(picked_planes[:], tab_planes[:].indirect(offsets[:]))
-        runs = P // RUN
-        shares = (
-            [(nc.scalar.copy, runs)],
-            [(nc.scalar.copy, 12), (nc.vector.tensor_copy, runs - 12)],
-        )
-        first_rounded = [round_wa(0, a, shares[a], "rounded0%d" % a) for a in range(2)]
-        for a in range(2):
-            wa_quantised[0, a] = quantise(first_rounded[a][:], "wa0%d" % a)
+        quantise_wa(0, 0, 0, round_wa(0, 0, 0, PACK, nc.scalar.copy, "rounded00"))
+        scalar_share = round_wa(0, 1, 0, 2, nc.scalar.copy, "rounded01")
+        vector_share = round_wa(0, 1, 2, 2, nc.vector.tensor_copy, "rounded00")
+        quantise_wa(0, 1, 0, scalar_share)
+        quantise_wa(0, 1, 2, vector_share)
         for first, count in ((0, QUARTER), (QUARTER, QUARTER), (HALF, HALF)):
             nc.vector.tensor_copy(
                 picked[1][:, first : first + count],
                 table[1][:].bitcast(U32).indirect(list_part(first, count)),
             )
 
-        for r in range(4):
+        for r in range(ROWS):
             nc.sync.dma_start(
-                wb_planes[r:P:32, :, :].bitcast(I32),
-                wb_scales.rearrange("a (q r) c -> r q a c", r=4)[r].bitcast(I32),
+                moved_plane[r:P:QUADRANT, :].bitcast(I32),
+                picked_planes[ROWS + r : P : QUADRANT, :].bitcast(I32),
             )
-        for r in range(4):
-            nc.sync.dma_start(moved_plane[r:P:32, :].bitcast(I32), picked_planes[4 + r : P : 32, :].bitcast(I32))
-        for s in range(1, 3):
+        for s in BATCHES[0][1:]:
             load_factors(s)
         wo_raw = []
 
@@ -148,10 +155,10 @@ def tile_list_softplus_step_input_kernel(
             wo_raw.append(raw)
 
         load_wo(0)
-        for s in range(3, 6):
+        for s in BATCHES[1]:
             load_factors(s)
         load_wo(1)
-        for s in range(6, 8):
+        for s in BATCHES[2]:
             load_factors(s)
 
         work = held([P, 2 * PACK * S], F32, "work")
@@ -172,14 +179,13 @@ def tile_list_softplus_step_input_kernel(
             return view.rearrange("p (r c) -> p r c", r=place.shape[1])
 
         def multiply(target, s, cols, a, start, stop):
-            codes, plane = wa_quantised[s // PACK, a]
-            channels = slice(s % PACK * P, (s % PACK + 1) * P)
+            codes, plane = wa_quantised[s, a]
             nc.tensor.matmul_mx(
                 out=target,
-                lhsT=codes[:, channels].bitcast(E4M3),
-                lhsT_scale=plane[:, channels],
+                lhsT=codes.bitcast(E4M3),
+                lhsT_scale=plane,
                 rhs=picked[a][:, cols].bitcast(E4M3),
-                rhs_scale=picked_planes[4 * a : P, cols],
+                rhs_scale=picked_planes[ROWS * a : P, cols],
                 start=start,
                 stop=stop,
             )
@@ -207,47 +213,44 @@ def tile_list_softplus_step_input_kernel(
             strips = HALF // STRIP
             region = work[:, HALF : HALF + strips * (HALF + STRIP)].rearrange("p (r c) -> p r c", r=strips)
             views = [bank[:] for bank in banks[:-1]] + [banks[-1][:, 0, :].rearrange("p (r c) -> p r c", c=STRIP)]
-            places = [
-                region[:, row, 0:HALF].rearrange("p (r c) -> p r c", r=view.shape[1])
-                for row, view in zip(first_rows, views)
-            ]
+            places = [shaped(region[:, row, 0:HALF], view) for row, view in zip(first_rows, views)]
             places.append(region[:, :, HALF:])
-            for view, logs in zip(views, places):
-                nc.scalar.activation(logs, view, SIGMOID, scale=-1.0)
+            for view, place in zip(views, places):
+                nc.scalar.activation(place, view, SIGMOID, scale=-1.0)
             parts = [region[:, row, :] for row in first_rows]
             parts.insert(len(parts) - 1, region[:, len(first_rows) :, HALF:])
             for part in parts:
                 nc.scalar.activation(part, part, LN, bias=FLOOR)
             return views, places
 
-        def first_guard(banks, places):
-            steps = held([P, 3, S], F32, "steps")
-            for (slices, first, count), bank, logs in zip(first_units, banks, places):
+        def first_guard(views, places):
+            steps = held([P, len(BATCHES[0]), S], F32, "steps")
+            for (slices, first, count), view, place in zip(first_units, views, places):
                 target = steps[:, slices[0] : slices[-1] + 1, first : first + count]
                 if len(slices) == 1:
-                    target = shaped(target[:, 0, :], logs)
-                nc.vector.scalar_tensor_tensor(target, logs, -1.0, bank, MULT, MAX)
+                    target = shaped(target[:, 0, :], place)
+                nc.vector.scalar_tensor_tensor(target, place, -1.0, view, MULT, MAX)
             return steps
 
-        def logs_of(batch, numbers, slot=None):
+        def logs_of(batch, numbers, gate_slot=None):
             units = units_of(batch)
             banks = [bank_tile(number, [P, HALF]) for number in numbers]
             for (s, half), bank in zip(units, banks):
                 for a in range(2):
                     multiply(bank[:], s, slice(half * HALF, (half + 1) * HALF), a, a == 0, a == 1)
             region, places = log_parts(work[:, batch[0] * S : (batch[-1] + 1) * S], len(units))
-            before, targets = region, places
-            if slot:
-                gates = held([P, len(units) * HALF], F32, slot)
-                before, targets = log_parts(gates[:], len(units))
-            for bank, target in zip(banks, targets):
-                nc.scalar.activation(target, shaped(bank[:], target), SIGMOID, scale=-1.0)
+            gate_region, gate_places = region, places
+            if gate_slot:
+                gates = held([P, len(units) * HALF], F32, gate_slot)
+                gate_region, gate_places = log_parts(gates[:], len(units))
+            for bank, place in zip(banks, gate_places):
+                nc.scalar.activation(place, shaped(bank[:], place), SIGMOID, scale=-1.0)
             for r in range(region.shape[1]):
-                nc.scalar.activation(region[:, r, :], before[:, r, :], LN, bias=FLOOR)
+                nc.scalar.activation(region[:, r, :], gate_region[:, r, :], LN, bias=FLOOR)
             return banks, places
 
         def guard(batch, banks, places, slot):
-            steps = held([P, 3, S], F32, slot)
+            steps = held([P, len(BATCHES[0]), S], F32, slot)
             for (s, half), bank, place in zip(units_of(batch), banks, places):
                 target = steps[:, s - batch[0], half * HALF : (half + 1) * HALF]
                 nc.vector.scalar_tensor_tensor(
@@ -255,10 +258,10 @@ def tile_list_softplus_step_input_kernel(
                 )
             return steps
 
-        def scale_steps(batch, steps, s, first, count, place=None):
-            place = first if place is None else place
+        def scale_steps(batch, steps, s, first, count, column=None):
+            column = first if column is None else column
             nc.vector.tensor_tensor(
-                work[:, s * S + place : s * S + place + count],
+                work[:, s * S + column : s * S + column + count],
                 factors[s][:].indirect(list_part(first, count)),
                 steps[:, s - batch[0], first : first + count],
                 MULT,
@@ -266,14 +269,13 @@ def tile_list_softplus_step_input_kernel(
 
         pending = first_logs()
 
-        rounded = round_wa(1, 0, [(nc.vector.tensor_copy, runs)], "tab_planes")
-        wa_quantised[1, 0] = quantise(rounded[:], "wa10")
-        rounded = round_wa(1, 1, [(nc.vector.tensor_copy, runs)], "table1")
+        quantise_wa(1, 0, 0, round_wa(1, 0, 0, PACK, nc.vector.tensor_copy, "tab_planes"))
+        last_rounded = round_wa(1, 1, 0, PACK, nc.vector.tensor_copy, "table1")
         wb_codes = held([P, 4, PACK, P // RUN, 2], I32, "wb_codes")
         nc.vector.tensor_copy(
             wb_codes[:], wb_raw[:].rearrange("p a (b m t w) -> p (a b) t m w", b=2, t=PACK, w=2)
         )
-        wa_quantised[1, 1] = quantise(rounded[:], "wa11")
+        quantise_wa(1, 1, 0, last_rounded)
 
         h_rounded = [held([P, S, PACK], BF16, "table0")]
         h_codes = [held([P, S], U32, "h_codes%d" % b) for b in range(2)]
@@ -296,13 +298,14 @@ def tile_list_softplus_step_input_kernel(
                     )
             return bank
 
-        def finish(b, block, bank, place=None):
+        def finish(b, block, bank, column=None):
             cols = slice(block * BLOCK, (block + 1) * BLOCK)
-            place = block * BLOCK if place is None else place
+            column = block * BLOCK if column is None else column
+            sources = scaled[:, b * PACK : (b + 1) * PACK, column : column + BLOCK]
             nc.vector.tensor_tensor(
-                h_rounded[b][:, cols, :].rearrange("p (c i) t -> p c t i", i=4),
-                bank[:].rearrange("p t (c i) -> p c t i", i=4),
-                scaled[:, b * PACK : (b + 1) * PACK, place : place + BLOCK].rearrange("p t (c i) -> p c t i", i=4),
+                h_rounded[b][:, cols, :].rearrange("p (c i) t -> p c t i", i=LINE),
+                bank[:].rearrange("p t (c i) -> p c t i", i=LINE),
+                sources.rearrange("p t (c i) -> p c t i", i=LINE),
                 MULT,
             )
 
@@ -327,7 +330,7 @@ def tile_list_softplus_step_input_kernel(
 
         batch = BATCHES[0]
         steps = first_guard(*pending)
-        wb_dealt_planes = held([P, 4, PACK, P // RUN], I32, "wb_dealt_planes")
+        wb_dealt_planes = held([P, 4, PACK, P // RUN], I32, "table1")
         nc.gpsimd.tensor_copy(
             wb_dealt_planes[:],
             wb_planes[:].bitcast(I32).rearrange("p a (b m t) -> p (a b) t m", b=2, t=PACK),
@@ -335,13 +338,16 @@ def tile_list_softplus_step_input_kernel(
         pending = logs_of(BATCHES[1], range(6))
         for s in batch:
             scale_steps(batch, steps, s, 0, S)
-        spare = (6, 7, 4, 5)
+
         batch = BATCHES[1]
         wo_rounded = [held([P, N, PACK], BF16, "factors2")]
         nc.gpsimd.tensor_scalar(wo_rounded[0][:], wo_raw[0][:].rearrange("p t n -> p n t"), 1.0, 0.0, MULT, ADD)
         steps = guard(batch, *pending, "steps")
-        aside = [finish_aside(0, block, inputs_of(0, block, block - 4), "rounded0%d" % (block % 2)) for block in (4, 5)]
-        pending = logs_of(BATCHES[2], (2, 3, 0, 1), "wa11_codes")
+        aside = [
+            finish_aside(0, block, inputs_of(0, block, number), "rounded0%d" % number)
+            for number, block in enumerate((4, 5))
+        ]
+        pending = logs_of(BATCHES[2], (2, 3, 0, 1), "gates")
         scale_steps(batch, steps, 3, 0, HALF)
         scale_steps(batch, steps, 4, 0, HALF)
         scale_steps(batch, steps, 3, HALF, HALF)
@@ -354,23 +360,23 @@ def tile_list_softplus_step_input_kernel(
         for s in (4, 5):
             scale_steps(batch, steps, s, HALF, QUARTER)
         finish_aside(0, 7, inputs_of(0, 7, 6), "rounded00")()
-        wo_quantised = []
-        wo_rounded.append(held([P, N, PACK], BF16, "wa11_codes"))
+        wo_rounded.append(held([P, N, PACK], BF16, "gates"))
         nc.scalar.copy(
-            wo_rounded[1][:].rearrange("p (c i) t -> p c t i", i=4),
-            wo_raw[1][:].rearrange("p t (c i) -> p c t i", i=4),
+            wo_rounded[1][:].rearrange("p (c i) t -> p c t i", i=LINE),
+            wo_raw[1][:].rearrange("p t (c i) -> p c t i", i=LINE),
         )
 
-        earlier = (batch, steps)
+        second = (batch, steps)
         batch = BATCHES[2]
         steps = guard(batch, *pending, "late_steps")
         quantise_h(0, 4, 4)
         for s in batch:
             scale_steps(batch, steps, s, 0, HALF)
-        for b in range(2):
-            rounded = wo_rounded[b][:].rearrange("p n t -> p (n t)")
-            wo_quantised.append(quantise(rounded, "wo%d" % b, ("rounded01", None)[b]))
-        h_rounded.append(held([P, S, PACK], BF16, "wa11_codes"))
+        wo_quantised = [
+            quantise(wo_rounded[b][:].rearrange("p n t -> p (n t)"), "wo%d" % b, slot)
+            for b, slot in enumerate(("rounded01", None))
+        ]
+        h_rounded.append(held([P, S, PACK], BF16, "gates"))
 
         def project(target, c, b, cols, start, stop):
             codes, plane = wo_quantised[b]
@@ -386,10 +392,10 @@ def tile_list_softplus_step_input_kernel(
 
         late_banks = (4, 5, 3, 2, 7, 6)
         late = {block: inputs_of(1, block, late_banks[block]) for block in (4, 5, 0, 1, 3, 2)}
-        aside = finish_aside(1, 3, late[3], "wb_raw")
+        product_of_block_3 = finish_aside(1, 3, late[3], "wb_raw")
         out_rows = out.rearrange("(c p) s -> p c s", p=P)
 
-        def emit(first, count, numbers, copies, slot, apart=False):
+        def emit(first, count, numbers, copies, slot, stores=1):
             cols = slice(first * BLOCK, (first + count) * BLOCK)
             share = (N // P) // len(numbers)
             result = held([P, N // P, count * BLOCK], F32, slot)
@@ -398,37 +404,35 @@ def tile_list_softplus_step_input_kernel(
                 for n, bank in enumerate(banks):
                     for c in range(share):
                         project(bank[:, c, :], n * share + c, b, cols, (b, c) == (0, 0), (b, c) == (1, share - 1))
+            banks_a_store = len(banks) // stores
             for n, bank in enumerate(banks):
-                rows = slice(n * share, (n + 1) * share)
-                copies[n](result[:, rows, :], bank[:])
-                if apart:
+                copies[n](result[:, n * share : (n + 1) * share, :], bank[:])
+                if (n + 1) % banks_a_store == 0:
+                    rows = slice((n + 1 - banks_a_store) * share, (n + 1) * share)
                     nc.sync.dma_start(out_rows[:, rows, cols], result[:, rows, :])
-            if not apart:
-                nc.sync.dma_start(out_rows[:, :, cols], result[:])
 
-        def scale_four(slices, first, count, place):
-            for s in slices:
-                scale_steps(*(earlier if s in earlier[0] else (batch, steps)), s, first, count, place)
+        def scale_group(block, column):
+            for s in range(PACK, 2 * PACK):
+                scale_steps(*(second if s in second[0] else (batch, steps)), s, block * BLOCK, BLOCK, column)
 
-        on_scalar = (nc.scalar.copy, nc.scalar.copy)
-        aside()
+        scalar_copies = (nc.scalar.copy, nc.scalar.copy)
+        product_of_block_3()
         for block in range(3):
             finish(1, block, late[block])
-        for pair in range(2):
-            scale_four((6 + pair,), HALF, QUARTER, HALF)
+        for pair, numbers in enumerate(((0, 1), (4, 5))):
+            scale_steps(batch, steps, batch[pair], HALF, QUARTER)
             quantise_h(1, 2 * pair, 2)
-            emit(2 * pair, 2, ((0, 1), (4, 5))[pair], on_scalar, "raw0%d" % pair)
-        finish(1, 4, late[4])
-        late[6] = inputs_of(1, 6, late_banks[4])
-        finish(1, 5, late[5])
-        late[7] = inputs_of(1, 7, late_banks[5])
-        scale_four((4, 5, 6, 7), 6 * BLOCK, BLOCK, HALF)
+            emit(2 * pair, 2, numbers, scalar_copies, "raw0%d" % pair)
+        for block in (4, 5):
+            finish(1, block, late[block])
+            late[block + 2] = inputs_of(1, block + 2, late_banks[block])
+        scale_group(6, 4 * BLOCK)
         quantise_h(1, 4, 2)
-        emit(4, 2, (2, 3), on_scalar, "rounded00")
-        finish(1, 6, late[6], HALF)
-        scale_four((4, 5, 6, 7), 7 * BLOCK, BLOCK, HALF + BLOCK)
+        emit(4, 2, (2, 3), scalar_copies, "rounded00")
+        finish(1, 6, late[6], 4 * BLOCK)
+        scale_group(7, 5 * BLOCK)
         quantise_h(1, 6, 1)
-        emit(6, 1, (0,), on_scalar, "factors3")
-        finish(1, 7, late[7], HALF + BLOCK)
+        emit(6, 1, (0,), scalar_copies, "factors3")
+        finish(1, 7, late[7], 5 * BLOCK)
         quantise_h(1, 7, 1)
-        emit(7, 1, (1, 4), (nc.scalar.copy, nc.vector.tensor_copy), "table0", True)
+        emit(7, 1, (1, 4), (nc.scalar.copy, nc.vector.tensor_copy), "table0", 2)

@@ -30,8 +30,6 @@ HALF = 512
 QUARTER = 256
 BLOCK = 128
 FLOOR = 1e-12
-BATCHES = ((0, 1, 2), (3, 4, 5), (6, 7))
-LEAD = 4
 STRIP = 64
 
 
@@ -59,7 +57,7 @@ def tile_list_softplus_step_input_kernel(
         tab_planes = held([P, T], U8, "tab_planes")
         wb_planes = held([P, 2, H], U8, "wb_planes")
         moved_plane = held([P, S], U8, "moved_plane")
-        nc.vector.memset(tab_planes[:].bitcast(I32), 0)
+        nc.gpsimd.memset(tab_planes[:].bitcast(I32), 0)
         nc.vector.memset(wb_planes[:].rearrange("p a c -> p (a c)").bitcast(I32), 0)
         nc.vector.memset(moved_plane[:].bitcast(I32), 0)
 
@@ -74,33 +72,22 @@ def tile_list_softplus_step_input_kernel(
             nc.sync.dma_start(raw[:], rows.rearrange("(p j) c -> p j c", j=PACK))
             return raw
 
-        table = [load_table(0)]
+        g_rows = gT.rearrange("(b m t e) n -> b t m e n", b=2, t=PACK, e=RUN)
+        wo_rows = wo.rearrange("(b m t e) n -> b t m e n", b=2, t=PACK, e=RUN)
+        factors = {}
+
+        def load_factors(s, slot):
+            factors[s] = held([P, T], F32, slot)
+            nc.sync.dma_start(factors[s][:], g_rows[s // PACK, s % PACK])
+
         for q in range(P // QUADRANT):
             nc.sync.dma_start(
                 tab_planes[QUADRANT * q : QUADRANT * q + 2 * ROWS, :].bitcast(I32),
                 tab_scales[:, ROWS * q : ROWS * (q + 1), :].bitcast(I32),
             )
+        table = [load_table(0)]
         wa_raw = {(0, a): load_wa(0, a) for a in range(2)}
         table.append(load_table(1))
-        for a in range(2):
-            wa_raw[1, a] = load_wa(1, a)
-        wb_raw = held([P, 2, H // 2], I32, "wb_raw")
-        nc.sync.dma_start(wb_raw[:], wb_words.rearrange("a p w -> p a w").bitcast(I32))
-        for r in range(ROWS):
-            nc.sync.dma_start(
-                wb_planes[r:P:QUADRANT, :, :].bitcast(I32),
-                wb_scales.rearrange("a (q r) c -> r q a c", r=ROWS)[r].bitcast(I32),
-            )
-        g_rows = gT.rearrange("(b m t e) n -> b t m e n", b=2, t=PACK, e=RUN)
-        wo_rows = wo.rearrange("(b m t e) n -> b t m e n", b=2, t=PACK, e=RUN)
-        factors = []
-
-        def load_factors(s):
-            rows = held([P, T], F32, "factors%d" % s)
-            nc.sync.dma_start(rows[:], g_rows[s // PACK, s % PACK])
-            factors.append(rows)
-
-        load_factors(0)
 
         picked = [held([P, S], U32, "picked%d" % a) for a in range(2)]
         picked_planes = held([P, S], U8, "picked_planes")
@@ -126,8 +113,30 @@ def tile_list_softplus_step_input_kernel(
                 cols = slice(t * P, (t + 1) * P)
                 wa_quantised[PACK * b + first + t, a] = (codes[:, cols], plane[:, cols])
 
-        nc.vector.tensor_copy(picked[0][:], table[0][:].bitcast(U32).indirect(offsets[:]))
         nc.vector.tensor_copy(picked_planes[:], tab_planes[:].indirect(offsets[:]))
+
+        def load_wb_plane(r):
+            nc.sync.dma_start(
+                wb_planes[r:P:QUADRANT, :, :].bitcast(I32),
+                wb_scales.rearrange("a (q r) c -> r q a c", r=ROWS)[r].bitcast(I32),
+            )
+
+        def move_plane(r):
+            nc.sync.dma_start(
+                moved_plane[r:P:QUADRANT, :].bitcast(I32),
+                picked_planes[ROWS + r : P : QUADRANT, :].bitcast(I32),
+            )
+
+        for a in range(2):
+            wa_raw[1, a] = load_wa(1, a)
+        load_factors(0, "factors0")
+        wb_raw = held([P, 2, H // 2], I32, "wb_raw")
+        nc.sync.dma_start(wb_raw[:], wb_words.rearrange("a p w -> p a w").bitcast(I32))
+        for r in range(ROWS):
+            load_wb_plane(r)
+        for r in range(ROWS):
+            move_plane(r)
+        nc.vector.tensor_copy(picked[0][:], table[0][:].bitcast(U32).indirect(offsets[:]))
         quantise_wa(0, 0, 0, round_wa(0, 0, 0, PACK, nc.scalar.copy, "rounded00"))
         scalar_share = round_wa(0, 1, 0, 2, nc.scalar.copy, "rounded01")
         vector_share = round_wa(0, 1, 2, 2, nc.vector.tensor_copy, "rounded00")
@@ -139,44 +148,24 @@ def tile_list_softplus_step_input_kernel(
                 table[1][:].bitcast(U32).indirect(list_part(first, count)),
             )
 
-        for r in range(ROWS):
-            nc.sync.dma_start(
-                moved_plane[r:P:QUADRANT, :].bitcast(I32),
-                picked_planes[ROWS + r : P : QUADRANT, :].bitcast(I32),
-            )
-        for s in BATCHES[0][1:]:
-            load_factors(s)
         wo_raw = []
 
         def load_wo(b):
-            raw = held([P, PACK, N], F32, "raw1%d" % b)
+            raw = held([P, PACK, N], F32, "raw0%d" % b)
             for t in range(PACK):
                 nc.sync.dma_start(raw[:, t, :], wo_rows[b, t])
             wo_raw.append(raw)
 
+        for s in (1, 2, 3):
+            load_factors(s, "factors%d" % s)
         load_wo(0)
-        for s in BATCHES[1]:
-            load_factors(s)
+        for s in (4, 5):
+            load_factors(s, "factors%d" % s)
         load_wo(1)
-        for s in BATCHES[2]:
-            load_factors(s)
+        load_factors(6, "factors6")
 
         work = held([P, 2 * PACK * S], F32, "work")
-
-        def units_of(batch):
-            return [(s, half) for half in range(2) for s in batch]
-
-        def log_parts(span, count):
-            rows = count - 2
-            region = span.rearrange("p (r c) -> p r c", r=rows)
-            strip = HALF // rows
-            places = [region[:, r : r + 1, strip : strip + HALF] for r in range(rows)]
-            places.append(region[:, :, 0:strip])
-            places.append(region[:, :, HALF + strip : HALF + 2 * strip])
-            return region, places
-
-        def shaped(view, place):
-            return view.rearrange("p (r c) -> p r c", r=place.shape[1])
+        scaled = work[:].rearrange("p (s n) -> p s n", n=S)
 
         def multiply(target, s, cols, a, start, stop):
             codes, plane = wa_quantised[s, a]
@@ -190,97 +179,96 @@ def tile_list_softplus_step_input_kernel(
                 stop=stop,
             )
 
-        first_units = (
-            ((1, 2), 0, QUARTER),
-            ((0,), 0, HALF),
-            ((1, 2), QUARTER, QUARTER),
-            ((0,), HALF, HALF),
-            ((1,), HALF, HALF),
-            ((2,), HALF, HALF),
-        )
-        first_rows = (1, 2, 3, 4, 0)
+        def shaped(view, like):
+            return view.rearrange("p (r c) -> p r c", r=like.shape[1])
 
-        def first_logs():
-            banks = [bank_tile(n, [P, len(unit[0]), unit[2]]) for n, unit in enumerate(first_units)]
-            order = [(n, turn) for turn in range(2) for n in range(LEAD)]
-            order += [(n, turn) for n in range(LEAD, len(banks)) for turn in range(2)]
+        def sums_of(units, numbers, lead=0):
+            banks = [bank_tile(n, [P, unit[1], unit[3]]) for n, unit in zip(numbers, units)]
+            order = [(n, turn) for turn in range(2) for n in range(lead)]
+            order += [(n, turn) for n in range(lead, len(units)) for turn in range(2)]
             for n, turn in order:
-                slices, first, count = first_units[n]
-                a = turn if n < LEAD else 1 - turn
-                for k, s in enumerate(slices):
-                    opens, closes = (turn, k) == (0, 0), (turn, k) == (1, len(slices) - 1)
-                    multiply(banks[n][:, k, :], s, slice(first, first + count), a, opens, closes)
-            strips = HALF // STRIP
-            region = work[:, HALF : HALF + strips * (HALF + STRIP)].rearrange("p (r c) -> p r c", r=strips)
-            views = [bank[:] for bank in banks[:-1]] + [banks[-1][:, 0, :].rearrange("p (r c) -> p r c", c=STRIP)]
-            places = [shaped(region[:, row, 0:HALF], view) for row, view in zip(first_rows, views)]
-            places.append(region[:, :, HALF:])
-            for view, place in zip(views, places):
+                s, slices, first, count = units[n]
+                a = turn if n < lead else 1 - turn
+                for k in range(slices):
+                    opens, closes = (turn, k) == (0, 0), (turn, k) == (1, slices - 1)
+                    multiply(banks[n][:, k, :], s + k, slice(first, first + count), a, opens, closes)
+            return banks
+
+        def logs_of(banks, logs, strip, rows, spans, gates=None):
+            pitch = HALF + strip
+            views = [bank[:] for bank in banks[:-1]]
+            views.append(banks[-1][:].rearrange("p s n -> p (s n)").rearrange("p (r c) -> p r c", c=strip))
+
+            def strips_of(area):
+                return area[:, 0 : (HALF // strip) * pitch].rearrange("p (r c) -> p r c", c=pitch)[:, :, 0:strip]
+
+            def places_in(area):
+                places = [shaped(area[:, column : column + HALF], view) for view, column in zip(views, rows)]
+                return places + [strips_of(area)]
+
+            gates = logs if gates is None else gates
+            for view, place in zip(views, places_in(gates)):
                 nc.scalar.activation(place, view, SIGMOID, scale=-1.0)
-            parts = [region[:, row, :] for row in first_rows]
-            parts.insert(len(parts) - 1, region[:, len(first_rows) :, HALF:])
-            for part in parts:
-                nc.scalar.activation(part, part, LN, bias=FLOOR)
-            return views, places
+            for span in spans:
+                if isinstance(span, int):
+                    nc.scalar.activation(strips_of(logs)[:, 0:span], strips_of(gates)[:, 0:span], LN, bias=FLOOR)
+                else:
+                    nc.scalar.activation(logs[:, span[0] : span[1]], gates[:, span[0] : span[1]], LN, bias=FLOOR)
+            return views, places_in(logs)
 
-        def first_guard(views, places):
-            steps = held([P, len(BATCHES[0]), S], F32, "steps")
-            for (slices, first, count), view, place in zip(first_units, views, places):
-                target = steps[:, slices[0] : slices[-1] + 1, first : first + count]
-                if len(slices) == 1:
-                    target = shaped(target[:, 0, :], place)
-                nc.vector.scalar_tensor_tensor(target, place, -1.0, view, MULT, MAX)
-            return steps
+        def guard(targets, views, places, order):
+            for n in order:
+                nc.vector.scalar_tensor_tensor(targets[n], places[n], -1.0, views[n], MULT, MAX)
 
-        def logs_of(batch, numbers, gate_slot=None):
-            units = units_of(batch)
-            banks = [bank_tile(number, [P, HALF]) for number in numbers]
-            for (s, half), bank in zip(units, banks):
-                for a in range(2):
-                    multiply(bank[:], s, slice(half * HALF, (half + 1) * HALF), a, a == 0, a == 1)
-            region, places = log_parts(work[:, batch[0] * S : (batch[-1] + 1) * S], len(units))
-            gate_region, gate_places = region, places
-            if gate_slot:
-                gates = held([P, len(units) * HALF], F32, gate_slot)
-                gate_region, gate_places = log_parts(gates[:], len(units))
-            for bank, place in zip(banks, gate_places):
-                nc.scalar.activation(place, shaped(bank[:], place), SIGMOID, scale=-1.0)
-            for r in range(region.shape[1]):
-                nc.scalar.activation(region[:, r, :], gate_region[:, r, :], LN, bias=FLOOR)
-            return banks, places
-
-        def guard(batch, banks, places, slot):
-            steps = held([P, len(BATCHES[0]), S], F32, slot)
-            for (s, half), bank, place in zip(units_of(batch), banks, places):
-                target = steps[:, s - batch[0], half * HALF : (half + 1) * HALF]
-                nc.vector.scalar_tensor_tensor(
-                    shaped(target, place), place, -1.0, shaped(bank[:], place), MULT, MAX
-                )
-            return steps
-
-        def scale_steps(batch, steps, s, first, count, column=None):
+        def scale_steps(steps, s, first, count, column=None):
             column = first if column is None else column
             nc.vector.tensor_tensor(
-                work[:, s * S + column : s * S + column + count],
-                factors[s][:].indirect(list_part(first, count)),
-                steps[:, s - batch[0], first : first + count],
-                MULT,
+                scaled[:, s, column : column + count], factors[s][:].indirect(list_part(first, count)), steps, MULT
             )
 
-        pending = first_logs()
+        first_units = (
+            (0, 2, 0, QUARTER),
+            (2, 2, 0, QUARTER),
+            (0, 2, QUARTER, QUARTER),
+            (2, 2, QUARTER, QUARTER),
+            (0, 1, HALF, HALF),
+            (1, 1, HALF, HALF),
+            (3, 1, HALF, HALF),
+            (2, 1, HALF, HALF),
+        )
+        row = HALF + STRIP
+        starts = [STRIP + row * k for k in (2, 3, 4, 5, 6, 1, 0)]
+        spans = [(c, c + row) for c in starts[:5]] + [3] + [(c, c + HALF) for c in starts[5:]]
+        pending = logs_of(sums_of(first_units, range(8), 4), work[:, 2 * S :], STRIP, starts, spans)
 
-        quantise_wa(1, 0, 0, round_wa(1, 0, 0, PACK, nc.vector.tensor_copy, "tab_planes"))
-        last_rounded = round_wa(1, 1, 0, PACK, nc.vector.tensor_copy, "table1")
-        wb_codes = held([P, 4, PACK, P // RUN, 2], I32, "wb_codes")
-        nc.vector.tensor_copy(
+        quantise_wa(1, 0, 0, round_wa(1, 0, 0, PACK, nc.vector.tensor_copy, "rounded10"))
+        last_shares = [round_wa(1, 1, first, 2, nc.vector.tensor_copy, "rounded11%d" % first) for first in (0, 2)]
+        for first, share in zip((0, 2), last_shares):
+            quantise_wa(1, 1, first, share)
+
+        first_factors = held([P, S], F32, "first_factors")
+        nc.vector.tensor_copy(first_factors[:], factors[0][:].indirect(offsets[:]))
+        load_factors(7, "factors0")
+
+        h_rounded = [held([P, S, PACK], BF16, "table%d" % b) for b in range(2)]
+        h_quantised = {}
+
+        steps = held([P, PACK, S], F32, "steps")
+        targets = [steps[:, s : s + slices, first : first + count] for s, slices, first, count in first_units]
+        targets[-1] = shaped(targets[-1][:, 0, :], pending[1][-1])
+        guard(targets, *pending, (0, 1, 2, 3, 4, 7, 5, 6))
+        wb_codes = held([P, 4, PACK, P // RUN, 2], I32, "rounded112")
+        nc.gpsimd.tensor_copy(
             wb_codes[:], wb_raw[:].rearrange("p a (b m t w) -> p (a b) t m w", b=2, t=PACK, w=2)
         )
-        quantise_wa(1, 1, 0, last_rounded)
-
-        h_rounded = [held([P, S, PACK], BF16, "table0")]
-        h_codes = [held([P, S], U32, "h_codes%d" % b) for b in range(2)]
-        h_planes = [held([P, S], U8, "h_planes%d" % b) for b in range(2)]
-        scaled = work[:].rearrange("p (s n) -> p s n", n=S)
+        wb_dealt_planes = held([P, 4, PACK, P // RUN], I32, "rounded110")
+        nc.gpsimd.tensor_copy(
+            wb_dealt_planes[:],
+            wb_planes[:].bitcast(I32).rearrange("p a (b m t) -> p (a b) t m", b=2, t=PACK),
+        )
+        for half in range(2):
+            cols = slice(half * HALF, (half + 1) * HALF)
+            nc.gpsimd.tensor_tensor(scaled[:, 0, cols], steps[:, 0, cols], first_factors[:, cols], MULT)
 
         def inputs_of(b, block, number):
             cols = slice(block * BLOCK, (block + 1) * BLOCK)
@@ -320,79 +308,87 @@ def tile_list_softplus_step_input_kernel(
                 MULT,
             )
 
-        def quantise_h(b, first, count):
-            cols = slice(first * BLOCK, (first + count) * BLOCK)
-            nc.vector.quantize_mx(
-                out=h_codes[b][:, cols].bitcast(E4M3),
-                scales=h_planes[b][:, cols],
-                in_=h_rounded[b][:, cols, :].rearrange("p n t -> p (n t)"),
+        def quantise_h(b, first, count, slot=None):
+            rounded = h_rounded[b][:, first * BLOCK : (first + count) * BLOCK, :].rearrange("p n t -> p (n t)")
+            codes, plane = quantise(rounded, "h%d%d" % (b, first), slot)
+            for block in range(first, first + count):
+                h_quantised[b, block] = (codes, plane, (block - first) * BLOCK)
+
+        def half_logs(half, numbers, logs, gates):
+            first = half * HALF
+            units = (
+                (4, 2, first, QUARTER),
+                (6, 2, first, QUARTER),
+                (4, 4, first + QUARTER, BLOCK),
+                (4, 4, first + QUARTER + BLOCK, BLOCK),
             )
+            wide = HALF + BLOCK
+            starts = [BLOCK + wide * k for k in range(3)]
+            spans = [(0, wide), (wide, 2 * wide), (2 * wide, 3 * wide + BLOCK)]
+            return units, logs_of(sums_of(units, numbers), logs, BLOCK, starts, spans, gates)
 
-        batch = BATCHES[0]
-        steps = first_guard(*pending)
-        wb_dealt_planes = held([P, 4, PACK, P // RUN], I32, "table1")
-        nc.gpsimd.tensor_copy(
-            wb_dealt_planes[:],
-            wb_planes[:].bitcast(I32).rearrange("p a (b m t) -> p (a b) t m", b=2, t=PACK),
-        )
-        pending = logs_of(BATCHES[1], range(6))
-        for s in batch:
-            scale_steps(batch, steps, s, 0, S)
+        def half_guard(units, pending, slot):
+            steps = held([P, PACK, HALF], F32, slot)
+            targets = [steps[:, s - PACK : s - PACK + slices, first % HALF : first % HALF + count] for s, slices, first, count in units]
+            guard(targets, *pending, range(4))
+            return steps
 
-        batch = BATCHES[1]
-        wo_rounded = [held([P, N, PACK], BF16, "factors2")]
-        nc.gpsimd.tensor_scalar(wo_rounded[0][:], wo_raw[0][:].rearrange("p t n -> p n t"), 1.0, 0.0, MULT, ADD)
-        steps = guard(batch, *pending, "steps")
-        aside = [
-            finish_aside(0, block, inputs_of(0, block, number), "rounded0%d" % number)
-            for number, block in enumerate((4, 5))
-        ]
-        pending = logs_of(BATCHES[2], (2, 3, 0, 1), "gates")
-        scale_steps(batch, steps, 3, 0, HALF)
-        scale_steps(batch, steps, 4, 0, HALF)
-        scale_steps(batch, steps, 3, HALF, HALF)
+        aside = [finish_aside(0, 4 + n, inputs_of(0, 4 + n, number), "woven%d" % n) for n, number in enumerate((3, 4, 7, 5))]
+        gates = held([P, PACK * (HALF + BLOCK)], F32, "raw11")
+        logs = held([P, PACK * (HALF + BLOCK)], F32, "first_factors")
+        units, pending = half_logs(0, range(4), logs[:], gates[:])
+        own = [inputs_of(0, block, number) for block, number in enumerate((6, 4, 7, 5))]
+        for s in (1, 2, 3):
+            scale_steps(steps[:, s, :], s, 0, S)
         for product in aside:
             product()
-        for block, number in zip((0, 1, 2, 3, 6), (6, 7, 4, 5, 6)):
-            finish(0, block, inputs_of(0, block, number))
+        for block in range(4):
+            finish(0, block, own[block])
+        steps = half_guard(units, pending, "steps")
+
+        def round_wo(b, slot):
+            rounded = held([P, N, PACK], BF16, slot)
+            nc.scalar.copy(
+                rounded[:].rearrange("p (c i) t -> p c t i", i=LINE),
+                wo_raw[b][:].rearrange("p t (c i) -> p c t i", i=LINE),
+            )
+            return rounded
+
+        wo_rounded = [round_wo(0, "raw11")]
+        late = {block: inputs_of(1, block, number) for block, number in ((2, 6), (3, 4))}
+        aside = [finish_aside(1, block, late[block], "woven%d" % (block - 2)) for block in (2, 3)]
+        gates = held([P, PACK * (HALF + BLOCK)], F32, "raw10")
+        units, pending = half_logs(1, (7, 5, 0, 6), work[:], gates[:])
+        wo_rounded.append(round_wo(1, "raw10"))
+        for block, number in zip((0, 1, 4, 5), (1, 4, 2, 3)):
+            late[block] = inputs_of(1, block, number)
+
         quantise_h(0, 0, 4)
-        scale_steps(batch, steps, 5, 0, HALF)
-        for s in (4, 5):
-            scale_steps(batch, steps, s, HALF, QUARTER)
-        finish_aside(0, 7, inputs_of(0, 7, 6), "rounded00")()
-        wo_rounded.append(held([P, N, PACK], BF16, "gates"))
-        nc.scalar.copy(
-            wo_rounded[1][:].rearrange("p (c i) t -> p c t i", i=LINE),
-            wo_raw[1][:].rearrange("p t (c i) -> p c t i", i=LINE),
-        )
+        scale_steps(steps[:, 0, :], 4, 0, HALF)
+        scale_steps(steps[:, 1, :], 5, 0, HALF)
+        quantise_h(0, 4, 4, "first_factors")
+        scale_steps(steps[:, 2, :], 6, 0, HALF)
+        scale_steps(steps[:, 3, :], 7, 0, HALF)
+        for product in aside:
+            product()
+        for block in range(2):
+            finish(1, block, late[block])
+        steps = half_guard(units, pending, "steps")
 
-        second = (batch, steps)
-        batch = BATCHES[2]
-        steps = guard(batch, *pending, "late_steps")
-        quantise_h(0, 4, 4)
-        for s in batch:
-            scale_steps(batch, steps, s, 0, HALF)
-        wo_quantised = [
-            quantise(wo_rounded[b][:].rearrange("p n t -> p (n t)"), "wo%d" % b, slot)
-            for b, slot in enumerate(("rounded01", None))
-        ]
-        h_rounded.append(held([P, S, PACK], BF16, "gates"))
-
-        def project(target, c, b, cols, start, stop):
+        def project(target, c, b, first, count, start, stop):
             codes, plane = wo_quantised[b]
+            h_codes, h_plane, column = h_quantised[b, first]
+            cols = slice(column, column + count * BLOCK)
             nc.tensor.matmul_mx(
                 out=target,
                 lhsT=codes[:, c * P : (c + 1) * P].bitcast(E4M3),
                 lhsT_scale=plane[:, c * P : (c + 1) * P],
-                rhs=h_codes[b][:, cols].bitcast(E4M3),
-                rhs_scale=h_planes[b][:, cols],
+                rhs=h_codes[:, cols].bitcast(E4M3),
+                rhs_scale=h_plane[:, cols],
                 start=start,
                 stop=stop,
             )
 
-        late_banks = (4, 5, 3, 2, 7, 6)
-        late = {block: inputs_of(1, block, late_banks[block]) for block in (4, 5, 0, 1, 3, 2)}
-        product_of_block_3 = finish_aside(1, 3, late[3], "wb_raw")
         out_rows = out.rearrange("(c p) s -> p c s", p=P)
 
         def emit(first, count, numbers, copies, slot, stores=1):
@@ -403,7 +399,7 @@ def tile_list_softplus_step_input_kernel(
             for b in range(2):
                 for n, bank in enumerate(banks):
                     for c in range(share):
-                        project(bank[:, c, :], n * share + c, b, cols, (b, c) == (0, 0), (b, c) == (1, share - 1))
+                        project(bank[:, c, :], n * share + c, b, first, count, (b, c) == (0, 0), (b, c) == (1, share - 1))
             banks_a_store = len(banks) // stores
             for n, bank in enumerate(banks):
                 copies[n](result[:, n * share : (n + 1) * share, :], bank[:])
@@ -411,28 +407,30 @@ def tile_list_softplus_step_input_kernel(
                     rows = slice((n + 1 - banks_a_store) * share, (n + 1) * share)
                     nc.sync.dma_start(out_rows[:, rows, cols], result[:, rows, :])
 
-        def scale_group(block, column):
+        def scale_group(first, count, column):
             for s in range(PACK, 2 * PACK):
-                scale_steps(*(second if s in second[0] else (batch, steps)), s, block * BLOCK, BLOCK, column)
+                scale_steps(steps[:, s - PACK, first - HALF : first - HALF + count], s, first, count, column)
 
         scalar_copies = (nc.scalar.copy, nc.scalar.copy)
-        product_of_block_3()
-        for block in range(3):
-            finish(1, block, late[block])
-        for pair, numbers in enumerate(((0, 1), (4, 5))):
-            scale_steps(batch, steps, batch[pair], HALF, QUARTER)
-            quantise_h(1, 2 * pair, 2)
-            emit(2 * pair, 2, numbers, scalar_copies, "raw0%d" % pair)
+        scale_group(HALF, QUARTER, HALF)
+        wo_quantised = [
+            quantise(wo_rounded[b][:].rearrange("p n t -> p (n t)"), "wo%d" % b, slot)
+            for b, slot in enumerate((None, "woven1"))
+        ]
+        quantise_h(1, 0, 4)
+        emit(0, 2, (1, 4), scalar_copies, "factors1")
+        emit(2, 2, (7, 5), scalar_copies, "factors2")
+        for block, number in ((6, 0), (7, 6)):
+            late[block] = inputs_of(1, block, number)
         for block in (4, 5):
             finish(1, block, late[block])
-            late[block + 2] = inputs_of(1, block + 2, late_banks[block])
-        scale_group(6, 4 * BLOCK)
+        scale_group(6 * BLOCK, BLOCK, 4 * BLOCK)
         quantise_h(1, 4, 2)
-        emit(4, 2, (2, 3), scalar_copies, "rounded00")
+        emit(4, 2, (1, 4), scalar_copies, "factors3")
         finish(1, 6, late[6], 4 * BLOCK)
-        scale_group(7, 5 * BLOCK)
+        scale_group(7 * BLOCK, BLOCK, 5 * BLOCK)
         quantise_h(1, 6, 1)
-        emit(6, 1, (0,), scalar_copies, "factors3")
+        emit(6, 1, (2,), scalar_copies, "raw10")
         finish(1, 7, late[7], 5 * BLOCK)
         quantise_h(1, 7, 1)
-        emit(7, 1, (1, 4), (nc.scalar.copy, nc.vector.tensor_copy), "table0", 2)
+        emit(7, 1, (3, 7), (nc.scalar.copy, nc.vector.tensor_copy), "raw11", 2)

@@ -238,16 +238,19 @@ def tile_list_softplus_step_input_kernel(
         )
         row = HALF + STRIP
         starts = [STRIP + row * k for k in (2, 3, 4, 5, 6, 1, 0)]
-        spans = [(c, c + row) for c in starts[:5]] + [3] + [(c, c + HALF) for c in starts[5:]]
+        spans = [(starts[n], starts[n] + row) for n in (0, 2, 4, 1, 3)] + [3] + [(c, c + HALF) for c in starts[5:]]
         pending = logs_of(sums_of(first_units, range(8), 4), work[:, 2 * S :], STRIP, starts, spans)
 
         quantise_wa(1, 0, 0, round_wa(1, 0, 0, PACK, nc.vector.tensor_copy, "rounded10"))
-        last_shares = [round_wa(1, 1, first, 2, nc.vector.tensor_copy, "rounded11%d" % first) for first in (0, 2)]
-        for first, share in zip((0, 2), last_shares):
-            quantise_wa(1, 1, first, share)
+        quantise_wa(1, 1, 0, round_wa(1, 1, 0, PACK, nc.vector.tensor_copy, "rounded11"))
 
-        first_factors = held([P, S], F32, "first_factors")
-        nc.vector.tensor_copy(first_factors[:], factors[0][:].indirect(offsets[:]))
+        first_factors = [held([P, HALF], F32, "first_factors%d" % half) for half in range(2)]
+        for half in range(2):
+            nc.vector.tensor_copy(first_factors[half][:], factors[0][:].indirect(list_part(half * HALF, HALF)))
+        wb_codes = held([P, 4, PACK, P // RUN, 2], I32, "wb_codes")
+        nc.vector.tensor_copy(
+            wb_codes[:], wb_raw[:].rearrange("p a (b m t w) -> p (a b) t m w", b=2, t=PACK, w=2)
+        )
         load_factors(7, "factors0")
 
         h_rounded = [held([P, S, PACK], BF16, "table%d" % b) for b in range(2)]
@@ -256,19 +259,14 @@ def tile_list_softplus_step_input_kernel(
         steps = held([P, PACK, S], F32, "steps")
         targets = [steps[:, s : s + slices, first : first + count] for s, slices, first, count in first_units]
         targets[-1] = shaped(targets[-1][:, 0, :], pending[1][-1])
-        guard(targets, *pending, (0, 1, 2, 3, 4, 7, 5, 6))
-        wb_codes = held([P, 4, PACK, P // RUN, 2], I32, "rounded112")
-        nc.gpsimd.tensor_copy(
-            wb_codes[:], wb_raw[:].rearrange("p a (b m t w) -> p (a b) t m w", b=2, t=PACK, w=2)
-        )
-        wb_dealt_planes = held([P, 4, PACK, P // RUN], I32, "rounded110")
+        guard(targets, *pending, (0, 2, 4, 1, 3, 7, 5, 6))
+        nc.gpsimd.tensor_tensor(scaled[:, 0, :HALF], steps[:, 0, :HALF], first_factors[0][:], MULT)
+        wb_dealt_planes = held([P, 4, PACK, P // RUN], I32, "first_factors0")
         nc.gpsimd.tensor_copy(
             wb_dealt_planes[:],
             wb_planes[:].bitcast(I32).rearrange("p a (b m t) -> p (a b) t m", b=2, t=PACK),
         )
-        for half in range(2):
-            cols = slice(half * HALF, (half + 1) * HALF)
-            nc.gpsimd.tensor_tensor(scaled[:, 0, cols], steps[:, 0, cols], first_factors[:, cols], MULT)
+        nc.gpsimd.tensor_tensor(scaled[:, 0, HALF:], steps[:, 0, HALF:], first_factors[1][:], MULT)
 
         def inputs_of(b, block, number):
             cols = slice(block * BLOCK, (block + 1) * BLOCK)
@@ -333,16 +331,18 @@ def tile_list_softplus_step_input_kernel(
             guard(targets, *pending, range(4))
             return steps
 
-        aside = [finish_aside(0, 4 + n, inputs_of(0, 4 + n, number), "woven%d" % n) for n, number in enumerate((3, 4, 7, 5))]
+        aside = [finish_aside(0, 5 + n, inputs_of(0, 5 + n, number), "woven%d" % n) for n, number in enumerate((1, 3, 7))]
         gates = held([P, PACK * (HALF + BLOCK)], F32, "raw11")
-        logs = held([P, PACK * (HALF + BLOCK)], F32, "first_factors")
-        units, pending = half_logs(0, range(4), logs[:], gates[:])
-        own = [inputs_of(0, block, number) for block, number in enumerate((6, 4, 7, 5))]
+        logs = held([P, PACK * (HALF + BLOCK)], F32, "first_factors1")
+        units, pending = half_logs(0, (0, 2, 4, 1), logs[:], gates[:])
+        own = [inputs_of(0, block, number) for block, number in enumerate((5, 6, 3, 7))]
         for s in (1, 2, 3):
             scale_steps(steps[:, s, :], s, 0, S)
         for product in aside:
             product()
-        for block in range(4):
+        finish(0, 0, own[0])
+        own.append(inputs_of(0, 4, 5))
+        for block in range(1, 5):
             finish(0, block, own[block])
         steps = half_guard(units, pending, "steps")
 
@@ -355,18 +355,17 @@ def tile_list_softplus_step_input_kernel(
             return rounded
 
         wo_rounded = [round_wo(0, "raw11")]
-        late = {block: inputs_of(1, block, number) for block, number in ((2, 6), (3, 4))}
+        late = {block: inputs_of(1, block, number) for block, number in ((2, 6), (3, 3))}
         aside = [finish_aside(1, block, late[block], "woven%d" % (block - 2)) for block in (2, 3)]
         gates = held([P, PACK * (HALF + BLOCK)], F32, "raw10")
         units, pending = half_logs(1, (7, 5, 0, 6), work[:], gates[:])
         wo_rounded.append(round_wo(1, "raw10"))
-        for block, number in zip((0, 1, 4, 5), (1, 4, 2, 3)):
+        for block, number in zip((0, 1, 4, 5), (2, 3, 4, 1)):
             late[block] = inputs_of(1, block, number)
 
-        quantise_h(0, 0, 4)
         scale_steps(steps[:, 0, :], 4, 0, HALF)
+        quantise_h(0, 0, 8, "first_factors1")
         scale_steps(steps[:, 1, :], 5, 0, HALF)
-        quantise_h(0, 4, 4, "first_factors")
         scale_steps(steps[:, 2, :], 6, 0, HALF)
         scale_steps(steps[:, 3, :], 7, 0, HALF)
         for product in aside:
@@ -415,10 +414,10 @@ def tile_list_softplus_step_input_kernel(
         scale_group(HALF, QUARTER, HALF)
         wo_quantised = [
             quantise(wo_rounded[b][:].rearrange("p n t -> p (n t)"), "wo%d" % b, slot)
-            for b, slot in enumerate((None, "woven1"))
+            for b, slot in enumerate(("woven1", "woven0"))
         ]
         quantise_h(1, 0, 4)
-        emit(0, 2, (1, 4), scalar_copies, "factors1")
+        emit(0, 2, (2, 3), scalar_copies, "factors1")
         emit(2, 2, (7, 5), scalar_copies, "factors2")
         for block, number in ((6, 0), (7, 6)):
             late[block] = inputs_of(1, block, number)
@@ -426,11 +425,11 @@ def tile_list_softplus_step_input_kernel(
             finish(1, block, late[block])
         scale_group(6 * BLOCK, BLOCK, 4 * BLOCK)
         quantise_h(1, 4, 2)
-        emit(4, 2, (1, 4), scalar_copies, "factors3")
+        emit(4, 2, (2, 3), scalar_copies, "factors3")
         finish(1, 6, late[6], 4 * BLOCK)
         scale_group(7 * BLOCK, BLOCK, 5 * BLOCK)
         quantise_h(1, 6, 1)
-        emit(6, 1, (2,), scalar_copies, "raw10")
+        emit(6, 1, (4,), scalar_copies, "raw10")
         finish(1, 7, late[7], 5 * BLOCK)
         quantise_h(1, 7, 1)
-        emit(7, 1, (3, 7), (nc.scalar.copy, nc.vector.tensor_copy), "raw11", 2)
+        emit(7, 1, (1, 7), (nc.scalar.copy, nc.vector.tensor_copy), "raw11", 2)

@@ -251,21 +251,21 @@ def tile_list_softplus_step_input_kernel(
         nc.vector.tensor_copy(
             wb_codes[:], wb_raw[:].rearrange("p a (b m t w) -> p (a b) t m w", b=2, t=PACK, w=2)
         )
+        wb_dealt_planes = held([P, 4, PACK, P // RUN], I32, "wb_dealt_planes")
+        nc.vector.tensor_copy(
+            wb_dealt_planes[:].rearrange("p g t (q i) -> p g q t i", i=LINE),
+            wb_planes[:].bitcast(I32).rearrange("p a (b q i t) -> p (a b) q t i", b=2, i=LINE, t=PACK),
+        )
         load_factors(7, "factors0")
 
         h_rounded = [held([P, S, PACK], BF16, "table%d" % b) for b in range(2)]
         h_quantised = {}
 
-        steps = held([P, PACK, S], F32, "steps")
+        steps = held([P, PACK, S], F32, "wb_planes")
         targets = [steps[:, s : s + slices, first : first + count] for s, slices, first, count in first_units]
         targets[-1] = shaped(targets[-1][:, 0, :], pending[1][-1])
         guard(targets, *pending, (0, 2, 4, 1, 3, 7, 5, 6))
         nc.gpsimd.tensor_tensor(scaled[:, 0, :HALF], steps[:, 0, :HALF], first_factors[0][:], MULT)
-        wb_dealt_planes = held([P, 4, PACK, P // RUN], I32, "first_factors0")
-        nc.gpsimd.tensor_copy(
-            wb_dealt_planes[:],
-            wb_planes[:].bitcast(I32).rearrange("p a (b m t) -> p (a b) t m", b=2, t=PACK),
-        )
         nc.gpsimd.tensor_tensor(scaled[:, 0, HALF:], steps[:, 0, HALF:], first_factors[1][:], MULT)
 
         def inputs_of(b, block, number):
@@ -344,7 +344,7 @@ def tile_list_softplus_step_input_kernel(
         own.append(inputs_of(0, 4, 5))
         for block in range(1, 5):
             finish(0, block, own[block])
-        steps = half_guard(units, pending, "steps")
+        steps = half_guard(units, pending, "wb_planes")
 
         def round_wo(b, slot):
             rounded = held([P, N, PACK], BF16, slot)
@@ -372,7 +372,7 @@ def tile_list_softplus_step_input_kernel(
             product()
         for block in range(2):
             finish(1, block, late[block])
-        steps = half_guard(units, pending, "steps")
+        steps = half_guard(units, pending, "wb_planes")
 
         def project(target, c, b, first, count, start, stop):
             codes, plane = wo_quantised[b]

@@ -80,11 +80,17 @@ def tile_list_softplus_step_input_kernel(
             factors[s] = held([P, T], F32, slot)
             nc.sync.dma_start(factors[s][:], g_rows[s // PACK, s % PACK])
 
-        for q in range(P // QUADRANT):
+        for q in range(2):
             nc.sync.dma_start(
                 tab_planes[QUADRANT * q : QUADRANT * q + 2 * ROWS, :].bitcast(I32),
                 tab_scales[:, ROWS * q : ROWS * (q + 1), :].bitcast(I32),
             )
+        for q in range(2, P // QUADRANT):
+            for a in range(2):
+                nc.sync.dma_start(
+                    tab_planes[QUADRANT * q + ROWS * a : QUADRANT * q + ROWS * (a + 1), :].bitcast(I32),
+                    tab_scales[a, ROWS * q : ROWS * (q + 1), :].bitcast(I32),
+                )
         table = [load_table(0)]
         wa_raw = {(0, a): load_wa(0, a) for a in range(2)}
         table.append(load_table(1))
@@ -244,9 +250,8 @@ def tile_list_softplus_step_input_kernel(
         quantise_wa(1, 0, 0, round_wa(1, 0, 0, PACK, nc.vector.tensor_copy, "rounded10"))
         quantise_wa(1, 1, 0, round_wa(1, 1, 0, PACK, nc.vector.tensor_copy, "rounded11"))
 
-        first_factors = [held([P, HALF], F32, "first_factors%d" % half) for half in range(2)]
-        for half in range(2):
-            nc.vector.tensor_copy(first_factors[half][:], factors[0][:].indirect(list_part(half * HALF, HALF)))
+        first_factors = held([P, S], F32, "first_factors")
+        nc.vector.tensor_copy(first_factors[:], factors[0][:].indirect(offsets[:]))
         wb_codes = held([P, 4, PACK, P // RUN, 2], I32, "wb_codes")
         nc.vector.tensor_copy(
             wb_codes[:], wb_raw[:].rearrange("p a (b m t w) -> p (a b) t m w", b=2, t=PACK, w=2)
@@ -265,8 +270,8 @@ def tile_list_softplus_step_input_kernel(
         targets = [steps[:, s : s + slices, first : first + count] for s, slices, first, count in first_units]
         targets[-1] = shaped(targets[-1][:, 0, :], pending[1][-1])
         guard(targets, *pending, (0, 2, 4, 1, 3, 7, 5, 6))
-        nc.gpsimd.tensor_tensor(scaled[:, 0, :HALF], steps[:, 0, :HALF], first_factors[0][:], MULT)
-        nc.gpsimd.tensor_tensor(scaled[:, 0, HALF:], steps[:, 0, HALF:], first_factors[1][:], MULT)
+        nc.gpsimd.tensor_tensor(scaled[:, 0, :HALF], steps[:, 0, :HALF], first_factors[:, :HALF], MULT)
+        nc.gpsimd.tensor_tensor(scaled[:, 0, HALF:], steps[:, 0, HALF:], first_factors[:, HALF:], MULT)
 
         def inputs_of(b, block, number):
             cols = slice(block * BLOCK, (block + 1) * BLOCK)
@@ -333,7 +338,7 @@ def tile_list_softplus_step_input_kernel(
 
         aside = [finish_aside(0, 5 + n, inputs_of(0, 5 + n, number), "woven%d" % n) for n, number in enumerate((1, 3, 7))]
         gates = held([P, PACK * (HALF + BLOCK)], F32, "raw11")
-        logs = held([P, PACK * (HALF + BLOCK)], F32, "first_factors1")
+        logs = held([P, PACK * (HALF + BLOCK)], F32, "first_factors")
         units, pending = half_logs(0, (0, 2, 4, 1), logs[:], gates[:])
         own = [inputs_of(0, block, number) for block, number in enumerate((5, 6, 3, 7))]
         for s in (1, 2, 3):
@@ -364,7 +369,7 @@ def tile_list_softplus_step_input_kernel(
             late[block] = inputs_of(1, block, number)
 
         scale_steps(steps[:, 0, :], 4, 0, HALF)
-        quantise_h(0, 0, 8, "first_factors1")
+        quantise_h(0, 0, 8, "first_factors")
         scale_steps(steps[:, 1, :], 5, 0, HALF)
         scale_steps(steps[:, 2, :], 6, 0, HALF)
         scale_steps(steps[:, 3, :], 7, 0, HALF)

@@ -107,14 +107,14 @@ def tile_list_softplus_step_input_kernel(
             return codes, plane
 
         def round_wa(b, a, first, count, copy, slot):
-            rounded = held([P, count * PASS], BF16, slot)
-            dealt = rounded[:].rearrange("p (t m e j) -> p m t j e", t=count, e=RUN, j=PACK)
+            rounded = held([P, count * PASS], BF16, slot)[:] if isinstance(slot, str) else slot
+            dealt = rounded.rearrange("p (t m e j) -> p m t j e", t=count, e=RUN, j=PACK)
             source = wa_raw[b, a][:].rearrange("p j (m t e) -> p m t j e", t=PACK, e=RUN)
             copy(dealt, source[:, :, first : first + count])
             return rounded
 
         def quantise_wa(b, a, first, rounded):
-            codes, plane = quantise(rounded[:], "wa%d%d%d" % (b, a, first))
+            codes, plane = quantise(rounded, "wa%d%d%d" % (b, a, first))
             for t in range(rounded.shape[1] // PASS):
                 cols = slice(t * P, (t + 1) * P)
                 wa_quantised[PACK * b + first + t, a] = (codes[:, cols], plane[:, cols])
@@ -133,13 +133,14 @@ def tile_list_softplus_step_input_kernel(
                 picked_planes[ROWS + r : P : QUADRANT, :].bitcast(I32),
             )
 
-        for a in range(2):
-            wa_raw[1, a] = load_wa(1, a)
+        wa_raw[1, 0] = load_wa(1, 0)
         load_factors(0, "factors0")
+        wa_raw[1, 1] = load_wa(1, 1)
         wb_raw = held([P, 2, H // 2], I32, "wb_raw")
         nc.sync.dma_start(wb_raw[:], wb_words.rearrange("a p w -> p a w").bitcast(I32))
         for r in range(ROWS):
             load_wb_plane(r)
+        load_factors(1, "factors1")
         for r in range(ROWS):
             move_plane(r)
         nc.vector.tensor_copy(picked[0][:], table[0][:].bitcast(U32).indirect(offsets[:]))
@@ -162,7 +163,7 @@ def tile_list_softplus_step_input_kernel(
                 nc.sync.dma_start(raw[:, t, :], wo_rows[b, t])
             wo_raw.append(raw)
 
-        for s in (1, 2, 3):
+        for s in (2, 3):
             load_factors(s, "factors%d" % s)
         load_wo(0)
         for s in (4, 5):
@@ -242,16 +243,19 @@ def tile_list_softplus_step_input_kernel(
             (3, 1, HALF, HALF),
             (2, 1, HALF, HALF),
         )
+        third_rounded = held([P, PACK * PASS], BF16, "rounded10")
+        round_wa(1, 0, 3, 1, nc.scalar.copy, third_rounded[:, 3 * PASS :])
         row = HALF + STRIP
         starts = [STRIP + row * k for k in (2, 3, 4, 5, 6, 1, 0)]
         spans = [(starts[n], starts[n] + row) for n in (0, 2, 4, 1, 3)] + [3] + [(c, c + HALF) for c in starts[5:]]
         pending = logs_of(sums_of(first_units, range(8), 4), work[:, 2 * S :], STRIP, starts, spans)
 
-        quantise_wa(1, 0, 0, round_wa(1, 0, 0, PACK, nc.vector.tensor_copy, "rounded10"))
-        quantise_wa(1, 1, 0, round_wa(1, 1, 0, PACK, nc.vector.tensor_copy, "rounded11"))
-
+        round_wa(1, 0, 0, 3, nc.vector.tensor_copy, third_rounded[:, : 3 * PASS])
+        quantise_wa(1, 0, 0, third_rounded[:])
         first_factors = held([P, S], F32, "first_factors")
         nc.vector.tensor_copy(first_factors[:], factors[0][:].indirect(offsets[:]))
+        quantise_wa(1, 1, 0, round_wa(1, 1, 0, PACK, nc.vector.tensor_copy, "rounded11"))
+
         wb_codes = held([P, 4, PACK, P // RUN, 2], I32, "wb_codes")
         nc.vector.tensor_copy(
             wb_codes[:], wb_raw[:].rearrange("p a (b m t w) -> p (a b) t m w", b=2, t=PACK, w=2)
@@ -289,21 +293,21 @@ def tile_list_softplus_step_input_kernel(
                     )
             return bank
 
-        def finish(b, block, bank, column=None):
-            cols = slice(block * BLOCK, (block + 1) * BLOCK)
+        def finish(b, block, bank, column=None, count=BLOCK):
+            cols = slice(block * BLOCK, block * BLOCK + count)
             column = block * BLOCK if column is None else column
-            sources = scaled[:, b * PACK : (b + 1) * PACK, column : column + BLOCK]
+            sources = scaled[:, b * PACK : (b + 1) * PACK, column : column + count]
             nc.vector.tensor_tensor(
                 h_rounded[b][:, cols, :].rearrange("p (c i) t -> p c t i", i=LINE),
-                bank[:].rearrange("p t (c i) -> p c t i", i=LINE),
+                bank[:, :, :count].rearrange("p t (c i) -> p c t i", i=LINE),
                 sources.rearrange("p t (c i) -> p c t i", i=LINE),
                 MULT,
             )
 
-        def finish_aside(b, block, bank, slot):
-            cols = slice(block * BLOCK, (block + 1) * BLOCK)
-            woven = held([P, BLOCK, PACK], F32, slot)
-            nc.scalar.copy(woven[:], bank[:].rearrange("p t n -> p n t"))
+        def finish_aside(b, block, bank, slot, first=0):
+            cols = slice(block * BLOCK + first, (block + 1) * BLOCK)
+            woven = held([P, BLOCK - first, PACK], F32, slot)
+            nc.scalar.copy(woven[:], bank[:, :, first:].rearrange("p t n -> p n t"))
             return lambda: nc.gpsimd.tensor_tensor(
                 h_rounded[b][:, cols, :],
                 woven[:],
@@ -346,9 +350,11 @@ def tile_list_softplus_step_input_kernel(
         for product in aside:
             product()
         finish(0, 0, own[0])
-        own.append(inputs_of(0, 4, 5))
-        for block in range(1, 5):
+        shared = inputs_of(0, 4, 5)
+        finish_aside(0, 4, shared, "woven3", BLOCK // 2)()
+        for block in range(1, 4):
             finish(0, block, own[block])
+        finish(0, 4, shared, None, BLOCK // 2)
         steps = half_guard(units, pending, "wb_planes")
 
         def round_wo(b, slot):
@@ -437,4 +443,4 @@ def tile_list_softplus_step_input_kernel(
         emit(6, 1, (4,), scalar_copies, "raw10")
         finish(1, 7, late[7], 5 * BLOCK)
         quantise_h(1, 7, 1)
-        emit(7, 1, (1, 7), (nc.scalar.copy, nc.vector.tensor_copy), "raw11", 2)
+        emit(7, 1, (1, 7, 5, 0), (nc.scalar.copy, nc.vector.tensor_copy) * 2, "raw11", 2)

@@ -351,11 +351,10 @@ def tile_list_softplus_step_input_kernel(
             product()
         finish(0, 0, own[0])
         shared = inputs_of(0, 4, 5)
-        finish_aside(0, 4, shared, "woven3", BLOCK // 2)()
         for block in range(1, 4):
             finish(0, block, own[block])
-        finish(0, 4, shared, None, BLOCK // 2)
         steps = half_guard(units, pending, "wb_planes")
+        finish(0, 4, shared)
 
         def round_wo(b, slot):
             rounded = held([P, N, PACK], BF16, slot)
@@ -369,7 +368,7 @@ def tile_list_softplus_step_input_kernel(
         late = {block: inputs_of(1, block, number) for block, number in ((2, 6), (3, 3))}
         aside = [finish_aside(1, block, late[block], "woven%d" % (block - 2)) for block in (2, 3)]
         gates = held([P, PACK * (HALF + BLOCK)], F32, "raw10")
-        units, pending = half_logs(1, (7, 5, 0, 6), work[:], gates[:])
+        units, pending = half_logs(1, (7, 0, 5, 6), work[:], gates[:])
         wo_rounded.append(round_wo(1, "raw10"))
         for block, number in zip((0, 1, 4, 5), (2, 3, 4, 1)):
             late[block] = inputs_of(1, block, number)

@@ -1,6 +1,7 @@
 from contextlib import ExitStack
 
 import concourse.mybir as mybir
+from concourse.masks import make_identity
 
 K, T, S, H, N = 1024, 2048, 1024, 1024, 512
 FLOPS = 2 * (2 * K * H * S + H * N * S)
@@ -18,6 +19,8 @@ ADD = mybir.AluOpType.add
 MAX = mybir.AluOpType.max
 SIGMOID = mybir.ActivationFunctionType.Sigmoid
 LN = mybir.ActivationFunctionType.Ln
+COPY = mybir.ActivationFunctionType.Copy
+RELU = mybir.ActivationFunctionType.Relu
 
 P = 128
 PACK = 4
@@ -31,6 +34,8 @@ QUARTER = 256
 BLOCK = 128
 FLOOR = 1e-12
 STRIP = 64
+LEAD = 2
+SHIFT = 3
 
 
 def tile_list_softplus_step_input_kernel(
@@ -61,16 +66,20 @@ def tile_list_softplus_step_input_kernel(
         nc.vector.memset(wb_planes[:].rearrange("p a c -> p (a c)").bitcast(I32), 0)
         nc.vector.memset(moved_plane[:].bitcast(I32), 0)
 
+        identity = held([P, P], F32, "identity")
+        make_identity(nc, identity[:])
+
         def load_table(a):
             words = held([P, T], I32, "table%d" % a)
             nc.sync.dma_start(words[:], tab_words[a].rearrange("p t i -> p (t i)").bitcast(I32))
             return words
 
+        wa_raw = {}
+
         def load_wa(b, a):
-            raw = held([P, PACK, PASS], F32, "raw%d%d" % (b, a))
+            wa_raw[b, a] = held([P, PACK, PASS], F32, "raw%d%d" % (b, a))
             rows = wa[a * PASS : (a + 1) * PASS, b * PASS : (b + 1) * PASS]
-            nc.sync.dma_start(raw[:], rows.rearrange("(p j) c -> p j c", j=PACK))
-            return raw
+            nc.sync.dma_start(wa_raw[b, a][:], rows.rearrange("(p j) c -> p j c", j=PACK))
 
         g_rows = gT.rearrange("(b m t e) n -> b t m e n", b=2, t=PACK, e=RUN)
         wo_rows = wo.rearrange("(b m t e) n -> b t m e n", b=2, t=PACK, e=RUN)
@@ -92,12 +101,33 @@ def tile_list_softplus_step_input_kernel(
                     tab_scales[a, ROWS * q : ROWS * (q + 1), :].bitcast(I32),
                 )
         table = [load_table(0)]
-        wa_raw = {(0, a): load_wa(0, a) for a in range(2)}
+        for a in range(2):
+            load_wa(0, a)
         table.append(load_table(1))
 
         picked = [held([P, S], U32, "picked%d" % a) for a in range(2)]
         picked_planes = held([P, S], U8, "picked_planes")
+        nc.vector.tensor_copy(picked_planes[:], tab_planes[:].indirect(offsets[:]))
+
+        load_wa(1, 0)
+        load_factors(0, "factors0")
+        load_wa(1, 1)
+        wb_raw = held([P, 2, H // 2], I32, "wb_raw")
+        nc.sync.dma_start(wb_raw[:], wb_words.rearrange("a p w -> p a w").bitcast(I32))
+        for r in range(ROWS):
+            nc.sync.dma_start(
+                wb_planes[r:P:QUADRANT, :, :].bitcast(I32),
+                wb_scales.rearrange("a (q r) c -> r q a c", r=ROWS)[r].bitcast(I32),
+            )
+        load_factors(1, "factors1")
+        for r in range(ROWS):
+            nc.sync.dma_start(
+                moved_plane[r:P:QUADRANT, :].bitcast(I32),
+                picked_planes[ROWS + r : P : QUADRANT, :].bitcast(I32),
+            )
+
         wa_quantised = {}
+        wa_moving = {}
 
         def quantise(rounded, name, slot=None):
             width = rounded.shape[1] // PACK
@@ -107,46 +137,23 @@ def tile_list_softplus_step_input_kernel(
             return codes, plane
 
         def round_wa(b, a, first, count, copy, slot):
-            rounded = held([P, count * PASS], BF16, slot)[:] if isinstance(slot, str) else slot
-            dealt = rounded.rearrange("p (t m e j) -> p m t j e", t=count, e=RUN, j=PACK)
+            rounded = held([P, count * PASS], BF16, slot)
+            dealt = rounded[:].rearrange("p (t m e j) -> p m t j e", t=count, e=RUN, j=PACK)
             source = wa_raw[b, a][:].rearrange("p j (m t e) -> p m t j e", t=PACK, e=RUN)
             copy(dealt, source[:, :, first : first + count])
-            return rounded
+            return rounded[:]
 
-        def quantise_wa(b, a, first, rounded):
-            codes, plane = quantise(rounded, "wa%d%d%d" % (b, a, first))
+        def quantise_wa(b, a, first, rounded, slot=None):
+            codes, plane = quantise(rounded, "wa%d%d%d" % (b, a, first), slot)
+            wa_moving[b, a] = (codes, plane)
             for t in range(rounded.shape[1] // PASS):
                 cols = slice(t * P, (t + 1) * P)
                 wa_quantised[PACK * b + first + t, a] = (codes[:, cols], plane[:, cols])
 
-        nc.vector.tensor_copy(picked_planes[:], tab_planes[:].indirect(offsets[:]))
-
-        def load_wb_plane(r):
-            nc.sync.dma_start(
-                wb_planes[r:P:QUADRANT, :, :].bitcast(I32),
-                wb_scales.rearrange("a (q r) c -> r q a c", r=ROWS)[r].bitcast(I32),
-            )
-
-        def move_plane(r):
-            nc.sync.dma_start(
-                moved_plane[r:P:QUADRANT, :].bitcast(I32),
-                picked_planes[ROWS + r : P : QUADRANT, :].bitcast(I32),
-            )
-
-        wa_raw[1, 0] = load_wa(1, 0)
-        load_factors(0, "factors0")
-        wa_raw[1, 1] = load_wa(1, 1)
-        wb_raw = held([P, 2, H // 2], I32, "wb_raw")
-        nc.sync.dma_start(wb_raw[:], wb_words.rearrange("a p w -> p a w").bitcast(I32))
-        for r in range(ROWS):
-            load_wb_plane(r)
-        load_factors(1, "factors1")
-        for r in range(ROWS):
-            move_plane(r)
         nc.vector.tensor_copy(picked[0][:], table[0][:].bitcast(U32).indirect(offsets[:]))
-        quantise_wa(0, 0, 0, round_wa(0, 0, 0, PACK, nc.scalar.copy, "rounded00"))
-        scalar_share = round_wa(0, 1, 0, 2, nc.scalar.copy, "rounded01")
-        vector_share = round_wa(0, 1, 2, 2, nc.vector.tensor_copy, "rounded00")
+        quantise_wa(0, 0, 0, round_wa(0, 0, 0, PACK, nc.scalar.copy, "rounded_wide"))
+        scalar_share = round_wa(0, 1, 0, 2, nc.scalar.copy, "rounded_narrow")
+        vector_share = round_wa(0, 1, 2, 2, nc.vector.tensor_copy, "rounded_wide")
         quantise_wa(0, 1, 0, scalar_share)
         quantise_wa(0, 1, 2, vector_share)
         for first, count in ((0, QUARTER), (QUARTER, QUARTER), (HALF, HALF)):
@@ -155,106 +162,24 @@ def tile_list_softplus_step_input_kernel(
                 table[1][:].bitcast(U32).indirect(list_part(first, count)),
             )
 
+        quantise_wa(1, 0, 0, round_wa(1, 0, 0, PACK, nc.vector.tensor_copy, "rounded_wide"))
+        early_factors = held([P, S], F32, "early_factors")
+        nc.vector.tensor_copy(early_factors[:], factors[0][:].indirect(offsets[:]))
+        quantise_wa(1, 1, 0, round_wa(1, 1, 0, PACK, nc.vector.tensor_copy, "rounded_wide"))
+
         wo_raw = []
 
-        def load_wo(b):
-            raw = held([P, PACK, N], F32, "raw0%d" % b)
+        def load_wo(b, slot):
+            wo_raw.append(held([P, PACK, N], F32, slot))
             for t in range(PACK):
-                nc.sync.dma_start(raw[:, t, :], wo_rows[b, t])
-            wo_raw.append(raw)
+                nc.sync.dma_start(wo_raw[b][:, t, :], wo_rows[b, t])
 
         for s in (2, 3):
             load_factors(s, "factors%d" % s)
-        load_wo(0)
-        for s in (4, 5):
-            load_factors(s, "factors%d" % s)
-        load_wo(1)
-        load_factors(6, "factors6")
-
-        work = held([P, 2 * PACK * S], F32, "work")
-        scaled = work[:].rearrange("p (s n) -> p s n", n=S)
-
-        def multiply(target, s, cols, a, start, stop):
-            codes, plane = wa_quantised[s, a]
-            nc.tensor.matmul_mx(
-                out=target,
-                lhsT=codes.bitcast(E4M3),
-                lhsT_scale=plane,
-                rhs=picked[a][:, cols].bitcast(E4M3),
-                rhs_scale=picked_planes[ROWS * a : P, cols],
-                start=start,
-                stop=stop,
-            )
-
-        def shaped(view, like):
-            return view.rearrange("p (r c) -> p r c", r=like.shape[1])
-
-        def sums_of(units, numbers, lead=0):
-            banks = [bank_tile(n, [P, unit[1], unit[3]]) for n, unit in zip(numbers, units)]
-            order = [(n, turn) for turn in range(2) for n in range(lead)]
-            order += [(n, turn) for n in range(lead, len(units)) for turn in range(2)]
-            for n, turn in order:
-                s, slices, first, count = units[n]
-                a = turn if n < lead else 1 - turn
-                for k in range(slices):
-                    opens, closes = (turn, k) == (0, 0), (turn, k) == (1, slices - 1)
-                    multiply(banks[n][:, k, :], s + k, slice(first, first + count), a, opens, closes)
-            return banks
-
-        def logs_of(banks, logs, strip, rows, spans, gates=None):
-            pitch = HALF + strip
-            views = [bank[:] for bank in banks[:-1]]
-            views.append(banks[-1][:].rearrange("p s n -> p (s n)").rearrange("p (r c) -> p r c", c=strip))
-
-            def strips_of(area):
-                return area[:, 0 : (HALF // strip) * pitch].rearrange("p (r c) -> p r c", c=pitch)[:, :, 0:strip]
-
-            def places_in(area):
-                places = [shaped(area[:, column : column + HALF], view) for view, column in zip(views, rows)]
-                return places + [strips_of(area)]
-
-            gates = logs if gates is None else gates
-            for view, place in zip(views, places_in(gates)):
-                nc.scalar.activation(place, view, SIGMOID, scale=-1.0)
-            for span in spans:
-                if isinstance(span, int):
-                    nc.scalar.activation(strips_of(logs)[:, 0:span], strips_of(gates)[:, 0:span], LN, bias=FLOOR)
-                else:
-                    nc.scalar.activation(logs[:, span[0] : span[1]], gates[:, span[0] : span[1]], LN, bias=FLOOR)
-            return views, places_in(logs)
-
-        def guard(targets, views, places, order):
-            for n in order:
-                nc.vector.scalar_tensor_tensor(targets[n], places[n], -1.0, views[n], MULT, MAX)
-
-        def scale_steps(steps, s, first, count, column=None):
-            column = first if column is None else column
-            nc.vector.tensor_tensor(
-                scaled[:, s, column : column + count], factors[s][:].indirect(list_part(first, count)), steps, MULT
-            )
-
-        first_units = (
-            (0, 2, 0, QUARTER),
-            (2, 2, 0, QUARTER),
-            (0, 2, QUARTER, QUARTER),
-            (2, 2, QUARTER, QUARTER),
-            (0, 1, HALF, HALF),
-            (1, 1, HALF, HALF),
-            (3, 1, HALF, HALF),
-            (2, 1, HALF, HALF),
-        )
-        third_rounded = held([P, PACK * PASS], BF16, "rounded10")
-        round_wa(1, 0, 3, 1, nc.scalar.copy, third_rounded[:, 3 * PASS :])
-        row = HALF + STRIP
-        starts = [STRIP + row * k for k in (2, 3, 4, 5, 6, 1, 0)]
-        spans = [(starts[n], starts[n] + row) for n in (0, 2, 4, 1, 3)] + [3] + [(c, c + HALF) for c in starts[5:]]
-        pending = logs_of(sums_of(first_units, range(8), 4), work[:, 2 * S :], STRIP, starts, spans)
-
-        round_wa(1, 0, 0, 3, nc.vector.tensor_copy, third_rounded[:, : 3 * PASS])
-        quantise_wa(1, 0, 0, third_rounded[:])
-        first_factors = held([P, S], F32, "first_factors")
-        nc.vector.tensor_copy(first_factors[:], factors[0][:].indirect(offsets[:]))
-        quantise_wa(1, 1, 0, round_wa(1, 1, 0, PACK, nc.vector.tensor_copy, "rounded11"))
+        load_wo(0, "raw00")
+        for s, slot in zip(range(4, 8), ("factors0", "raw01", "raw10", "raw11")):
+            load_factors(s, slot)
+        load_wo(1, "wo_raw")
 
         wb_codes = held([P, 4, PACK, P // RUN, 2], I32, "wb_codes")
         nc.vector.tensor_copy(
@@ -265,17 +190,58 @@ def tile_list_softplus_step_input_kernel(
             wb_dealt_planes[:].rearrange("p g t (q i) -> p g q t i", i=LINE),
             wb_planes[:].bitcast(I32).rearrange("p a (b q i t) -> p (a b) q t i", b=2, i=LINE, t=PACK),
         )
-        load_factors(7, "factors0")
 
-        h_rounded = [held([P, S, PACK], BF16, "table%d" % b) for b in range(2)]
-        h_quantised = {}
+        def sums(unit, number, passes=(0, 1), bank=None):
+            s, slices, first, count = unit
+            bank = bank_tile(number, [P, slices, count]) if bank is None else bank
+            cols = slice(first, first + count)
+            for a, turn in passes if isinstance(passes[0], tuple) else zip(passes, range(2)):
+                for k in range(slices):
+                    codes, plane = wa_quantised[s + k, a]
+                    nc.tensor.matmul_mx(
+                        out=bank[:, k, :],
+                        lhsT=codes.bitcast(E4M3),
+                        lhsT_scale=plane,
+                        rhs=picked[a][:, cols].bitcast(E4M3),
+                        rhs_scale=picked_planes[ROWS * a : P, cols],
+                        start=(turn, k) == (0, 0),
+                        stop=(turn, k) == (1, slices - 1),
+                    )
+            return bank
 
-        steps = held([P, PACK, S], F32, "wb_planes")
-        targets = [steps[:, s : s + slices, first : first + count] for s, slices, first, count in first_units]
-        targets[-1] = shaped(targets[-1][:, 0, :], pending[1][-1])
-        guard(targets, *pending, (0, 2, 4, 1, 3, 7, 5, 6))
-        nc.gpsimd.tensor_tensor(scaled[:, 0, :HALF], steps[:, 0, :HALF], first_factors[:, :HALF], MULT)
-        nc.gpsimd.tensor_tensor(scaled[:, 0, HALF:], steps[:, 0, HALF:], first_factors[:, HALF:], MULT)
+        def turned_sums(block, number):
+            cols = slice(block * BLOCK, (block + 1) * BLOCK)
+            bank = bank_tile(number, [P, PASS])
+            for a in range(2):
+                codes, plane = wa_moving[1, a]
+                nc.tensor.matmul_mx(
+                    out=bank[:],
+                    lhsT=picked[a][:, cols].bitcast(E4M3),
+                    lhsT_scale=picked_planes[ROWS * a : P, cols],
+                    rhs=codes[:].bitcast(E4M3),
+                    rhs_scale=plane[:],
+                    start=(a == 0),
+                    stop=(a == 1),
+                )
+            return bank
+
+        def shaped(view, like):
+            return view.rearrange("p (r c) -> p r c", r=like.shape[1])
+
+        def in_strips(bank, strip):
+            return bank[:].rearrange("p s n -> p (s n)").rearrange("p (r c) -> p r c", c=strip)
+
+        def sigmoid(place, view):
+            nc.scalar.activation(place, view, SIGMOID, scale=-1.0)
+
+        def logarithm(place, gates):
+            nc.scalar.activation(place, gates, LN, bias=FLOOR)
+
+        def guard(target, logs, view):
+            nc.vector.scalar_tensor_tensor(target, logs, -1.0, view, MULT, MAX)
+
+        def scale_steps(target, steps, s, first, count):
+            nc.vector.tensor_tensor(target, factors[s][:].indirect(list_part(first, count)), steps, MULT)
 
         def inputs_of(b, block, number):
             cols = slice(block * BLOCK, (block + 1) * BLOCK)
@@ -293,25 +259,27 @@ def tile_list_softplus_step_input_kernel(
                     )
             return bank
 
-        def finish(b, block, bank, column=None, count=BLOCK):
-            cols = slice(block * BLOCK, block * BLOCK + count)
-            column = block * BLOCK if column is None else column
-            sources = scaled[:, b * PACK : (b + 1) * PACK, column : column + count]
+        h_rounded = [held([P, S, PACK], BF16, "table%d" % b) for b in range(2)]
+        h_quantised = {}
+
+        def finish(b, block, bank, scaled):
             nc.vector.tensor_tensor(
-                h_rounded[b][:, cols, :].rearrange("p (c i) t -> p c t i", i=LINE),
-                bank[:, :, :count].rearrange("p t (c i) -> p c t i", i=LINE),
-                sources.rearrange("p t (c i) -> p c t i", i=LINE),
+                h_rounded[b][:, block * BLOCK : (block + 1) * BLOCK, :].rearrange("p (c i) t -> p c t i", i=LINE),
+                bank[:].rearrange("p t (c i) -> p c t i", i=LINE),
+                scaled.rearrange("p t (c i) -> p c t i", i=LINE),
                 MULT,
             )
 
-        def finish_aside(b, block, bank, slot, first=0):
-            cols = slice(block * BLOCK + first, (block + 1) * BLOCK)
-            woven = held([P, BLOCK - first, PACK], F32, slot)
-            nc.scalar.copy(woven[:], bank[:, :, first:].rearrange("p t n -> p n t"))
-            return lambda: nc.gpsimd.tensor_tensor(
-                h_rounded[b][:, cols, :],
+        def weave(bank, slot):
+            woven = held([P, BLOCK, PACK], F32, slot)
+            nc.scalar.copy(woven[:], bank[:].rearrange("p t n -> p n t"))
+            return woven
+
+        def finish_aside(b, block, woven, scaled):
+            nc.gpsimd.tensor_tensor(
+                h_rounded[b][:, block * BLOCK : (block + 1) * BLOCK, :],
                 woven[:],
-                scaled[:, b * PACK : (b + 1) * PACK, cols].rearrange("p t n -> p n t"),
+                scaled.rearrange("p t n -> p n t"),
                 MULT,
             )
 
@@ -321,68 +289,131 @@ def tile_list_softplus_step_input_kernel(
             for block in range(first, first + count):
                 h_quantised[b, block] = (codes, plane, (block - first) * BLOCK)
 
-        def half_logs(half, numbers, logs, gates):
-            first = half * HALF
-            units = (
-                (4, 2, first, QUARTER),
-                (6, 2, first, QUARTER),
-                (4, 4, first + QUARTER, BLOCK),
-                (4, 4, first + QUARTER + BLOCK, BLOCK),
-            )
-            wide = HALF + BLOCK
-            starts = [BLOCK + wide * k for k in range(3)]
-            spans = [(0, wide), (wide, 2 * wide), (2 * wide, 3 * wide + BLOCK)]
-            return units, logs_of(sums_of(units, numbers), logs, BLOCK, starts, spans, gates)
+        def block_of(view, block):
+            return view[:, :, block * BLOCK : (block + 1) * BLOCK]
 
-        def half_guard(units, pending, slot):
-            steps = held([P, PACK, HALF], F32, slot)
-            targets = [steps[:, s - PACK : s - PACK + slices, first % HALF : first % HALF + count] for s, slices, first, count in units]
-            guard(targets, *pending, range(4))
-            return steps
+        first_units = (
+            (0, 2, 0, QUARTER),
+            (2, 2, 0, QUARTER),
+            (0, 2, QUARTER, QUARTER),
+            (2, 2, QUARTER, QUARTER),
+            (0, 1, HALF, HALF),
+            (1, 1, HALF, HALF),
+            (3, 1, HALF, HALF),
+            (2, 1, HALF, HALF),
+        )
+        banks = [sums(first_units[n], n, ((0, 0),)) for n in range(LEAD)]
+        for n in range(LEAD):
+            sums(first_units[n], n, ((1, 1),), banks[n])
+        banks += [sums(first_units[n], n, (1, 0)) for n in range(LEAD, 8)]
+        order = (0, 2, 4, 1, 3, 5, 6)
+        area = held([P, len(first_units) + SHIFT, HALF + STRIP], F32, "logs")
+        views = [bank[:] for bank in banks[:-1]] + [in_strips(banks[-1], STRIP)]
 
-        aside = [finish_aside(0, 5 + n, inputs_of(0, 5 + n, number), "woven%d" % n) for n, number in enumerate((1, 3, 7))]
-        gates = held([P, PACK * (HALF + BLOCK)], F32, "raw11")
-        logs = held([P, PACK * (HALF + BLOCK)], F32, "first_factors")
-        units, pending = half_logs(0, (0, 2, 4, 1), logs[:], gates[:])
-        own = [inputs_of(0, block, number) for block, number in enumerate((5, 6, 3, 7))]
+        def places_from(first):
+            rows = {n: shaped(area[:, first + k, :HALF], views[n]) for k, n in enumerate(order)}
+            return [rows[n] for n in range(len(order))] + [area[:, first : first + HALF // STRIP, HALF:]]
+
+        places = places_from(0)
+        for place, view in zip(places_from(SHIFT), views):
+            sigmoid(place, view)
+        for k in range(5):
+            logarithm(area[:, k, :], area[:, SHIFT + k, :])
+        logarithm(area[:, 5:8, HALF:], area[:, SHIFT + 5 :, HALF:])
+        for k in (5, 6):
+            logarithm(area[:, k, :HALF], area[:, SHIFT + k, :HALF])
+
+        steps = held([P, PACK, S], F32, "wb_planes")
+        scaled = held([P, PACK, S], F32, "scaled")
+        targets = [steps[:, s : s + slices, first : first + count] for s, slices, first, count in first_units]
+        targets[-1] = shaped(targets[-1][:, 0, :], places[-1])
+        for n in (0, 2, 4, 1, 3, 7, 5, 6):
+            guard(targets[n], places[n], views[n])
+        for half in (slice(0, HALF), slice(HALF, S)):
+            nc.gpsimd.tensor_tensor(scaled[:, 0, half], steps[:, 0, half], early_factors[:, half], MULT)
+        woven = [weave(inputs_of(0, 5 + n, number), "woven%d" % n) for n, number in enumerate((0, 2, 4))]
+
         for s in (1, 2, 3):
-            scale_steps(steps[:, s, :], s, 0, S)
-        for product in aside:
-            product()
-        finish(0, 0, own[0])
-        shared = inputs_of(0, 4, 5)
-        for block in range(1, 4):
-            finish(0, block, own[block])
-        steps = half_guard(units, pending, "wb_planes")
-        finish(0, 4, shared)
+            scale_steps(scaled[:, s, :], steps[:, s, :], s, 0, S)
 
-        def round_wo(b, slot):
-            rounded = held([P, N, PACK], BF16, slot)
+        units = ((4, 2, 0, QUARTER), (6, 2, 0, QUARTER), (6, 2, QUARTER, QUARTER), (4, 2, QUARTER, QUARTER))
+        numbers = (7, 4, 6, 5)
+        late_gates = held([P, PACK, HALF], F32, "late_gates")
+        wide = HALF + QUARTER
+        gates = held([P, 5 * HALF], F32, "logs")
+        logs = held([P, 2 * wide], F32, "early_logs")
+
+        def pair(area, column):
+            return area[:, column : column + HALF].rearrange("p (s n) -> p s n", s=2)
+
+        def strips(area):
+            return area[:, 0 : 2 * wide].rearrange("p (s n) -> p s n", s=2)[:, :, 0:QUARTER]
+
+        gate_places = (pair(gates, QUARTER), pair(gates, wide + QUARTER), strips(gates), pair(gates, 2 * wide))
+        log_places = (pair(logs, QUARTER), pair(logs, wide + QUARTER), strips(logs), pair(gates, 0))
+        banks = {}
+        for first, passing, kept in ((0, (1, 3), (0, 3)), (2, (0, 2), (1, 2))):
+            for k in range(2):
+                nc.scalar.activation(late_gates[:, first + k, :], turned_sums(PACK + first + k, passing[k])[:], SIGMOID)
+            for n in kept:
+                banks[n] = sums(units[n], numbers[n])
+                sigmoid(gate_places[n], banks[n][:])
+        for k in range(2):
+            logarithm(logs[:, k * wide : (k + 1) * wide], gates[:, k * wide : (k + 1) * wide])
+        logarithm(log_places[3], gate_places[3])
+        late_logs = gates[:, HALF:]
+        logarithm(late_logs, late_gates[:].rearrange("p s n -> p (s n)"))
+
+        own = [inputs_of(0, block, number) for block, number in enumerate((1, 3, 0, 2))]
+        for n in range(3):
+            finish_aside(0, 5 + n, woven[n], block_of(scaled, 5 + n))
+        finish(0, 0, own[0], block_of(scaled, 0))
+        own.append(inputs_of(0, 4, 1))
+        for block in range(1, 5):
+            finish(0, block, own[block], block_of(scaled, block))
+        steps = held([P, PACK, HALF], F32, "wb_planes")
+        for n, (s, slices, first, count) in enumerate(units):
+            guard(steps[:, s - PACK : s - PACK + slices, first : first + count], log_places[n], banks[n][:])
+
+        negated = held([P, PACK, PASS], F32, "factors2")
+        for k, number in enumerate((3, 0, 2, 1)):
+            nc.scalar.activation(negated[:, k, :], turned_sums(PACK + k, number)[:], COPY, scale=-1.0)
+        woven = weave(inputs_of(1, 3, 3), "woven0")
+        late = {block: inputs_of(1, block, number) for block, number in enumerate((0, 2, 1))}
+        banks = [bank_tile(number, [P, PACK, BLOCK]) for number in numbers]
+        terms = (late_logs.rearrange("p (k c) -> p k c", k=PACK), negated[:])
+        for n, term in enumerate(terms):
+            for k in range(PACK):
+                for t in range(PACK):
+                    nc.tensor.matmul(
+                        banks[t][:, k, :],
+                        lhsT=term[:, k, t * P : (t + 1) * P],
+                        rhs=identity[:],
+                        is_transpose=True,
+                        start=(n, k) == (0, 0),
+                        stop=(n, k) == (1, PACK - 1),
+                    )
+        late_steps = held([P, PACK, HALF], F32, "factors1")
+        for t in range(PACK):
+            nc.scalar.activation(late_steps[:, t, :], banks[t][:].rearrange("p k n -> p (k n)"), RELU, scale=-1.0)
+        wo_rounded = []
+        for b, slot in enumerate(("late_gates", "factors2")):
+            wo_rounded.append(held([P, N, PACK], BF16, slot))
             nc.scalar.copy(
-                rounded[:].rearrange("p (c i) t -> p c t i", i=LINE),
+                wo_rounded[b][:].rearrange("p (c i) t -> p c t i", i=LINE),
                 wo_raw[b][:].rearrange("p t (c i) -> p c t i", i=LINE),
             )
-            return rounded
-
-        wo_rounded = [round_wo(0, "raw11")]
-        late = {block: inputs_of(1, block, number) for block, number in ((2, 6), (3, 3))}
-        aside = [finish_aside(1, block, late[block], "woven%d" % (block - 2)) for block in (2, 3)]
-        gates = held([P, PACK * (HALF + BLOCK)], F32, "raw10")
-        units, pending = half_logs(1, (7, 0, 5, 6), work[:], gates[:])
-        wo_rounded.append(round_wo(1, "raw10"))
-        for block, number in zip((0, 1, 4, 5), (2, 3, 4, 1)):
+        for block, number in ((4, 7), (5, 4)):
             late[block] = inputs_of(1, block, number)
 
-        scale_steps(steps[:, 0, :], 4, 0, HALF)
-        quantise_h(0, 0, 8, "first_factors")
-        scale_steps(steps[:, 1, :], 5, 0, HALF)
-        scale_steps(steps[:, 2, :], 6, 0, HALF)
-        scale_steps(steps[:, 3, :], 7, 0, HALF)
-        for product in aside:
-            product()
-        for block in range(2):
-            finish(1, block, late[block])
-        steps = half_guard(units, pending, "wb_planes")
+        scaled = held([P, PACK, HALF], F32, "scaled")
+        scale_steps(scaled[:, 0, :], steps[:, 0, :], 4, 0, HALF)
+        quantise_h(0, 0, 8, "early_logs")
+        for k in range(1, PACK):
+            scale_steps(scaled[:, k, :], steps[:, k, :], PACK + k, 0, HALF)
+        finish_aside(1, 3, woven, block_of(scaled, 3))
+        for block in range(3):
+            finish(1, block, late[block], block_of(scaled, block))
 
         def project(target, c, b, first, count, start, stop):
             codes, plane = wo_quantised[b]
@@ -416,30 +447,33 @@ def tile_list_softplus_step_input_kernel(
                     rows = slice((n + 1 - banks_a_store) * share, (n + 1) * share)
                     nc.sync.dma_start(out_rows[:, rows, cols], result[:, rows, :])
 
+        tail = held([P, PACK, QUARTER], F32, "early_factors")
+
         def scale_group(first, count, column):
-            for s in range(PACK, 2 * PACK):
-                scale_steps(steps[:, s - PACK, first - HALF : first - HALF + count], s, first, count, column)
+            for k in range(PACK):
+                part = late_steps[:, k, first - HALF : first - HALF + count]
+                scale_steps(tail[:, k, column : column + count], part, PACK + k, first, count)
 
         scalar_copies = (nc.scalar.copy, nc.scalar.copy)
-        scale_group(HALF, QUARTER, HALF)
+        scale_group(HALF, QUARTER, 0)
         wo_quantised = [
             quantise(wo_rounded[b][:].rearrange("p n t -> p (n t)"), "wo%d" % b, slot)
-            for b, slot in enumerate(("woven1", "woven0"))
+            for b, slot in enumerate(("woven0", "woven1"))
         ]
         quantise_h(1, 0, 4)
-        emit(0, 2, (2, 3), scalar_copies, "factors1")
-        emit(2, 2, (7, 5), scalar_copies, "factors2")
-        for block, number in ((6, 0), (7, 6)):
+        emit(0, 2, (3, 0), scalar_copies, "factors3")
+        emit(2, 2, (2, 1), scalar_copies, "logs")
+        for block, number in ((6, 6), (7, 5)):
             late[block] = inputs_of(1, block, number)
         for block in (4, 5):
-            finish(1, block, late[block])
-        scale_group(6 * BLOCK, BLOCK, 4 * BLOCK)
+            finish(1, block, late[block], block_of(tail, block - 4))
+        scale_group(6 * BLOCK, BLOCK, 0)
         quantise_h(1, 4, 2)
-        emit(4, 2, (2, 3), scalar_copies, "factors3")
-        finish(1, 6, late[6], 4 * BLOCK)
-        scale_group(7 * BLOCK, BLOCK, 5 * BLOCK)
+        emit(4, 2, (3, 0), scalar_copies, "raw00")
+        finish(1, 6, late[6], block_of(tail, 0))
+        scale_group(7 * BLOCK, BLOCK, BLOCK)
         quantise_h(1, 6, 1)
-        emit(6, 1, (4,), scalar_copies, "raw10")
-        finish(1, 7, late[7], 5 * BLOCK)
+        emit(6, 1, (7,), scalar_copies, "wo_raw")
+        finish(1, 7, late[7], block_of(tail, 1))
         quantise_h(1, 7, 1)
-        emit(7, 1, (1, 7, 5, 0), (nc.scalar.copy, nc.vector.tensor_copy) * 2, "raw11", 2)
+        emit(7, 1, (4, 2, 1, 6), (nc.scalar.copy, nc.vector.tensor_copy) * 2, "rounded_wide", 2)

@@ -331,13 +331,11 @@ def tile_list_softplus_step_input_kernel(
             guard(targets[n], places[n], views[n])
         for half in (slice(0, HALF), slice(HALF, S)):
             nc.gpsimd.tensor_tensor(scaled[:, 0, half], steps[:, 0, half], early_factors[:, half], MULT)
-        woven = [weave(inputs_of(0, 5 + n, number), "woven%d" % n) for n, number in enumerate((0, 2, 4))]
-
         for s in (1, 2, 3):
             scale_steps(scaled[:, s, :], steps[:, s, :], s, 0, S)
 
         units = ((4, 2, 0, QUARTER), (6, 2, 0, QUARTER), (6, 2, QUARTER, QUARTER), (4, 2, QUARTER, QUARTER))
-        numbers = (7, 4, 6, 5)
+        numbers = (3, 7, 0, 5)
         late_gates = held([P, PACK, HALF], F32, "late_gates")
         wide = HALF + QUARTER
         gates = held([P, 5 * HALF], F32, "logs")
@@ -351,51 +349,57 @@ def tile_list_softplus_step_input_kernel(
 
         gate_places = (pair(gates, QUARTER), pair(gates, wide + QUARTER), strips(gates), pair(gates, 2 * wide))
         log_places = (pair(logs, QUARTER), pair(logs, wide + QUARTER), strips(logs), pair(gates, 0))
+        for k, number in enumerate((0, 2, 4, 1)):
+            nc.scalar.activation(late_gates[:, k, :], turned_sums(PACK + k, number)[:], SIGMOID)
         banks = {}
-        for first, passing, kept in ((0, (1, 3), (0, 3)), (2, (0, 2), (1, 2))):
-            for k in range(2):
-                nc.scalar.activation(late_gates[:, first + k, :], turned_sums(PACK + first + k, passing[k])[:], SIGMOID)
-            for n in kept:
-                banks[n] = sums(units[n], numbers[n])
-                sigmoid(gate_places[n], banks[n][:])
+        woven = []
+        for n, number in zip((0, 1, 3), (0, 2, 4)):
+            banks[n] = sums(units[n], numbers[n])
+            sigmoid(gate_places[n], banks[n][:])
+            woven.append(weave(inputs_of(0, 5 + len(woven), number), "woven%d" % len(woven)))
+        banks[2] = sums(units[2], numbers[2])
+        sigmoid(gate_places[2], banks[2][:])
         for k in range(2):
             logarithm(logs[:, k * wide : (k + 1) * wide], gates[:, k * wide : (k + 1) * wide])
         logarithm(log_places[3], gate_places[3])
         late_logs = gates[:, HALF:]
         logarithm(late_logs, late_gates[:].rearrange("p s n -> p (s n)"))
 
-        own = [inputs_of(0, block, number) for block, number in enumerate((1, 3, 0, 2))]
+        own = [inputs_of(0, block, number) for block, number in enumerate((6, 1, 2, 4))]
         for n in range(3):
             finish_aside(0, 5 + n, woven[n], block_of(scaled, 5 + n))
         finish(0, 0, own[0], block_of(scaled, 0))
-        own.append(inputs_of(0, 4, 1))
+        own.append(inputs_of(0, 4, 6))
         for block in range(1, 5):
             finish(0, block, own[block], block_of(scaled, block))
         steps = held([P, PACK, HALF], F32, "wb_planes")
         for n, (s, slices, first, count) in enumerate(units):
             guard(steps[:, s - PACK : s - PACK + slices, first : first + count], log_places[n], banks[n][:])
 
+        woven = weave(inputs_of(1, 3, 4), "woven0")
         negated = held([P, PACK, PASS], F32, "factors2")
-        for k, number in enumerate((3, 0, 2, 1)):
+        differences = [bank_tile(number, [P, PACK, BLOCK]) for number in numbers]
+
+        def add_turned(k, term, opens):
+            for t in range(PACK):
+                nc.tensor.matmul(
+                    differences[k][:, t, :],
+                    lhsT=term[:, t * P : (t + 1) * P],
+                    rhs=identity[:],
+                    is_transpose=True,
+                    start=opens and t == 0,
+                    stop=not opens and t == PACK - 1,
+                )
+
+        for k, number in enumerate((1, 2, 1, 2)):
             nc.scalar.activation(negated[:, k, :], turned_sums(PACK + k, number)[:], COPY, scale=-1.0)
-        woven = weave(inputs_of(1, 3, 3), "woven0")
-        late = {block: inputs_of(1, block, number) for block, number in enumerate((0, 2, 1))}
-        banks = [bank_tile(number, [P, PACK, BLOCK]) for number in numbers]
-        terms = (late_logs.rearrange("p (k c) -> p k c", k=PACK), negated[:])
-        for n, term in enumerate(terms):
-            for k in range(PACK):
-                for t in range(PACK):
-                    nc.tensor.matmul(
-                        banks[t][:, k, :],
-                        lhsT=term[:, k, t * P : (t + 1) * P],
-                        rhs=identity[:],
-                        is_transpose=True,
-                        start=(n, k) == (0, 0),
-                        stop=(n, k) == (1, PACK - 1),
-                    )
+        for k in range(PACK):
+            add_turned(k, late_logs[:, k * PASS : (k + 1) * PASS], True)
+            add_turned(k, negated[:, k, :], False)
+        late = {block: inputs_of(1, block, number) for block, number in enumerate((6, 4, 1))}
         late_steps = held([P, PACK, HALF], F32, "factors1")
-        for t in range(PACK):
-            nc.scalar.activation(late_steps[:, t, :], banks[t][:].rearrange("p k n -> p (k n)"), RELU, scale=-1.0)
+        for k in range(PACK):
+            nc.scalar.activation(block_of(late_steps, k), differences[k][:], RELU, scale=-1.0)
         wo_rounded = []
         for b, slot in enumerate(("late_gates", "factors2")):
             wo_rounded.append(held([P, N, PACK], BF16, slot))
@@ -403,7 +407,7 @@ def tile_list_softplus_step_input_kernel(
                 wo_rounded[b][:].rearrange("p (c i) t -> p c t i", i=LINE),
                 wo_raw[b][:].rearrange("p t (c i) -> p c t i", i=LINE),
             )
-        for block, number in ((4, 7), (5, 4)):
+        for block, number in ((4, 3), (5, 7)):
             late[block] = inputs_of(1, block, number)
 
         scaled = held([P, PACK, HALF], F32, "scaled")
@@ -447,33 +451,34 @@ def tile_list_softplus_step_input_kernel(
                     rows = slice((n + 1 - banks_a_store) * share, (n + 1) * share)
                     nc.sync.dma_start(out_rows[:, rows, cols], result[:, rows, :])
 
-        tail = held([P, PACK, QUARTER], F32, "early_factors")
+        tail = held([P, PACK, QUARTER], F32, "scaled")
 
-        def scale_group(first, count, column):
+        def scale_group(tail, first, count, column):
             for k in range(PACK):
                 part = late_steps[:, k, first - HALF : first - HALF + count]
                 scale_steps(tail[:, k, column : column + count], part, PACK + k, first, count)
 
         scalar_copies = (nc.scalar.copy, nc.scalar.copy)
-        scale_group(HALF, QUARTER, 0)
+        scale_group(tail, HALF, QUARTER, 0)
         wo_quantised = [
             quantise(wo_rounded[b][:].rearrange("p n t -> p (n t)"), "wo%d" % b, slot)
             for b, slot in enumerate(("woven0", "woven1"))
         ]
         quantise_h(1, 0, 4)
-        emit(0, 2, (3, 0), scalar_copies, "factors3")
-        emit(2, 2, (2, 1), scalar_copies, "logs")
-        for block, number in ((6, 6), (7, 5)):
+        emit(0, 2, (2, 6), scalar_copies, "factors3")
+        emit(2, 2, (4, 1), scalar_copies, "logs")
+        for block, number in ((6, 0), (7, 5)):
             late[block] = inputs_of(1, block, number)
         for block in (4, 5):
             finish(1, block, late[block], block_of(tail, block - 4))
-        scale_group(6 * BLOCK, BLOCK, 0)
+        tail = held([P, PACK, QUARTER], F32, "factors2")
+        scale_group(tail, 6 * BLOCK, BLOCK, 0)
         quantise_h(1, 4, 2)
-        emit(4, 2, (3, 0), scalar_copies, "raw00")
+        emit(4, 2, (2, 6), scalar_copies, "raw00")
         finish(1, 6, late[6], block_of(tail, 0))
-        scale_group(7 * BLOCK, BLOCK, BLOCK)
+        scale_group(tail, 7 * BLOCK, BLOCK, BLOCK)
         quantise_h(1, 6, 1)
-        emit(6, 1, (7,), scalar_copies, "wo_raw")
+        emit(6, 1, (3,), scalar_copies, "wo_raw")
         finish(1, 7, late[7], block_of(tail, 1))
         quantise_h(1, 7, 1)
-        emit(7, 1, (4, 2, 1, 6), (nc.scalar.copy, nc.vector.tensor_copy) * 2, "rounded_wide", 2)
+        emit(7, 1, (7, 4, 1, 0), (nc.scalar.copy, nc.vector.tensor_copy) * 2, "rounded_wide", 2)

@@ -112,14 +112,20 @@ def tile_list_softplus_step_input_kernel(
         load_wa(1, 0)
         load_factors(0, "factors0")
         load_wa(1, 1)
-        wb_raw = held([P, 2, H // 2], I32, "wb_raw")
-        nc.sync.dma_start(wb_raw[:], wb_words.rearrange("a p w -> p a w").bitcast(I32))
         for r in range(ROWS):
             nc.sync.dma_start(
                 wb_planes[r:P:QUADRANT, :, :].bitcast(I32),
                 wb_scales.rearrange("a (q r) c -> r q a c", r=ROWS)[r].bitcast(I32),
             )
+        wb_raw = {}
+
+        def load_wb(b, slot):
+            wb_raw[b] = held([P, 2, H // 4], I32, slot)
+            nc.sync.dma_start(wb_raw[b][:], wb_words.rearrange("a p (b w) -> b p a w", b=2)[b].bitcast(I32))
+
+        load_wb(0, "wb_early_raw")
         load_factors(1, "factors1")
+        load_wb(1, "wb_raw")
         for r in range(ROWS):
             nc.sync.dma_start(
                 moved_plane[r:P:QUADRANT, :].bitcast(I32),
@@ -165,7 +171,7 @@ def tile_list_softplus_step_input_kernel(
         quantise_wa(1, 0, 0, round_wa(1, 0, 0, PACK, nc.vector.tensor_copy, "rounded_wide"))
         early_factors = held([P, S], F32, "early_factors")
         nc.vector.tensor_copy(early_factors[:], factors[0][:].indirect(offsets[:]))
-        quantise_wa(1, 1, 0, round_wa(1, 1, 0, PACK, nc.vector.tensor_copy, "rounded_wide"))
+        last_rounded = round_wa(1, 1, 0, PACK, nc.vector.tensor_copy, "steps")
 
         wo_raw = []
 
@@ -177,19 +183,23 @@ def tile_list_softplus_step_input_kernel(
         for s in (2, 3):
             load_factors(s, "factors%d" % s)
         load_wo(0, "raw00")
-        for s, slot in zip(range(4, 8), ("factors0", "raw01", "raw10", "raw11")):
-            load_factors(s, slot)
+        load_factors(4, "factors0")
         load_wo(1, "wo_raw")
+        for s, slot in zip(range(5, 8), ("raw01", "raw10", "raw11")):
+            load_factors(s, slot)
 
-        wb_codes = held([P, 4, PACK, P // RUN, 2], I32, "wb_codes")
-        nc.vector.tensor_copy(
-            wb_codes[:], wb_raw[:].rearrange("p a (b m t w) -> p (a b) t m w", b=2, t=PACK, w=2)
-        )
-        wb_dealt_planes = held([P, 4, PACK, P // RUN], I32, "wb_dealt_planes")
-        nc.vector.tensor_copy(
-            wb_dealt_planes[:].rearrange("p g t (q i) -> p g q t i", i=LINE),
-            wb_planes[:].bitcast(I32).rearrange("p a (b q i t) -> p (a b) q t i", b=2, i=LINE, t=PACK),
-        )
+        wb_codes = {}
+        wb_dealt_planes = {}
+
+        def deal_wb(b, copy, dtype, slot):
+            wb_dealt_planes[b] = held([P, 2, PACK, P // RUN], dtype, "wb_dealt_planes%d" % b)
+            rows = wb_planes[:].bitcast(dtype).rearrange("p a (b q i t) -> p b a q t i", b=2, i=LINE, t=PACK)
+            copy(wb_dealt_planes[b][:].rearrange("p a t (q i) -> p a q t i", i=LINE), rows[:, b])
+            wb_codes[b] = held([P, 2, PACK, P // RUN, 2], dtype, slot)
+            copy(wb_codes[b][:], wb_raw[b][:].bitcast(dtype).rearrange("p a (m t w) -> p a t m w", t=PACK, w=2))
+
+        deal_wb(0, nc.vector.tensor_copy, I32, "wb_codes")
+        quantise_wa(1, 1, 0, last_rounded, "wb_early_raw")
 
         def sums(unit, number, passes=(0, 1), bank=None):
             s, slices, first, count = unit
@@ -250,8 +260,8 @@ def tile_list_softplus_step_input_kernel(
                 for a in range(2):
                     nc.tensor.matmul_mx(
                         out=bank[:, t, :],
-                        lhsT=wb_codes[:, 2 * a + b, t].rearrange("p m w -> p (m w)").bitcast(E2M1),
-                        lhsT_scale=wb_dealt_planes[:, 2 * a + b, t].bitcast(U8),
+                        lhsT=wb_codes[b][:, a, t].rearrange("p m w -> p (m w)").bitcast(E2M1),
+                        lhsT_scale=wb_dealt_planes[b][:, a, t].bitcast(U8),
                         rhs=picked[a][:, cols].bitcast(E4M3),
                         rhs_scale=(picked_planes, moved_plane)[a][:, cols],
                         start=(a == 0),
@@ -323,7 +333,7 @@ def tile_list_softplus_step_input_kernel(
         for k in (5, 6):
             logarithm(area[:, k, :HALF], area[:, SHIFT + k, :HALF])
 
-        steps = held([P, PACK, S], F32, "wb_planes")
+        steps = held([P, PACK, S], F32, "steps")
         scaled = held([P, PACK, S], F32, "scaled")
         targets = [steps[:, s : s + slices, first : first + count] for s, slices, first, count in first_units]
         targets[-1] = shaped(targets[-1][:, 0, :], places[-1])
@@ -331,10 +341,11 @@ def tile_list_softplus_step_input_kernel(
             guard(targets[n], places[n], views[n])
         for half in (slice(0, HALF), slice(HALF, S)):
             nc.gpsimd.tensor_tensor(scaled[:, 0, half], steps[:, 0, half], early_factors[:, half], MULT)
-        for s in (1, 2, 3):
-            scale_steps(scaled[:, s, :], steps[:, s, :], s, 0, S)
+        for s, first, count in ((1, 0, S), (2, 0, S), (3, 0, HALF), (3, HALF, HALF)):
+            cols = slice(first, first + count)
+            scale_steps(scaled[:, s, cols], steps[:, s, cols], s, first, count)
 
-        units = ((4, 2, 0, QUARTER), (6, 2, 0, QUARTER), (6, 2, QUARTER, QUARTER), (4, 2, QUARTER, QUARTER))
+        units = ((6, 2, 0, QUARTER), (4, 2, 0, QUARTER), (4, 2, QUARTER, QUARTER), (6, 2, QUARTER, QUARTER))
         numbers = (3, 7, 0, 5)
         late_gates = held([P, PACK, HALF], F32, "late_gates")
         wide = HALF + QUARTER
@@ -357,6 +368,7 @@ def tile_list_softplus_step_input_kernel(
             banks[n] = sums(units[n], numbers[n])
             sigmoid(gate_places[n], banks[n][:])
             woven.append(weave(inputs_of(0, 5 + len(woven), number), "woven%d" % len(woven)))
+        deal_wb(1, nc.scalar.copy, U32, "wb_late_codes")
         banks[2] = sums(units[2], numbers[2])
         sigmoid(gate_places[2], banks[2][:])
         for k in range(2):
@@ -372,18 +384,17 @@ def tile_list_softplus_step_input_kernel(
         own.append(inputs_of(0, 4, 6))
         for block in range(1, 5):
             finish(0, block, own[block], block_of(scaled, block))
-        steps = held([P, PACK, HALF], F32, "wb_planes")
+        steps = held([P, PACK, HALF], F32, "steps")
         for n, (s, slices, first, count) in enumerate(units):
             guard(steps[:, s - PACK : s - PACK + slices, first : first + count], log_places[n], banks[n][:])
 
         woven = weave(inputs_of(1, 3, 4), "woven0")
-        negated = held([P, PACK, PASS], F32, "factors2")
-        differences = [bank_tile(number, [P, PACK, BLOCK]) for number in numbers]
+        late_steps = held([P, PACK, HALF], F32, "factors1")
 
-        def add_turned(k, term, opens):
+        def add_turned(bank, term, opens):
             for t in range(PACK):
                 nc.tensor.matmul(
-                    differences[k][:, t, :],
+                    bank[:, t, :],
                     lhsT=term[:, t * P : (t + 1) * P],
                     rhs=identity[:],
                     is_transpose=True,
@@ -391,20 +402,23 @@ def tile_list_softplus_step_input_kernel(
                     stop=not opens and t == PACK - 1,
                 )
 
-        for k, number in enumerate((1, 2, 1, 2)):
-            nc.scalar.activation(negated[:, k, :], turned_sums(PACK + k, number)[:], COPY, scale=-1.0)
-        for k in range(PACK):
-            add_turned(k, late_logs[:, k * PASS : (k + 1) * PASS], True)
-            add_turned(k, negated[:, k, :], False)
-        late = {block: inputs_of(1, block, number) for block, number in enumerate((6, 4, 1))}
-        late_steps = held([P, PACK, HALF], F32, "factors1")
-        for k in range(PACK):
-            nc.scalar.activation(block_of(late_steps, k), differences[k][:], RELU, scale=-1.0)
-        wo_rounded = []
-        for b, slot in enumerate(("late_gates", "factors2")):
-            wo_rounded.append(held([P, N, PACK], BF16, slot))
+        def steps_aside(first, slot, numbers):
+            negated = held([P, 2, PASS], F32, slot)
+            for n in range(2):
+                nc.scalar.activation(negated[:, n, :], turned_sums(PACK + first + n, 1 + n)[:], COPY, scale=-1.0)
+            for n, number in enumerate(numbers):
+                k = first + n
+                bank = bank_tile(number, [P, PACK, BLOCK])
+                add_turned(bank, late_logs[:, k * PASS : (k + 1) * PASS], True)
+                add_turned(bank, negated[:, n, :], False)
+                nc.scalar.activation(block_of(late_steps, k), bank[:], RELU, scale=-1.0)
+
+        steps_aside(0, "factors2", (3, 7))
+        late = {block: inputs_of(1, block, number) for block, number in enumerate((6, 4, 0))}
+        wo_rounded = held([P, 2, N, PACK], BF16, "factors2")
+        for b in range(2):
             nc.scalar.copy(
-                wo_rounded[b][:].rearrange("p (c i) t -> p c t i", i=LINE),
+                wo_rounded[:, b].rearrange("p (c i) t -> p c t i", i=LINE),
                 wo_raw[b][:].rearrange("p t (c i) -> p c t i", i=LINE),
             )
         for block, number in ((4, 3), (5, 7)):
@@ -413,20 +427,23 @@ def tile_list_softplus_step_input_kernel(
         scaled = held([P, PACK, HALF], F32, "scaled")
         scale_steps(scaled[:, 0, :], steps[:, 0, :], 4, 0, HALF)
         quantise_h(0, 0, 8, "early_logs")
-        for k in range(1, PACK):
-            scale_steps(scaled[:, k, :], steps[:, k, :], PACK + k, 0, HALF)
+        for k, first, count in ((1, 0, HALF), (2, 0, HALF), (3, 0, QUARTER), (3, QUARTER, QUARTER)):
+            cols = slice(first, first + count)
+            scale_steps(scaled[:, k, cols], steps[:, k, cols], PACK + k, first, count)
         finish_aside(1, 3, woven, block_of(scaled, 3))
         for block in range(3):
             finish(1, block, late[block], block_of(scaled, block))
 
+        steps_aside(2, "wo_raw", (6, 4))
+
         def project(target, c, b, first, count, start, stop):
-            codes, plane = wo_quantised[b]
+            rows = slice(b * N + c * P, b * N + (c + 1) * P)
             h_codes, h_plane, column = h_quantised[b, first]
             cols = slice(column, column + count * BLOCK)
             nc.tensor.matmul_mx(
                 out=target,
-                lhsT=codes[:, c * P : (c + 1) * P].bitcast(E4M3),
-                lhsT_scale=plane[:, c * P : (c + 1) * P],
+                lhsT=wo_codes[:, rows].bitcast(E4M3),
+                lhsT_scale=wo_plane[:, rows],
                 rhs=h_codes[:, cols].bitcast(E4M3),
                 rhs_scale=h_plane[:, cols],
                 start=start,
@@ -460,25 +477,22 @@ def tile_list_softplus_step_input_kernel(
 
         scalar_copies = (nc.scalar.copy, nc.scalar.copy)
         scale_group(tail, HALF, QUARTER, 0)
-        wo_quantised = [
-            quantise(wo_rounded[b][:].rearrange("p n t -> p (n t)"), "wo%d" % b, slot)
-            for b, slot in enumerate(("woven0", "woven1"))
-        ]
+        wo_codes, wo_plane = quantise(wo_rounded[:].rearrange("p b n t -> p (b n t)"), "wo", "woven0")
         quantise_h(1, 0, 4)
-        emit(0, 2, (2, 6), scalar_copies, "factors3")
-        emit(2, 2, (4, 1), scalar_copies, "logs")
-        for block, number in ((6, 0), (7, 5)):
+        emit(0, 2, (1, 2), scalar_copies, "factors3")
+        emit(2, 2, (6, 4), scalar_copies, "logs")
+        for block, number in ((6, 5), (7, 0)):
             late[block] = inputs_of(1, block, number)
         for block in (4, 5):
             finish(1, block, late[block], block_of(tail, block - 4))
         tail = held([P, PACK, QUARTER], F32, "factors2")
         scale_group(tail, 6 * BLOCK, BLOCK, 0)
         quantise_h(1, 4, 2)
-        emit(4, 2, (2, 6), scalar_copies, "raw00")
+        emit(4, 2, (1, 2), scalar_copies, "raw00")
         finish(1, 6, late[6], block_of(tail, 0))
         scale_group(tail, 7 * BLOCK, BLOCK, BLOCK)
         quantise_h(1, 6, 1)
-        emit(6, 1, (3,), scalar_copies, "wo_raw")
+        emit(6, 1, (3,), scalar_copies, "early_factors")
         finish(1, 7, late[7], block_of(tail, 1))
         quantise_h(1, 7, 1)
-        emit(7, 1, (7, 4, 1, 0), (nc.scalar.copy, nc.vector.tensor_copy) * 2, "rounded_wide", 2)
+        emit(7, 1, (7, 6, 4, 5), (nc.scalar.copy, nc.vector.tensor_copy) * 2, "rounded_wide", 2)

@@ -34,7 +34,7 @@ QUARTER = 256
 BLOCK = 128
 FLOOR = 1e-12
 STRIP = 64
-LEAD = 2
+LEAD = 4
 SHIFT = 3
 
 
@@ -66,6 +66,9 @@ def tile_list_softplus_step_input_kernel(
         nc.vector.memset(wb_planes[:].rearrange("p a c -> p (a c)").bitcast(I32), 0)
         nc.vector.memset(moved_plane[:].bitcast(I32), 0)
 
+        warm = held([P, 2], F32, "warm")
+        nc.vector.memset(warm[:, 0:1], 0.0)
+        nc.scalar.activation(warm[:, 1:2], warm[:, 0:1], SIGMOID)
         identity = held([P, P], F32, "identity")
         make_identity(nc, identity[:])
 
@@ -109,8 +112,8 @@ def tile_list_softplus_step_input_kernel(
         picked_planes = held([P, S], U8, "picked_planes")
         nc.vector.tensor_copy(picked_planes[:], tab_planes[:].indirect(offsets[:]))
 
-        load_wa(1, 0)
         load_factors(0, "factors0")
+        load_wa(1, 0)
         load_wa(1, 1)
         for r in range(ROWS):
             nc.sync.dma_start(
@@ -123,7 +126,10 @@ def tile_list_softplus_step_input_kernel(
             wb_raw[b] = held([P, 2, H // 4], I32, slot)
             nc.sync.dma_start(wb_raw[b][:], wb_words.rearrange("a p (b w) -> b p a w", b=2)[b].bitcast(I32))
 
-        load_wb(0, "wb_early_raw")
+        early_words = []
+        for a, slot in enumerate(("rounded_aside", "steps")):
+            early_words.append(held([P, H // 4], I32, slot))
+            nc.sync.dma_start(early_words[a][:], wb_words[a, :, :H].bitcast(I32))
         load_factors(1, "factors1")
         load_wb(1, "wb_raw")
         for r in range(ROWS):
@@ -143,35 +149,38 @@ def tile_list_softplus_step_input_kernel(
             return codes, plane
 
         def round_wa(b, a, first, count, copy, slot):
-            rounded = held([P, count * PASS], BF16, slot)
-            dealt = rounded[:].rearrange("p (t m e j) -> p m t j e", t=count, e=RUN, j=PACK)
+            rounded = held([P, count * PASS], BF16, slot)[:] if isinstance(slot, str) else slot
+            dealt = rounded.rearrange("p (t m e j) -> p m t j e", t=count, e=RUN, j=PACK)
             source = wa_raw[b, a][:].rearrange("p j (m t e) -> p m t j e", t=PACK, e=RUN)
             copy(dealt, source[:, :, first : first + count])
-            return rounded[:]
+            return rounded
 
         def quantise_wa(b, a, first, rounded, slot=None):
             codes, plane = quantise(rounded, "wa%d%d%d" % (b, a, first), slot)
-            wa_moving[b, a] = (codes, plane)
+            wa_moving[b, a, first] = (codes, plane)
             for t in range(rounded.shape[1] // PASS):
                 cols = slice(t * P, (t + 1) * P)
                 wa_quantised[PACK * b + first + t, a] = (codes[:, cols], plane[:, cols])
 
         nc.vector.tensor_copy(picked[0][:], table[0][:].bitcast(U32).indirect(offsets[:]))
-        quantise_wa(0, 0, 0, round_wa(0, 0, 0, PACK, nc.scalar.copy, "rounded_wide"))
-        scalar_share = round_wa(0, 1, 0, 2, nc.scalar.copy, "rounded_narrow")
-        vector_share = round_wa(0, 1, 2, 2, nc.vector.tensor_copy, "rounded_wide")
-        quantise_wa(0, 1, 0, scalar_share)
-        quantise_wa(0, 1, 2, vector_share)
-        for first, count in ((0, QUARTER), (QUARTER, QUARTER), (HALF, HALF)):
+        for first, slot in ((0, "rounded_first"), (2, "rounded_wide")):
+            quantise_wa(0, 0, first, round_wa(0, 0, first, 2, nc.scalar.copy, slot))
+        early_pair = round_wa(0, 1, 0, 2, nc.scalar.copy, "rounded_narrow")
+        late_pair = held([P, 2 * PASS], BF16, "rounded_late")[:]
+        round_wa(0, 1, 2, 1, nc.scalar.copy, late_pair[:, :PASS])
+        round_wa(0, 1, 3, 1, nc.vector.tensor_copy, late_pair[:, PASS:])
+        quantise_wa(0, 1, 0, early_pair)
+        quantise_wa(0, 1, 2, late_pair)
+        for first in range(0, S, QUARTER):
             nc.vector.tensor_copy(
-                picked[1][:, first : first + count],
-                table[1][:].bitcast(U32).indirect(list_part(first, count)),
+                picked[1][:, first : first + QUARTER],
+                table[1][:].bitcast(U32).indirect(list_part(first, QUARTER)),
             )
 
-        quantise_wa(1, 0, 0, round_wa(1, 0, 0, PACK, nc.vector.tensor_copy, "rounded_wide"))
         early_factors = held([P, S], F32, "early_factors")
         nc.vector.tensor_copy(early_factors[:], factors[0][:].indirect(offsets[:]))
-        last_rounded = round_wa(1, 1, 0, PACK, nc.vector.tensor_copy, "steps")
+        quantise_wa(1, 0, 0, round_wa(1, 0, 0, PACK, nc.vector.tensor_copy, "rounded_wide"))
+        quantise_wa(1, 1, 0, round_wa(1, 1, 0, 2, nc.vector.tensor_copy, "rounded_narrow"))
 
         wo_raw = []
 
@@ -183,23 +192,23 @@ def tile_list_softplus_step_input_kernel(
         for s in (2, 3):
             load_factors(s, "factors%d" % s)
         load_wo(0, "raw00")
-        load_factors(4, "factors0")
+        load_factors(6, "factors0")
         load_wo(1, "wo_raw")
-        for s, slot in zip(range(5, 8), ("raw01", "raw10", "raw11")):
+        for s, slot in zip((7, 4, 5), ("raw01", "raw10", "factors4")):
             load_factors(s, slot)
 
         wb_codes = {}
         wb_dealt_planes = {}
 
-        def deal_wb(b, copy, dtype, slot):
+        def deal_planes(b, copy, dtype):
             wb_dealt_planes[b] = held([P, 2, PACK, P // RUN], dtype, "wb_dealt_planes%d" % b)
             rows = wb_planes[:].bitcast(dtype).rearrange("p a (b q i t) -> p b a q t i", b=2, i=LINE, t=PACK)
             copy(wb_dealt_planes[b][:].rearrange("p a t (q i) -> p a q t i", i=LINE), rows[:, b])
-            wb_codes[b] = held([P, 2, PACK, P // RUN, 2], dtype, slot)
-            copy(wb_codes[b][:], wb_raw[b][:].bitcast(dtype).rearrange("p a (m t w) -> p a t m w", t=PACK, w=2))
 
-        deal_wb(0, nc.vector.tensor_copy, I32, "wb_codes")
-        quantise_wa(1, 1, 0, last_rounded, "wb_early_raw")
+        deal_planes(0, nc.vector.tensor_copy, I32)
+        wb_codes[0] = held([P, 2, PACK, P // RUN, 2], I32, "wb_codes")
+        for a in range(2):
+            nc.vector.tensor_copy(wb_codes[0][:, a], early_words[a][:].rearrange("p (m t w) -> p t m w", t=PACK, w=2))
 
         def sums(unit, number, passes=(0, 1), bank=None):
             s, slices, first, count = unit
@@ -222,16 +231,17 @@ def tile_list_softplus_step_input_kernel(
         def turned_sums(block, number):
             cols = slice(block * BLOCK, (block + 1) * BLOCK)
             bank = bank_tile(number, [P, PASS])
-            for a in range(2):
-                codes, plane = wa_moving[1, a]
+            parts = ((0, 0), (1, 0), (1, 2))
+            for a, first in parts:
+                codes, plane = wa_moving[1, a, first]
                 nc.tensor.matmul_mx(
-                    out=bank[:],
+                    out=bank[:, first * P : first * P + codes.shape[1]],
                     lhsT=picked[a][:, cols].bitcast(E4M3),
                     lhsT_scale=picked_planes[ROWS * a : P, cols],
                     rhs=codes[:].bitcast(E4M3),
                     rhs_scale=plane[:],
-                    start=(a == 0),
-                    stop=(a == 1),
+                    start=(a, first) == parts[0],
+                    stop=(a, first) == parts[-1],
                 )
             return bank
 
@@ -307,8 +317,8 @@ def tile_list_softplus_step_input_kernel(
             (2, 2, 0, QUARTER),
             (0, 2, QUARTER, QUARTER),
             (2, 2, QUARTER, QUARTER),
-            (0, 1, HALF, HALF),
-            (1, 1, HALF, HALF),
+            (0, 2, HALF, QUARTER),
+            (0, 2, HALF + QUARTER, QUARTER),
             (3, 1, HALF, HALF),
             (2, 1, HALF, HALF),
         )
@@ -316,7 +326,7 @@ def tile_list_softplus_step_input_kernel(
         for n in range(LEAD):
             sums(first_units[n], n, ((1, 1),), banks[n])
         banks += [sums(first_units[n], n, (1, 0)) for n in range(LEAD, 8)]
-        order = (0, 2, 4, 1, 3, 5, 6)
+        order = (0, 2, 4, 5, 1, 3, 6)
         area = held([P, len(first_units) + SHIFT, HALF + STRIP], F32, "logs")
         views = [bank[:] for bank in banks[:-1]] + [in_strips(banks[-1], STRIP)]
 
@@ -325,71 +335,96 @@ def tile_list_softplus_step_input_kernel(
             return [rows[n] for n in range(len(order))] + [area[:, first : first + HALF // STRIP, HALF:]]
 
         places = places_from(0)
-        for place, view in zip(places_from(SHIFT), views):
+        gate_places = places_from(SHIFT)
+        gate_places[order[-1]] = held([P, 1, HALF], F32, "last_gates")[:]
+        for place, view in zip(gate_places, views):
             sigmoid(place, view)
         for k in range(5):
             logarithm(area[:, k, :], area[:, SHIFT + k, :])
         logarithm(area[:, 5:8, HALF:], area[:, SHIFT + 5 :, HALF:])
-        for k in (5, 6):
-            logarithm(area[:, k, :HALF], area[:, SHIFT + k, :HALF])
+        for n in order[5:]:
+            logarithm(places[n], gate_places[n])
 
+        aside_rounded = held([P, 2, PASS], BF16, "rounded_aside")
+        for t in range(2):
+            nc.gpsimd.tensor_scalar(
+                aside_rounded[:, t, :].rearrange("p (m e j) -> p m j e", e=RUN, j=PACK),
+                wa_raw[1, 1][:].rearrange("p j (m t e) -> p t m j e", t=PACK, e=RUN)[:, 2 + t],
+                1.0,
+                0.0,
+                MULT,
+                ADD,
+            )
         steps = held([P, PACK, S], F32, "steps")
-        scaled = held([P, PACK, S], F32, "scaled")
+        scaled = held([P, PACK, S], F32, "raw11")
         targets = [steps[:, s : s + slices, first : first + count] for s, slices, first, count in first_units]
         targets[-1] = shaped(targets[-1][:, 0, :], places[-1])
-        for n in (0, 2, 4, 1, 3, 7, 5, 6):
+        for n in (0, 2, 4, 5, 1, 7, 3, 6):
             guard(targets[n], places[n], views[n])
         for half in (slice(0, HALF), slice(HALF, S)):
             nc.gpsimd.tensor_tensor(scaled[:, 0, half], steps[:, 0, half], early_factors[:, half], MULT)
+        quantise_wa(1, 1, 2, aside_rounded[:].rearrange("p t c -> p (t c)"), "last_gates")
         for s, first, count in ((1, 0, S), (2, 0, S), (3, 0, HALF), (3, HALF, HALF)):
             cols = slice(first, first + count)
             scale_steps(scaled[:, s, cols], steps[:, s, cols], s, first, count)
 
-        units = ((6, 2, 0, QUARTER), (4, 2, 0, QUARTER), (4, 2, QUARTER, QUARTER), (6, 2, QUARTER, QUARTER))
-        numbers = (3, 7, 0, 5)
-        late_gates = held([P, PACK, HALF], F32, "late_gates")
-        wide = HALF + QUARTER
-        gates = held([P, 5 * HALF], F32, "logs")
-        logs = held([P, 2 * wide], F32, "early_logs")
+        units = ((4, 2, 0, QUARTER), (6, 2, 0, QUARTER), (6, 2, QUARTER, QUARTER), (4, 2, QUARTER, QUARTER))
+        numbers = (0, 4, 5, 2)
+        gates = held([P, 3, HALF], F32, "gates")
+        late_gates = held([P, 3, HALF], F32, "late_gates")
+        logs = held([P, 6, HALF], F32, "late_logs")
+        gate_rows = (gates[:, 0, :], gates[:, 2, :], logs[:, 3, :], logs[:, 5, :])
+        log_places = (logs[:, 0, :], logs[:, 2, :], gates[:, 0, :], gates[:, 2, :])
+        turned_gates = [late_gates[:, k, :] for k in range(3)] + [gates[:, 1, :]]
+        turned_logs = [logs[:, 3 + k, :] for k in range(3)] + [logs[:, 1, :]]
 
-        def pair(area, column):
-            return area[:, column : column + HALF].rearrange("p (s n) -> p s n", s=2)
+        def pair(row):
+            return row.rearrange("p (s n) -> p s n", s=2)
 
-        def strips(area):
-            return area[:, 0 : 2 * wide].rearrange("p (s n) -> p s n", s=2)[:, :, 0:QUARTER]
-
-        gate_places = (pair(gates, QUARTER), pair(gates, wide + QUARTER), strips(gates), pair(gates, 2 * wide))
-        log_places = (pair(logs, QUARTER), pair(logs, wide + QUARTER), strips(logs), pair(gates, 0))
-        for k, number in enumerate((0, 2, 4, 1)):
-            nc.scalar.activation(late_gates[:, k, :], turned_sums(PACK + k, number)[:], SIGMOID)
         banks = {}
-        woven = []
-        for n, number in zip((0, 1, 3), (0, 2, 4)):
-            banks[n] = sums(units[n], numbers[n])
-            sigmoid(gate_places[n], banks[n][:])
-            woven.append(weave(inputs_of(0, 5 + len(woven), number), "woven%d" % len(woven)))
-        deal_wb(1, nc.scalar.copy, U32, "wb_late_codes")
-        banks[2] = sums(units[2], numbers[2])
-        sigmoid(gate_places[2], banks[2][:])
-        for k in range(2):
-            logarithm(logs[:, k * wide : (k + 1) * wide], gates[:, k * wide : (k + 1) * wide])
-        logarithm(log_places[3], gate_places[3])
-        late_logs = gates[:, HALF:]
-        logarithm(late_logs, late_gates[:].rearrange("p s n -> p (s n)"))
 
-        own = [inputs_of(0, block, number) for block, number in enumerate((6, 1, 2, 4))]
+        def held_sums(n):
+            banks[n] = sums(units[n], numbers[n])
+            sigmoid(pair(gate_rows[n]), banks[n][:])
+
+        def passing_sums(k, number):
+            nc.scalar.activation(turned_gates[k], turned_sums(PACK + k, number)[:], SIGMOID)
+
+        held_sums(0)
+        held_sums(3)
+        woven = []
+        for k, (copied, passing) in enumerate(((4, 7), (5, 3), (1, 6))):
+            woven.append(weave(inputs_of(0, 5 + k, copied), "woven%d" % k))
+            passing_sums(k, passing)
+        held_sums(1)
+        held_sums(2)
+        deal_planes(1, nc.scalar.copy, U32)
+        wb_codes[1] = held([P, 2, PACK, P // RUN, 2], U32, "wb_late_codes")
+        nc.scalar.copy(wb_codes[1][:], wb_raw[1][:].bitcast(U32).rearrange("p a (m t w) -> p a t m w", t=PACK, w=2))
+        passing_sums(3, 1)
+        gate_run = gates[:].rearrange("p r n -> p (r n)")
+        log_run = logs[:, 0:3, :].rearrange("p r n -> p (r n)")
+        for span in (slice(0, HALF + STRIP), slice(2 * HALF - STRIP, 3 * HALF)):
+            logarithm(log_run[:, span], gate_run[:, span])
+        for n in (2, 3):
+            logarithm(log_places[n], gate_rows[n])
+        middle = slice(HALF + STRIP, 2 * HALF - STRIP)
+        logarithm(log_run[:, middle], gate_run[:, middle])
+        logarithm(logs[:, 3:, :], late_gates[:])
+
+        own = [inputs_of(0, block, number) for block, number in enumerate((7, 3, 6, 1))]
         for n in range(3):
             finish_aside(0, 5 + n, woven[n], block_of(scaled, 5 + n))
         finish(0, 0, own[0], block_of(scaled, 0))
-        own.append(inputs_of(0, 4, 6))
+        own.append(inputs_of(0, 4, 7))
         for block in range(1, 5):
             finish(0, block, own[block], block_of(scaled, block))
         steps = held([P, PACK, HALF], F32, "steps")
         for n, (s, slices, first, count) in enumerate(units):
-            guard(steps[:, s - PACK : s - PACK + slices, first : first + count], log_places[n], banks[n][:])
+            guard(steps[:, s - PACK : s - PACK + slices, first : first + count], pair(log_places[n]), banks[n][:])
 
-        woven = weave(inputs_of(1, 3, 4), "woven0")
-        late_steps = held([P, PACK, HALF], F32, "factors1")
+        woven = weave(inputs_of(1, 3, 1), "woven0")
+        late_steps = [held([P, PACK, QUARTER], F32, slot) for slot in ("factors1", "last_steps")]
 
         def add_turned(bank, term, opens):
             for t in range(PACK):
@@ -405,36 +440,36 @@ def tile_list_softplus_step_input_kernel(
         def steps_aside(first, slot, numbers):
             negated = held([P, 2, PASS], F32, slot)
             for n in range(2):
-                nc.scalar.activation(negated[:, n, :], turned_sums(PACK + first + n, 1 + n)[:], COPY, scale=-1.0)
+                nc.scalar.activation(negated[:, n, :], turned_sums(PACK + first + n, (3, 6)[n])[:], COPY, scale=-1.0)
             for n, number in enumerate(numbers):
                 k = first + n
                 bank = bank_tile(number, [P, PACK, BLOCK])
-                add_turned(bank, late_logs[:, k * PASS : (k + 1) * PASS], True)
+                add_turned(bank, turned_logs[k], True)
                 add_turned(bank, negated[:, n, :], False)
-                nc.scalar.activation(block_of(late_steps, k), bank[:], RELU, scale=-1.0)
+                nc.scalar.activation(block_of(late_steps[first // 2], n), bank[:], RELU, scale=-1.0)
 
-        steps_aside(0, "factors2", (3, 7))
-        late = {block: inputs_of(1, block, number) for block, number in enumerate((6, 4, 0))}
+        steps_aside(0, "factors2", (0, 4))
+        late = {block: inputs_of(1, block, number) for block, number in enumerate((7, 1, 5))}
         wo_rounded = held([P, 2, N, PACK], BF16, "factors2")
         for b in range(2):
             nc.scalar.copy(
                 wo_rounded[:, b].rearrange("p (c i) t -> p c t i", i=LINE),
                 wo_raw[b][:].rearrange("p t (c i) -> p c t i", i=LINE),
             )
-        for block, number in ((4, 3), (5, 7)):
+        for block, number in ((4, 0), (5, 4)):
             late[block] = inputs_of(1, block, number)
 
-        scaled = held([P, PACK, HALF], F32, "scaled")
-        scale_steps(scaled[:, 0, :], steps[:, 0, :], 4, 0, HALF)
-        quantise_h(0, 0, 8, "early_logs")
-        for k, first, count in ((1, 0, HALF), (2, 0, HALF), (3, 0, QUARTER), (3, QUARTER, QUARTER)):
+        scaled = held([P, PACK, HALF], F32, "raw11")
+        scale_steps(scaled[:, 2, :], steps[:, 2, :], 6, 0, HALF)
+        quantise_h(0, 0, 8, "gates")
+        for k, first, count in ((3, 0, HALF), (0, 0, HALF), (1, 0, QUARTER), (1, QUARTER, QUARTER)):
             cols = slice(first, first + count)
             scale_steps(scaled[:, k, cols], steps[:, k, cols], PACK + k, first, count)
         finish_aside(1, 3, woven, block_of(scaled, 3))
         for block in range(3):
             finish(1, block, late[block], block_of(scaled, block))
 
-        steps_aside(2, "wo_raw", (6, 4))
+        steps_aside(2, "wo_raw", (7, 1))
 
         def project(target, c, b, first, count, start, stop):
             rows = slice(b * N + c * P, b * N + (c + 1) * P)
@@ -468,31 +503,31 @@ def tile_list_softplus_step_input_kernel(
                     rows = slice((n + 1 - banks_a_store) * share, (n + 1) * share)
                     nc.sync.dma_start(out_rows[:, rows, cols], result[:, rows, :])
 
-        tail = held([P, PACK, QUARTER], F32, "scaled")
+        tail = held([P, PACK, QUARTER], F32, "raw11")
 
         def scale_group(tail, first, count, column):
             for k in range(PACK):
-                part = late_steps[:, k, first - HALF : first - HALF + count]
+                part = late_steps[(first - HALF) // QUARTER][:, k, first % QUARTER : first % QUARTER + count]
                 scale_steps(tail[:, k, column : column + count], part, PACK + k, first, count)
 
         scalar_copies = (nc.scalar.copy, nc.scalar.copy)
         scale_group(tail, HALF, QUARTER, 0)
-        wo_codes, wo_plane = quantise(wo_rounded[:].rearrange("p b n t -> p (b n t)"), "wo", "woven0")
+        wo_codes, wo_plane = quantise(wo_rounded[:].rearrange("p b n t -> p (b n t)"), "wo", "factors1")
         quantise_h(1, 0, 4)
-        emit(0, 2, (1, 2), scalar_copies, "factors3")
-        emit(2, 2, (6, 4), scalar_copies, "logs")
-        for block, number in ((6, 5), (7, 0)):
+        emit(0, 2, (3, 6), scalar_copies, "factors3")
+        emit(2, 2, (7, 1), scalar_copies, "logs")
+        for block, number in ((6, 2), (7, 5)):
             late[block] = inputs_of(1, block, number)
         for block in (4, 5):
             finish(1, block, late[block], block_of(tail, block - 4))
         tail = held([P, PACK, QUARTER], F32, "factors2")
         scale_group(tail, 6 * BLOCK, BLOCK, 0)
         quantise_h(1, 4, 2)
-        emit(4, 2, (1, 2), scalar_copies, "raw00")
+        emit(4, 2, (3, 6), scalar_copies, "raw00")
         finish(1, 6, late[6], block_of(tail, 0))
         scale_group(tail, 7 * BLOCK, BLOCK, BLOCK)
         quantise_h(1, 6, 1)
-        emit(6, 1, (3,), scalar_copies, "early_factors")
+        emit(6, 1, (0,), scalar_copies, "early_factors")
         finish(1, 7, late[7], block_of(tail, 1))
         quantise_h(1, 7, 1)
-        emit(7, 1, (7, 6, 4, 5), (nc.scalar.copy, nc.vector.tensor_copy) * 2, "rounded_wide", 2)
+        emit(7, 1, (4, 7, 1, 2), (nc.scalar.copy, nc.vector.tensor_copy) * 2, "rounded_wide", 2)

@@ -171,10 +171,11 @@ def tile_list_softplus_step_input_kernel(
         round_wa(0, 1, 3, 1, nc.vector.tensor_copy, late_pair[:, PASS:])
         quantise_wa(0, 1, 0, early_pair)
         quantise_wa(0, 1, 2, late_pair)
-        for first in range(0, S, QUARTER):
+        pieces = [(0, BLOCK), (BLOCK, BLOCK)] + [(first, QUARTER) for first in range(QUARTER, S, QUARTER)]
+        for first, count in pieces:
             nc.vector.tensor_copy(
-                picked[1][:, first : first + QUARTER],
-                table[1][:].bitcast(U32).indirect(list_part(first, QUARTER)),
+                picked[1][:, first : first + count],
+                table[1][:].bitcast(U32).indirect(list_part(first, count)),
             )
 
         early_factors = held([P, S], F32, "early_factors")
@@ -313,8 +314,8 @@ def tile_list_softplus_step_input_kernel(
             return view[:, :, block * BLOCK : (block + 1) * BLOCK]
 
         first_units = (
-            (0, 2, 0, QUARTER),
-            (2, 2, 0, QUARTER),
+            (0, 4, 0, BLOCK),
+            (0, 4, BLOCK, BLOCK),
             (0, 2, QUARTER, QUARTER),
             (2, 2, QUARTER, QUARTER),
             (0, 2, HALF, QUARTER),
@@ -322,11 +323,12 @@ def tile_list_softplus_step_input_kernel(
             (3, 1, HALF, HALF),
             (2, 1, HALF, HALF),
         )
-        banks = [sums(first_units[n], n, ((0, 0),)) for n in range(LEAD)]
+        numbers = (0, 2, 4, 3, 5, 1, 6, 7)
+        banks = [sums(first_units[n], numbers[n], ((0, 0),)) for n in range(LEAD)]
         for n in range(LEAD):
-            sums(first_units[n], n, ((1, 1),), banks[n])
-        banks += [sums(first_units[n], n, (1, 0)) for n in range(LEAD, 8)]
-        order = (0, 2, 4, 5, 1, 3, 6)
+            sums(first_units[n], numbers[n], ((1, 1),), banks[n])
+        banks += [sums(first_units[n], numbers[n], (1, 0)) for n in range(LEAD, 8)]
+        order = (0, 1, 2, 4, 5, 3, 6)
         area = held([P, len(first_units) + SHIFT, HALF + STRIP], F32, "logs")
         views = [bank[:] for bank in banks[:-1]] + [in_strips(banks[-1], STRIP)]
 
@@ -359,7 +361,7 @@ def tile_list_softplus_step_input_kernel(
         scaled = held([P, PACK, S], F32, "raw11")
         targets = [steps[:, s : s + slices, first : first + count] for s, slices, first, count in first_units]
         targets[-1] = shaped(targets[-1][:, 0, :], places[-1])
-        for n in (0, 2, 4, 5, 1, 7, 3, 6):
+        for n in (0, 1, 2, 4, 5, 7, 3, 6):
             guard(targets[n], places[n], views[n])
         for half in (slice(0, HALF), slice(HALF, S)):
             nc.gpsimd.tensor_tensor(scaled[:, 0, half], steps[:, 0, half], early_factors[:, half], MULT)
@@ -394,7 +396,7 @@ def tile_list_softplus_step_input_kernel(
         held_sums(3)
         woven = []
         for k, (copied, passing) in enumerate(((4, 7), (5, 3), (1, 6))):
-            woven.append(weave(inputs_of(0, 5 + k, copied), "woven%d" % k))
+            woven.append(weave(inputs_of(0, k, copied), "woven%d" % k))
             passing_sums(k, passing)
         held_sums(1)
         held_sums(2)
@@ -412,18 +414,18 @@ def tile_list_softplus_step_input_kernel(
         logarithm(log_run[:, middle], gate_run[:, middle])
         logarithm(logs[:, 3:, :], late_gates[:])
 
-        own = [inputs_of(0, block, number) for block, number in enumerate((7, 3, 6, 1))]
-        for n in range(3):
-            finish_aside(0, 5 + n, woven[n], block_of(scaled, 5 + n))
-        finish(0, 0, own[0], block_of(scaled, 0))
-        own.append(inputs_of(0, 4, 7))
-        for block in range(1, 5):
+        own = {3 + n: inputs_of(0, 3 + n, number) for n, number in enumerate((7, 3, 6, 1))}
+        for block in range(3):
+            finish_aside(0, block, woven[block], block_of(scaled, block))
+        finish(0, 3, own[3], block_of(scaled, 3))
+        own[7] = inputs_of(0, 7, 7)
+        for block in range(4, 8):
             finish(0, block, own[block], block_of(scaled, block))
         steps = held([P, PACK, HALF], F32, "steps")
         for n, (s, slices, first, count) in enumerate(units):
             guard(steps[:, s - PACK : s - PACK + slices, first : first + count], pair(log_places[n]), banks[n][:])
 
-        woven = weave(inputs_of(1, 3, 1), "woven0")
+        woven = weave(inputs_of(1, 0, 1), "woven0")
         late_steps = [held([P, PACK, QUARTER], F32, slot) for slot in ("factors1", "last_steps")]
 
         def add_turned(bank, term, opens):
@@ -449,7 +451,7 @@ def tile_list_softplus_step_input_kernel(
                 nc.scalar.activation(block_of(late_steps[first // 2], n), bank[:], RELU, scale=-1.0)
 
         steps_aside(0, "factors2", (0, 4))
-        late = {block: inputs_of(1, block, number) for block, number in enumerate((7, 1, 5))}
+        late = {1 + n: inputs_of(1, 1 + n, number) for n, number in enumerate((7, 1, 5))}
         wo_rounded = held([P, 2, N, PACK], BF16, "factors2")
         for b in range(2):
             nc.scalar.copy(
@@ -465,8 +467,8 @@ def tile_list_softplus_step_input_kernel(
         for k, first, count in ((3, 0, HALF), (0, 0, HALF), (1, 0, QUARTER), (1, QUARTER, QUARTER)):
             cols = slice(first, first + count)
             scale_steps(scaled[:, k, cols], steps[:, k, cols], PACK + k, first, count)
-        finish_aside(1, 3, woven, block_of(scaled, 3))
-        for block in range(3):
+        finish_aside(1, 0, woven, block_of(scaled, 0))
+        for block in range(1, 4):
             finish(1, block, late[block], block_of(scaled, block))
 
         steps_aside(2, "wo_raw", (7, 1))

@@ -181,7 +181,7 @@ def tile_list_softplus_step_input_kernel(
         early_factors = held([P, S], F32, "early_factors")
         nc.vector.tensor_copy(early_factors[:], factors[0][:].indirect(offsets[:]))
         quantise_wa(1, 0, 0, round_wa(1, 0, 0, PACK, nc.vector.tensor_copy, "rounded_wide"))
-        quantise_wa(1, 1, 0, round_wa(1, 1, 0, 2, nc.vector.tensor_copy, "rounded_narrow"))
+        quantise_wa(1, 1, 0, round_wa(1, 1, 0, 1, nc.vector.tensor_copy, "rounded_narrow"))
 
         wo_raw = []
 
@@ -201,12 +201,12 @@ def tile_list_softplus_step_input_kernel(
         wb_codes = {}
         wb_dealt_planes = {}
 
-        def deal_planes(b, copy, dtype):
-            wb_dealt_planes[b] = held([P, 2, PACK, P // RUN], dtype, "wb_dealt_planes%d" % b)
+        def deal_planes(b, copy, dtype, place):
+            wb_dealt_planes[b] = place.rearrange("p (a t m) -> p a t m", a=2, t=PACK)
             rows = wb_planes[:].bitcast(dtype).rearrange("p a (b q i t) -> p b a q t i", b=2, i=LINE, t=PACK)
-            copy(wb_dealt_planes[b][:].rearrange("p a t (q i) -> p a q t i", i=LINE), rows[:, b])
+            copy(wb_dealt_planes[b].rearrange("p a t (q i) -> p a q t i", i=LINE), rows[:, b])
 
-        deal_planes(0, nc.vector.tensor_copy, I32)
+        deal_planes(0, nc.vector.tensor_copy, I32, held([P, H // 4], I32, "wb_dealt_planes")[:])
         wb_codes[0] = held([P, 2, PACK, P // RUN, 2], I32, "wb_codes")
         for a in range(2):
             nc.vector.tensor_copy(wb_codes[0][:, a], early_words[a][:].rearrange("p (m t w) -> p t m w", t=PACK, w=2))
@@ -232,17 +232,19 @@ def tile_list_softplus_step_input_kernel(
         def turned_sums(block, number):
             cols = slice(block * BLOCK, (block + 1) * BLOCK)
             bank = bank_tile(number, [P, PASS])
-            parts = ((0, 0), (1, 0), (1, 2))
-            for a, first in parts:
+            parts = ((0, 0, 0, PACK), (1, 0, 0, 1), (1, 1, 0, 1), (1, 1, 1, 2))
+            for part in parts:
+                a, first, skipped, slices = part
                 codes, plane = wa_moving[1, a, first]
+                window = slice(skipped * P, (skipped + slices) * P)
                 nc.tensor.matmul_mx(
-                    out=bank[:, first * P : first * P + codes.shape[1]],
+                    out=bank[:, (first + skipped) * P : (first + skipped + slices) * P],
                     lhsT=picked[a][:, cols].bitcast(E4M3),
                     lhsT_scale=picked_planes[ROWS * a : P, cols],
-                    rhs=codes[:].bitcast(E4M3),
-                    rhs_scale=plane[:],
-                    start=(a, first) == parts[0],
-                    stop=(a, first) == parts[-1],
+                    rhs=codes[:, window].bitcast(E4M3),
+                    rhs_scale=plane[:, window],
+                    start=part == parts[0],
+                    stop=part == parts[-1],
                 )
             return bank
 
@@ -347,11 +349,11 @@ def tile_list_softplus_step_input_kernel(
         for n in order[5:]:
             logarithm(places[n], gate_places[n])
 
-        aside_rounded = held([P, 2, PASS], BF16, "rounded_aside")
-        for t in range(2):
+        aside_rounded = held([P, 3, PASS], BF16, "rounded_aside")
+        for t in range(3):
             nc.gpsimd.tensor_scalar(
                 aside_rounded[:, t, :].rearrange("p (m e j) -> p m j e", e=RUN, j=PACK),
-                wa_raw[1, 1][:].rearrange("p j (m t e) -> p t m j e", t=PACK, e=RUN)[:, 2 + t],
+                wa_raw[1, 1][:].rearrange("p j (m t e) -> p t m j e", t=PACK, e=RUN)[:, 1 + t],
                 1.0,
                 0.0,
                 MULT,
@@ -365,23 +367,23 @@ def tile_list_softplus_step_input_kernel(
             guard(targets[n], places[n], views[n])
         for half in (slice(0, HALF), slice(HALF, S)):
             nc.gpsimd.tensor_tensor(scaled[:, 0, half], steps[:, 0, half], early_factors[:, half], MULT)
-        quantise_wa(1, 1, 2, aside_rounded[:].rearrange("p t c -> p (t c)"), "last_gates")
+        quantise_wa(1, 1, 1, aside_rounded[:].rearrange("p t c -> p (t c)"), "last_gates")
         for s, first, count in ((1, 0, S), (2, 0, S), (3, 0, HALF), (3, HALF, HALF)):
             cols = slice(first, first + count)
             scale_steps(scaled[:, s, cols], steps[:, s, cols], s, first, count)
 
-        units = ((4, 2, 0, QUARTER), (6, 2, 0, QUARTER), (6, 2, QUARTER, QUARTER), (4, 2, QUARTER, QUARTER))
+        units = [(s, 1, 0, HALF) for s in (4, 6, 7, 5)]
         numbers = (0, 4, 5, 2)
         gates = held([P, 3, HALF], F32, "gates")
         late_gates = held([P, 3, HALF], F32, "late_gates")
         logs = held([P, 6, HALF], F32, "late_logs")
-        gate_rows = (gates[:, 0, :], gates[:, 2, :], logs[:, 3, :], logs[:, 5, :])
+        gate_rows = (gates[:, 0, :], gates[:, 2, :], logs[:, 3, :], held([P, HALF], F32, "last_row")[:])
         log_places = (logs[:, 0, :], logs[:, 2, :], gates[:, 0, :], gates[:, 2, :])
         turned_gates = [late_gates[:, k, :] for k in range(3)] + [gates[:, 1, :]]
         turned_logs = [logs[:, 3 + k, :] for k in range(3)] + [logs[:, 1, :]]
 
         def pair(row):
-            return row.rearrange("p (s n) -> p s n", s=2)
+            return row.rearrange("p (s n) -> p s n", s=1)
 
         banks = {}
 
@@ -393,16 +395,14 @@ def tile_list_softplus_step_input_kernel(
             nc.scalar.activation(turned_gates[k], turned_sums(PACK + k, number)[:], SIGMOID)
 
         held_sums(0)
+        woven = [weave(inputs_of(0, 0, 4), "woven0")]
         held_sums(3)
-        woven = []
-        for k, (copied, passing) in enumerate(((4, 7), (5, 3), (1, 6))):
+        passing_sums(0, 7)
+        for k, (copied, passing) in enumerate(((5, 3), (1, 6)), 1):
             woven.append(weave(inputs_of(0, k, copied), "woven%d" % k))
             passing_sums(k, passing)
         held_sums(1)
         held_sums(2)
-        deal_planes(1, nc.scalar.copy, U32)
-        wb_codes[1] = held([P, 2, PACK, P // RUN, 2], U32, "wb_late_codes")
-        nc.scalar.copy(wb_codes[1][:], wb_raw[1][:].bitcast(U32).rearrange("p a (m t w) -> p a t m w", t=PACK, w=2))
         passing_sums(3, 1)
         gate_run = gates[:].rearrange("p r n -> p (r n)")
         log_run = logs[:, 0:3, :].rearrange("p r n -> p (r n)")
@@ -410,6 +410,10 @@ def tile_list_softplus_step_input_kernel(
             logarithm(log_run[:, span], gate_run[:, span])
         for n in (2, 3):
             logarithm(log_places[n], gate_rows[n])
+        late_wb = held([P, 3 * H // 4], U32, "last_row")
+        wb_codes[1] = late_wb[:, : H // 2].rearrange("p (a t m w) -> p a t m w", a=2, t=PACK, w=2)
+        nc.scalar.copy(wb_codes[1], wb_raw[1][:].bitcast(U32).rearrange("p a (m t w) -> p a t m w", t=PACK, w=2))
+        deal_planes(1, nc.scalar.copy, U32, late_wb[:, H // 2 :])
         middle = slice(HALF + STRIP, 2 * HALF - STRIP)
         logarithm(log_run[:, middle], gate_run[:, middle])
         logarithm(logs[:, 3:, :], late_gates[:])
@@ -426,7 +430,7 @@ def tile_list_softplus_step_input_kernel(
             guard(steps[:, s - PACK : s - PACK + slices, first : first + count], pair(log_places[n]), banks[n][:])
 
         woven = weave(inputs_of(1, 0, 1), "woven0")
-        late_steps = [held([P, PACK, QUARTER], F32, slot) for slot in ("factors1", "last_steps")]
+        late_steps = []
 
         def add_turned(bank, term, opens):
             for t in range(PACK):
@@ -439,7 +443,8 @@ def tile_list_softplus_step_input_kernel(
                     stop=not opens and t == PACK - 1,
                 )
 
-        def steps_aside(first, slot, numbers):
+        def steps_aside(first, slot, numbers, steps_slot):
+            late_steps.append(held([P, PACK, QUARTER], F32, steps_slot))
             negated = held([P, 2, PASS], F32, slot)
             for n in range(2):
                 nc.scalar.activation(negated[:, n, :], turned_sums(PACK + first + n, (3, 6)[n])[:], COPY, scale=-1.0)
@@ -450,7 +455,7 @@ def tile_list_softplus_step_input_kernel(
                 add_turned(bank, negated[:, n, :], False)
                 nc.scalar.activation(block_of(late_steps[first // 2], n), bank[:], RELU, scale=-1.0)
 
-        steps_aside(0, "factors2", (0, 4))
+        steps_aside(0, "factors2", (0, 4), "factors1")
         late = {1 + n: inputs_of(1, 1 + n, number) for n, number in enumerate((7, 1, 5))}
         wo_rounded = held([P, 2, N, PACK], BF16, "factors2")
         for b in range(2):
@@ -471,7 +476,7 @@ def tile_list_softplus_step_input_kernel(
         for block in range(1, 4):
             finish(1, block, late[block], block_of(scaled, block))
 
-        steps_aside(2, "wo_raw", (7, 1))
+        steps_aside(2, "last_negated", (7, 1), "wo_raw")
 
         def project(target, c, b, first, count, start, stop):
             rows = slice(b * N + c * P, b * N + (c + 1) * P)

@@ -35,6 +35,7 @@ BLOCK = 128
 FLOOR = 1e-12
 STRIP = 64
 LEAD = 4
+SHARE = 96
 SHIFT = 3
 
 
@@ -285,24 +286,26 @@ def tile_list_softplus_step_input_kernel(
         h_rounded = [held([P, S, PACK], BF16, "table%d" % b) for b in range(2)]
         h_quantised = {}
 
-        def finish(b, block, bank, scaled):
+        def finish(b, block, bank, scaled, first=0):
+            tokens = slice(block * BLOCK + first, (block + 1) * BLOCK)
             nc.vector.tensor_tensor(
-                h_rounded[b][:, block * BLOCK : (block + 1) * BLOCK, :].rearrange("p (c i) t -> p c t i", i=LINE),
-                bank[:].rearrange("p t (c i) -> p c t i", i=LINE),
-                scaled.rearrange("p t (c i) -> p c t i", i=LINE),
+                h_rounded[b][:, tokens, :].rearrange("p (c i) t -> p c t i", i=LINE),
+                bank[:, :, first:].rearrange("p t (c i) -> p c t i", i=LINE),
+                scaled[:, :, first:].rearrange("p t (c i) -> p c t i", i=LINE),
                 MULT,
             )
 
-        def weave(bank, slot):
-            woven = held([P, BLOCK, PACK], F32, slot)
-            nc.scalar.copy(woven[:], bank[:].rearrange("p t n -> p n t"))
+        def weave(bank, slot, count=BLOCK):
+            woven = held([P, PACK, count], F32, slot)
+            nc.scalar.copy(woven[:], bank[:, :, :count])
             return woven
 
         def finish_aside(b, block, woven, scaled):
+            count = woven.shape[2]
             nc.gpsimd.tensor_tensor(
-                h_rounded[b][:, block * BLOCK : (block + 1) * BLOCK, :],
-                woven[:],
-                scaled.rearrange("p t n -> p n t"),
+                h_rounded[b][:, block * BLOCK : block * BLOCK + count, :].rearrange("p (c i) t -> p c t i", i=LINE),
+                woven[:].rearrange("p t (c i) -> p c t i", i=LINE),
+                scaled[:, :, :count].rearrange("p t (c i) -> p c t i", i=LINE),
                 MULT,
             )
 
@@ -402,6 +405,8 @@ def tile_list_softplus_step_input_kernel(
             woven.append(weave(inputs_of(0, k, copied), "woven%d" % k))
             passing_sums(k, passing)
         held_sums(1)
+        own = {3: inputs_of(0, 3, 7)}
+        woven.append(weave(own[3], "woven3", SHARE))
         held_sums(2)
         passing_sums(3, 1)
         gate_run = gates[:].rearrange("p r n -> p (r n)")
@@ -418,10 +423,11 @@ def tile_list_softplus_step_input_kernel(
         logarithm(log_run[:, middle], gate_run[:, middle])
         logarithm(logs[:, 3:, :], late_gates[:])
 
-        own = {3 + n: inputs_of(0, 3 + n, number) for n, number in enumerate((7, 3, 6, 1))}
-        for block in range(3):
+        for block, number in ((4, 3), (5, 6), (6, 1)):
+            own[block] = inputs_of(0, block, number)
+        for block in range(4):
             finish_aside(0, block, woven[block], block_of(scaled, block))
-        finish(0, 3, own[3], block_of(scaled, 3))
+        finish(0, 3, own[3], block_of(scaled, 3), SHARE)
         own[7] = inputs_of(0, 7, 7)
         for block in range(4, 8):
             finish(0, block, own[block], block_of(scaled, block))

@@ -167,9 +167,7 @@ def tile_list_softplus_step_input_kernel(
         for first, slot in ((0, "rounded_first"), (2, "rounded_wide")):
             quantise_wa(0, 0, first, round_wa(0, 0, first, 2, nc.scalar.copy, slot))
         early_pair = round_wa(0, 1, 0, 2, nc.scalar.copy, "rounded_narrow")
-        late_pair = held([P, 2 * PASS], BF16, "rounded_late")[:]
-        round_wa(0, 1, 2, 1, nc.scalar.copy, late_pair[:, :PASS])
-        round_wa(0, 1, 3, 1, nc.vector.tensor_copy, late_pair[:, PASS:])
+        late_pair = round_wa(0, 1, 2, 2, nc.vector.tensor_copy, "rounded_late")
         quantise_wa(0, 1, 0, early_pair)
         quantise_wa(0, 1, 2, late_pair)
         pieces = [(0, BLOCK), (BLOCK, BLOCK)] + [(first, QUARTER) for first in range(QUARTER, S, QUARTER)]
@@ -328,28 +326,29 @@ def tile_list_softplus_step_input_kernel(
             (3, 1, HALF, HALF),
             (2, 1, HALF, HALF),
         )
-        numbers = (0, 2, 4, 3, 5, 1, 6, 7)
+        numbers = (6, 0, 2, 7, 4, 5, 3, 1)
         banks = [sums(first_units[n], numbers[n], ((0, 0),)) for n in range(LEAD)]
         for n in range(LEAD):
             sums(first_units[n], numbers[n], ((1, 1),), banks[n])
         banks += [sums(first_units[n], numbers[n], (1, 0)) for n in range(LEAD, 8)]
         order = (0, 1, 2, 4, 5, 3, 6)
-        area = held([P, len(first_units) + SHIFT, HALF + STRIP], F32, "logs")
-        views = [bank[:] for bank in banks[:-1]] + [in_strips(banks[-1], STRIP)]
+        area = held([P, len(first_units) + SHIFT, STRIP + HALF], F32, "logs")
+        views = [banks[0][:, :2]] + [bank[:] for bank in banks[1:-1]] + [in_strips(banks[-1], STRIP), banks[0][:, 2:]]
+        widths = [QUARTER] + [HALF] * 6
 
         def places_from(first):
-            rows = {n: shaped(area[:, first + k, :HALF], views[n]) for k, n in enumerate(order)}
-            return [rows[n] for n in range(len(order))] + [area[:, first : first + HALF // STRIP, HALF:]]
+            rows = {n: shaped(area[:, first + k, STRIP : STRIP + widths[n]], views[n]) for k, n in enumerate(order)}
+            return [rows[n] for n in range(len(order))] + [area[:, first : first + HALF // STRIP, :STRIP]]
 
-        places = places_from(0)
-        gate_places = places_from(SHIFT)
-        gate_places[order[-1]] = held([P, 1, HALF], F32, "last_gates")[:]
-        for place, view in zip(gate_places, views):
-            sigmoid(place, view)
+        places = places_from(0) + [shaped(area[:, SHIFT + 5, STRIP : STRIP + QUARTER], views[-1])]
+        gate_places = places_from(SHIFT) + [held([P, 2, BLOCK], F32, "last_gates")[:]]
+        for n in (0, 8, 1, 2, 3, 4, 5, 6, 7):
+            sigmoid(gate_places[n], views[n])
         for k in range(5):
-            logarithm(area[:, k, :], area[:, SHIFT + k, :])
-        logarithm(area[:, 5:8, HALF:], area[:, SHIFT + 5 :, HALF:])
-        for n in order[5:]:
+            span = slice(0, STRIP + widths[order[k]])
+            logarithm(area[:, k, span], area[:, SHIFT + k, span])
+        logarithm(area[:, 5:8, :STRIP], area[:, SHIFT + 5 :, :STRIP])
+        for n in order[5:] + (8,):
             logarithm(places[n], gate_places[n])
 
         aside_rounded = held([P, 3, PASS], BF16, "rounded_aside")
@@ -365,8 +364,10 @@ def tile_list_softplus_step_input_kernel(
         steps = held([P, PACK, S], F32, "steps")
         scaled = held([P, PACK, S], F32, "raw11")
         targets = [steps[:, s : s + slices, first : first + count] for s, slices, first, count in first_units]
-        targets[-1] = shaped(targets[-1][:, 0, :], places[-1])
-        for n in (0, 1, 2, 4, 5, 7, 3, 6):
+        targets[-1] = shaped(targets[-1][:, 0, :], places[7])
+        targets.append(targets[0][:, 2:])
+        targets[0] = targets[0][:, :2]
+        for n in (0, 1, 2, 4, 5, 7, 3, 6, 8):
             guard(targets[n], places[n], views[n])
         for half in (slice(0, HALF), slice(HALF, S)):
             nc.gpsimd.tensor_tensor(scaled[:, 0, half], steps[:, 0, half], early_factors[:, half], MULT)

@@ -180,7 +180,7 @@ def tile_list_softplus_step_input_kernel(
         early_factors = held([P, S], F32, "early_factors")
         nc.vector.tensor_copy(early_factors[:], factors[0][:].indirect(offsets[:]))
         quantise_wa(1, 0, 0, round_wa(1, 0, 0, PACK, nc.vector.tensor_copy, "rounded_wide"))
-        quantise_wa(1, 1, 0, round_wa(1, 1, 0, 1, nc.vector.tensor_copy, "rounded_narrow"))
+        quantise_wa(1, 1, 0, round_wa(1, 1, 0, 2, nc.vector.tensor_copy, "rounded_narrow"))
 
         wo_raw = []
 
@@ -231,17 +231,16 @@ def tile_list_softplus_step_input_kernel(
         def turned_sums(block, number):
             cols = slice(block * BLOCK, (block + 1) * BLOCK)
             bank = bank_tile(number, [P, PASS])
-            parts = ((0, 0, 0, PACK), (1, 0, 0, 1), (1, 1, 0, 1), (1, 1, 1, 2))
+            parts = ((0, 0, PACK), (1, 0, 2), (1, 2, 2))
             for part in parts:
-                a, first, skipped, slices = part
+                a, first, slices = part
                 codes, plane = wa_moving[1, a, first]
-                window = slice(skipped * P, (skipped + slices) * P)
                 nc.tensor.matmul_mx(
-                    out=bank[:, (first + skipped) * P : (first + skipped + slices) * P],
+                    out=bank[:, first * P : (first + slices) * P],
                     lhsT=picked[a][:, cols].bitcast(E4M3),
                     lhsT_scale=picked_planes[ROWS * a : P, cols],
-                    rhs=codes[:, window].bitcast(E4M3),
-                    rhs_scale=plane[:, window],
+                    rhs=codes[:].bitcast(E4M3),
+                    rhs_scale=plane[:],
                     start=part == parts[0],
                     stop=part == parts[-1],
                 )
@@ -351,11 +350,11 @@ def tile_list_softplus_step_input_kernel(
         for n in order[5:] + (8,):
             logarithm(places[n], gate_places[n])
 
-        aside_rounded = held([P, 3, PASS], BF16, "rounded_aside")
-        for t in range(3):
+        aside_rounded = held([P, 2, PASS], BF16, "rounded_aside")
+        for t in range(2):
             nc.gpsimd.tensor_scalar(
                 aside_rounded[:, t, :].rearrange("p (m e j) -> p m j e", e=RUN, j=PACK),
-                wa_raw[1, 1][:].rearrange("p j (m t e) -> p t m j e", t=PACK, e=RUN)[:, 1 + t],
+                wa_raw[1, 1][:].rearrange("p j (m t e) -> p t m j e", t=PACK, e=RUN)[:, 2 + t],
                 1.0,
                 0.0,
                 MULT,
@@ -371,7 +370,7 @@ def tile_list_softplus_step_input_kernel(
             guard(targets[n], places[n], views[n])
         for half in (slice(0, HALF), slice(HALF, S)):
             nc.gpsimd.tensor_tensor(scaled[:, 0, half], steps[:, 0, half], early_factors[:, half], MULT)
-        quantise_wa(1, 1, 1, aside_rounded[:].rearrange("p t c -> p (t c)"), "last_gates")
+        quantise_wa(1, 1, 2, aside_rounded[:].rearrange("p t c -> p (t c)"), "last_gates")
         for s, first, count in ((1, 0, S), (2, 0, S), (3, 0, HALF), (3, HALF, HALF)):
             cols = slice(first, first + count)
             scale_steps(scaled[:, s, cols], steps[:, s, cols], s, first, count)

@@ -35,7 +35,7 @@ BLOCK = 128
 FLOOR = 1e-12
 STRIP = 64
 LEAD = 4
-SHARE = 96
+SHARE = 48
 SHIFT = 3
 
 

from contextlib import ExitStack

import concourse.mybir as mybir
from concourse.masks import make_identity

K, T, S, H, N = 1024, 2048, 1024, 1024, 512
FLOPS = 2 * (2 * K * H * S + H * N * S)

F32 = mybir.dt.float32
BF16 = mybir.dt.bfloat16
I32 = mybir.dt.int32
U32 = mybir.dt.uint32
U16 = mybir.dt.uint16
U8 = mybir.dt.uint8
E4M3 = mybir.dt.float8_e4m3fn_x4
E2M1 = mybir.dt.float4_e2m1fn_x4
MULT = mybir.AluOpType.mult
ADD = mybir.AluOpType.add
MAX = mybir.AluOpType.max
SIGMOID = mybir.ActivationFunctionType.Sigmoid
LN = mybir.ActivationFunctionType.Ln
COPY = mybir.ActivationFunctionType.Copy
RELU = mybir.ActivationFunctionType.Relu

P = 128
PACK = 4
PASS = P * PACK
QUADRANT = 32
ROWS = 4
RUN = 4
LINE = 4
HALF = 512
QUARTER = 256
BLOCK = 128
FLOOR = 1e-12
STRIP = 64
LEAD = 4
SHARE = 48
SHIFT = 3


def tile_list_softplus_step_input_kernel(
    tc, tab_words, tab_scales, offs, wa, wb_words, wb_scales, wo, gT, out
):
    nc = tc.nc
    with ExitStack() as ctx:
        lists = ctx.enter_context(tc.tile_pool(name="lists", bufs=1))
        keep = ctx.enter_context(tc.tile_pool(name="keep", bufs=1))
        psum = ctx.enter_context(tc.psum_pool(name="psum", bufs=1))

        def held(shape, dtype, slot):
            return keep.tile(shape, dtype, name=slot, align_bytes=64)

        def bank_tile(number, shape):
            return psum.tile(shape, F32, name="bank%d" % number)

        offsets = lists.tile([P, S // 16], U16, name="offsets")
        nc.sync.dma_start(offsets[:], offs)

        def list_part(first, count):
            return offsets[:, first // 16 : (first + count) // 16]

        tab_planes = held([P, T], U8, "tab_planes")
        wb_planes = held([P, 2, H], U8, "wb_planes")
        moved_plane = held([P, S], U8, "moved_plane")
        nc.gpsimd.memset(tab_planes[:].bitcast(I32), 0)
        nc.vector.memset(wb_planes[:].rearrange("p a c -> p (a c)").bitcast(I32), 0)
        nc.vector.memset(moved_plane[:].bitcast(I32), 0)

        warm = held([P, 2], F32, "warm")
        nc.vector.memset(warm[:, 0:1], 0.0)
        nc.scalar.activation(warm[:, 1:2], warm[:, 0:1], SIGMOID)
        identity = held([P, P], F32, "identity")
        make_identity(nc, identity[:])

        def load_table(a):
            words = held([P, T], I32, "table%d" % a)
            nc.sync.dma_start(words[:], tab_words[a].rearrange("p t i -> p (t i)").bitcast(I32))
            return words

        wa_raw = {}

        def load_wa(b, a):
            wa_raw[b, a] = held([P, PACK, PASS], F32, "raw%d%d" % (b, a))
            rows = wa[a * PASS : (a + 1) * PASS, b * PASS : (b + 1) * PASS]
            nc.sync.dma_start(wa_raw[b, a][:], rows.rearrange("(p j) c -> p j c", j=PACK))

        g_rows = gT.rearrange("(b m t e) n -> b t m e n", b=2, t=PACK, e=RUN)
        wo_rows = wo.rearrange("(b m t e) n -> b t m e n", b=2, t=PACK, e=RUN)
        factors = {}

        def load_factors(s, slot):
            factors[s] = held([P, T], F32, slot)
            nc.sync.dma_start(factors[s][:], g_rows[s // PACK, s % PACK])

        for q in range(2):
            nc.sync.dma_start(
                tab_planes[QUADRANT * q : QUADRANT * q + 2 * ROWS, :].bitcast(I32),
                tab_scales[:, ROWS * q : ROWS * (q + 1), :].bitcast(I32),
            )
        for q in range(2, P // QUADRANT):
            for a in range(2):
                nc.sync.dma_start(
                    tab_planes[QUADRANT * q + ROWS * a : QUADRANT * q + ROWS * (a + 1), :].bitcast(I32),
                    tab_scales[a, ROWS * q : ROWS * (q + 1), :].bitcast(I32),
                )
        table = [load_table(0)]
        for a in range(2):
            load_wa(0, a)
        table.append(load_table(1))

        picked = [held([P, S], U32, "picked%d" % a) for a in range(2)]
        picked_planes = held([P, S], U8, "picked_planes")
        nc.vector.tensor_copy(picked_planes[:], tab_planes[:].indirect(offsets[:]))

        load_factors(0, "factors0")
        load_wa(1, 0)
        load_wa(1, 1)
        for r in range(ROWS):
            nc.sync.dma_start(
                wb_planes[r:P:QUADRANT, :, :].bitcast(I32),
                wb_scales.rearrange("a (q r) c -> r q a c", r=ROWS)[r].bitcast(I32),
            )
        wb_raw = {}

        def load_wb(b, slot):
            wb_raw[b] = held([P, 2, H // 4], I32, slot)
            nc.sync.dma_start(wb_raw[b][:], wb_words.rearrange("a p (b w) -> b p a w", b=2)[b].bitcast(I32))

        early_words = []
        for a, slot in enumerate(("rounded_aside", "steps")):
            early_words.append(held([P, H // 4], I32, slot))
            nc.sync.dma_start(early_words[a][:], wb_words[a, :, :H].bitcast(I32))
        load_factors(1, "factors1")
        load_wb(1, "wb_raw")
        for r in range(ROWS):
            nc.sync.dma_start(
                moved_plane[r:P:QUADRANT, :].bitcast(I32),
                picked_planes[ROWS + r : P : QUADRANT, :].bitcast(I32),
            )

        wa_quantised = {}
        wa_moving = {}

        def quantise(rounded, name, slot=None):
            width = rounded.shape[1] // PACK
            codes = held([P, width], U32, slot or name + "_codes")
            plane = held([P, width], U8, name + "_plane")
            nc.vector.quantize_mx(out=codes[:].bitcast(E4M3), scales=plane[:], in_=rounded)
            return codes, plane

        def round_wa(b, a, first, count, copy, slot):
            rounded = held([P, count * PASS], BF16, slot)[:] if isinstance(slot, str) else slot
            dealt = rounded.rearrange("p (t m e j) -> p m t j e", t=count, e=RUN, j=PACK)
            source = wa_raw[b, a][:].rearrange("p j (m t e) -> p m t j e", t=PACK, e=RUN)
            copy(dealt, source[:, :, first : first + count])
            return rounded

        def quantise_wa(b, a, first, rounded, slot=None):
            codes, plane = quantise(rounded, "wa%d%d%d" % (b, a, first), slot)
            wa_moving[b, a, first] = (codes, plane)
            for t in range(rounded.shape[1] // PASS):
                cols = slice(t * P, (t + 1) * P)
                wa_quantised[PACK * b + first + t, a] = (codes[:, cols], plane[:, cols])

        nc.vector.tensor_copy(picked[0][:], table[0][:].bitcast(U32).indirect(offsets[:]))
        for first, slot in ((0, "rounded_first"), (2, "rounded_wide")):
            quantise_wa(0, 0, first, round_wa(0, 0, first, 2, nc.scalar.copy, slot))
        early_pair = round_wa(0, 1, 0, 2, nc.scalar.copy, "rounded_narrow")
        late_pair = round_wa(0, 1, 2, 2, nc.vector.tensor_copy, "rounded_late")
        quantise_wa(0, 1, 0, early_pair)
        quantise_wa(0, 1, 2, late_pair)
        pieces = [(0, BLOCK), (BLOCK, BLOCK)] + [(first, QUARTER) for first in range(QUARTER, S, QUARTER)]
        for first, count in pieces:
            nc.vector.tensor_copy(
                picked[1][:, first : first + count],
                table[1][:].bitcast(U32).indirect(list_part(first, count)),
            )

        early_factors = held([P, S], F32, "early_factors")
        nc.vector.tensor_copy(early_factors[:], factors[0][:].indirect(offsets[:]))
        quantise_wa(1, 0, 0, round_wa(1, 0, 0, PACK, nc.vector.tensor_copy, "rounded_wide"))
        quantise_wa(1, 1, 0, round_wa(1, 1, 0, 2, nc.vector.tensor_copy, "rounded_narrow"))

        wo_raw = []

        def load_wo(b, slot):
            wo_raw.append(held([P, PACK, N], F32, slot))
            for t in range(PACK):
                nc.sync.dma_start(wo_raw[b][:, t, :], wo_rows[b, t])

        for s in (2, 3):
            load_factors(s, "factors%d" % s)
        load_wo(0, "raw00")
        load_factors(6, "factors0")
        load_wo(1, "wo_raw")
        for s, slot in zip((7, 4, 5), ("raw01", "raw10", "factors4")):
            load_factors(s, slot)

        wb_codes = {}
        wb_dealt_planes = {}

        def deal_planes(b, copy, dtype, place):
            wb_dealt_planes[b] = place.rearrange("p (a t m) -> p a t m", a=2, t=PACK)
            rows = wb_planes[:].bitcast(dtype).rearrange("p a (b q i t) -> p b a q t i", b=2, i=LINE, t=PACK)
            copy(wb_dealt_planes[b].rearrange("p a t (q i) -> p a q t i", i=LINE), rows[:, b])

        deal_planes(0, nc.vector.tensor_copy, I32, held([P, H // 4], I32, "wb_dealt_planes")[:])
        wb_codes[0] = held([P, 2, PACK, P // RUN, 2], I32, "wb_codes")
        for a in range(2):
            nc.vector.tensor_copy(wb_codes[0][:, a], early_words[a][:].rearrange("p (m t w) -> p t m w", t=PACK, w=2))

        def sums(unit, number, passes=(0, 1), bank=None):
            s, slices, first, count = unit
            bank = bank_tile(number, [P, slices, count]) if bank is None else bank
            cols = slice(first, first + count)
            for a, turn in passes if isinstance(passes[0], tuple) else zip(passes, range(2)):
                for k in range(slices):
                    codes, plane = wa_quantised[s + k, a]
                    nc.tensor.matmul_mx(
                        out=bank[:, k, :],
                        lhsT=codes.bitcast(E4M3),
                        lhsT_scale=plane,
                        rhs=picked[a][:, cols].bitcast(E4M3),
                        rhs_scale=picked_planes[ROWS * a : P, cols],
                        start=(turn, k) == (0, 0),
                        stop=(turn, k) == (1, slices - 1),
                    )
            return bank

        def turned_sums(block, number):
            cols = slice(block * BLOCK, (block + 1) * BLOCK)
            bank = bank_tile(number, [P, PASS])
            parts = ((0, 0, PACK), (1, 0, 2), (1, 2, 2))
            for part in parts:
                a, first, slices = part
                codes, plane = wa_moving[1, a, first]
                nc.tensor.matmul_mx(
                    out=bank[:, first * P : (first + slices) * P],
                    lhsT=picked[a][:, cols].bitcast(E4M3),
                    lhsT_scale=picked_planes[ROWS * a : P, cols],
                    rhs=codes[:].bitcast(E4M3),
                    rhs_scale=plane[:],
                    start=part == parts[0],
                    stop=part == parts[-1],
                )
            return bank

        def shaped(view, like):
            return view.rearrange("p (r c) -> p r c", r=like.shape[1])

        def in_strips(bank, strip):
            return bank[:].rearrange("p s n -> p (s n)").rearrange("p (r c) -> p r c", c=strip)

        def sigmoid(place, view):
            nc.scalar.activation(place, view, SIGMOID, scale=-1.0)

        def logarithm(place, gates):
            nc.scalar.activation(place, gates, LN, bias=FLOOR)

        def guard(target, logs, view):
            nc.vector.scalar_tensor_tensor(target, logs, -1.0, view, MULT, MAX)

        def scale_steps(target, steps, s, first, count):
            nc.vector.tensor_tensor(target, factors[s][:].indirect(list_part(first, count)), steps, MULT)

        def inputs_of(b, block, number):
            cols = slice(block * BLOCK, (block + 1) * BLOCK)
            bank = bank_tile(number, [P, PACK, BLOCK])
            for t in range(PACK):
                for a in range(2):
                    nc.tensor.matmul_mx(
                        out=bank[:, t, :],
                        lhsT=wb_codes[b][:, a, t].rearrange("p m w -> p (m w)").bitcast(E2M1),
                        lhsT_scale=wb_dealt_planes[b][:, a, t].bitcast(U8),
                        rhs=picked[a][:, cols].bitcast(E4M3),
                        rhs_scale=(picked_planes, moved_plane)[a][:, cols],
                        start=(a == 0),
                        stop=(a == 1),
                    )
            return bank

        h_rounded = [held([P, S, PACK], BF16, "table%d" % b) for b in range(2)]
        h_quantised = {}

        def finish(b, block, bank, scaled, first=0):
            tokens = slice(block * BLOCK + first, (block + 1) * BLOCK)
            nc.vector.tensor_tensor(
                h_rounded[b][:, tokens, :].rearrange("p (c i) t -> p c t i", i=LINE),
                bank[:, :, first:].rearrange("p t (c i) -> p c t i", i=LINE),
                scaled[:, :, first:].rearrange("p t (c i) -> p c t i", i=LINE),
                MULT,
            )

        def weave(bank, slot, count=BLOCK):
            woven = held([P, PACK, count], F32, slot)
            nc.scalar.copy(woven[:], bank[:, :, :count])
            return woven

        def finish_aside(b, block, woven, scaled):
            count = woven.shape[2]
            nc.gpsimd.tensor_tensor(
                h_rounded[b][:, block * BLOCK : block * BLOCK + count, :].rearrange("p (c i) t -> p c t i", i=LINE),
                woven[:].rearrange("p t (c i) -> p c t i", i=LINE),
                scaled[:, :, :count].rearrange("p t (c i) -> p c t i", i=LINE),
                MULT,
            )

        def quantise_h(b, first, count, slot=None):
            rounded = h_rounded[b][:, first * BLOCK : (first + count) * BLOCK, :].rearrange("p n t -> p (n t)")
            codes, plane = quantise(rounded, "h%d%d" % (b, first), slot)
            for block in range(first, first + count):
                h_quantised[b, block] = (codes, plane, (block - first) * BLOCK)

        def block_of(view, block):
            return view[:, :, block * BLOCK : (block + 1) * BLOCK]

        first_units = (
            (0, 4, 0, BLOCK),
            (0, 4, BLOCK, BLOCK),
            (0, 2, QUARTER, QUARTER),
            (2, 2, QUARTER, QUARTER),
            (0, 2, HALF, QUARTER),
            (0, 2, HALF + QUARTER, QUARTER),
            (3, 1, HALF, HALF),
            (2, 1, HALF, HALF),
        )
        numbers = (6, 0, 2, 7, 4, 5, 3, 1)
        banks = [sums(first_units[n], numbers[n], ((0, 0),)) for n in range(LEAD)]
        for n in range(LEAD):
            sums(first_units[n], numbers[n], ((1, 1),), banks[n])
        banks += [sums(first_units[n], numbers[n], (1, 0)) for n in range(LEAD, 8)]
        order = (0, 1, 2, 4, 5, 3, 6)
        area = held([P, len(first_units) + SHIFT, STRIP + HALF], F32, "logs")
        views = [banks[0][:, :2]] + [bank[:] for bank in banks[1:-1]] + [in_strips(banks[-1], STRIP), banks[0][:, 2:]]
        widths = [QUARTER] + [HALF] * 6

        def places_from(first):
            rows = {n: shaped(area[:, first + k, STRIP : STRIP + widths[n]], views[n]) for k, n in enumerate(order)}
            return [rows[n] for n in range(len(order))] + [area[:, first : first + HALF // STRIP, :STRIP]]

        places = places_from(0) + [shaped(area[:, SHIFT + 5, STRIP : STRIP + QUARTER], views[-1])]
        gate_places = places_from(SHIFT) + [held([P, 2, BLOCK], F32, "last_gates")[:]]
        for n in (0, 8, 1, 2, 3, 4, 5, 6, 7):
            sigmoid(gate_places[n], views[n])
        for k in range(5):
            span = slice(0, STRIP + widths[order[k]])
            logarithm(area[:, k, span], area[:, SHIFT + k, span])
        logarithm(area[:, 5:8, :STRIP], area[:, SHIFT + 5 :, :STRIP])
        for n in order[5:] + (8,):
            logarithm(places[n], gate_places[n])

        aside_rounded = held([P, 2, PASS], BF16, "rounded_aside")
        for t in range(2):
            nc.gpsimd.tensor_scalar(
                aside_rounded[:, t, :].rearrange("p (m e j) -> p m j e", e=RUN, j=PACK),
                wa_raw[1, 1][:].rearrange("p j (m t e) -> p t m j e", t=PACK, e=RUN)[:, 2 + t],
                1.0,
                0.0,
                MULT,
                ADD,
            )
        steps = held([P, PACK, S], F32, "steps")
        scaled = held([P, PACK, S], F32, "raw11")
        targets = [steps[:, s : s + slices, first : first + count] for s, slices, first, count in first_units]
        targets[-1] = shaped(targets[-1][:, 0, :], places[7])
        targets.append(targets[0][:, 2:])
        targets[0] = targets[0][:, :2]
        for n in (0, 1, 2, 4, 5, 7, 3, 6, 8):
            guard(targets[n], places[n], views[n])
        for half in (slice(0, HALF), slice(HALF, S)):
            nc.gpsimd.tensor_tensor(scaled[:, 0, half], steps[:, 0, half], early_factors[:, half], MULT)
        quantise_wa(1, 1, 2, aside_rounded[:].rearrange("p t c -> p (t c)"), "last_gates")
        for s, first, count in ((1, 0, S), (2, 0, S), (3, 0, HALF), (3, HALF, HALF)):
            cols = slice(first, first + count)
            scale_steps(scaled[:, s, cols], steps[:, s, cols], s, first, count)

        units = [(s, 1, 0, HALF) for s in (4, 6, 7, 5)]
        numbers = (0, 4, 5, 2)
        gates = held([P, 3, HALF], F32, "gates")
        late_gates = held([P, 3, HALF], F32, "late_gates")
        logs = held([P, 6, HALF], F32, "late_logs")
        gate_rows = (gates[:, 0, :], gates[:, 2, :], logs[:, 3, :], held([P, HALF], F32, "last_row")[:])
        log_places = (logs[:, 0, :], logs[:, 2, :], gates[:, 0, :], gates[:, 2, :])
        turned_gates = [late_gates[:, k, :] for k in range(3)] + [gates[:, 1, :]]
        turned_logs = [logs[:, 3 + k, :] for k in range(3)] + [logs[:, 1, :]]

        def pair(row):
            return row.rearrange("p (s n) -> p s n", s=1)

        banks = {}

        def held_sums(n):
            banks[n] = sums(units[n], numbers[n])
            sigmoid(pair(gate_rows[n]), banks[n][:])

        def passing_sums(k, number):
            nc.scalar.activation(turned_gates[k], turned_sums(PACK + k, number)[:], SIGMOID)

        held_sums(0)
        woven = [weave(inputs_of(0, 0, 4), "woven0")]
        held_sums(3)
        passing_sums(0, 7)
        for k, (copied, passing) in enumerate(((5, 3), (1, 6)), 1):
            woven.append(weave(inputs_of(0, k, copied), "woven%d" % k))
            passing_sums(k, passing)
        held_sums(1)
        own = {3: inputs_of(0, 3, 7)}
        woven.append(weave(own[3], "woven3", SHARE))
        held_sums(2)
        passing_sums(3, 1)
        gate_run = gates[:].rearrange("p r n -> p (r n)")
        log_run = logs[:, 0:3, :].rearrange("p r n -> p (r n)")
        for span in (slice(0, HALF + STRIP), slice(2 * HALF - STRIP, 3 * HALF)):
            logarithm(log_run[:, span], gate_run[:, span])
        for n in (2, 3):
            logarithm(log_places[n], gate_rows[n])
        late_wb = held([P, 3 * H // 4], U32, "last_row")
        wb_codes[1] = late_wb[:, : H // 2].rearrange("p (a t m w) -> p a t m w", a=2, t=PACK, w=2)
        nc.scalar.copy(wb_codes[1], wb_raw[1][:].bitcast(U32).rearrange("p a (m t w) -> p a t m w", t=PACK, w=2))
        deal_planes(1, nc.scalar.copy, U32, late_wb[:, H // 2 :])
        middle = slice(HALF + STRIP, 2 * HALF - STRIP)
        logarithm(log_run[:, middle], gate_run[:, middle])
        logarithm(logs[:, 3:, :], late_gates[:])

        for block, number in ((4, 3), (5, 6), (6, 1)):
            own[block] = inputs_of(0, block, number)
        for block in range(4):
            finish_aside(0, block, woven[block], block_of(scaled, block))
        finish(0, 3, own[3], block_of(scaled, 3), SHARE)
        own[7] = inputs_of(0, 7, 7)
        for block in range(4, 8):
            finish(0, block, own[block], block_of(scaled, block))
        steps = held([P, PACK, HALF], F32, "steps")
        for n, (s, slices, first, count) in enumerate(units):
            guard(steps[:, s - PACK : s - PACK + slices, first : first + count], pair(log_places[n]), banks[n][:])

        woven = weave(inputs_of(1, 0, 1), "woven0")
        late_steps = []

        def add_turned(bank, term, opens):
            for t in range(PACK):
                nc.tensor.matmul(
                    bank[:, t, :],
                    lhsT=term[:, t * P : (t + 1) * P],
                    rhs=identity[:],
                    is_transpose=True,
                    start=opens and t == 0,
                    stop=not opens and t == PACK - 1,
                )

        def steps_aside(first, slot, numbers, steps_slot):
            late_steps.append(held([P, PACK, QUARTER], F32, steps_slot))
            negated = held([P, 2, PASS], F32, slot)
            for n in range(2):
                nc.scalar.activation(negated[:, n, :], turned_sums(PACK + first + n, (3, 6)[n])[:], COPY, scale=-1.0)
            for n, number in enumerate(numbers):
                k = first + n
                bank = bank_tile(number, [P, PACK, BLOCK])
                add_turned(bank, turned_logs[k], True)
                add_turned(bank, negated[:, n, :], False)
                nc.scalar.activation(block_of(late_steps[first // 2], n), bank[:], RELU, scale=-1.0)

        steps_aside(0, "factors2", (0, 4), "factors1")
        late = {1 + n: inputs_of(1, 1 + n, number) for n, number in enumerate((7, 1, 5))}
        wo_rounded = held([P, 2, N, PACK], BF16, "factors2")
        for b in range(2):
            nc.scalar.copy(
                wo_rounded[:, b].rearrange("p (c i) t -> p c t i", i=LINE),
                wo_raw[b][:].rearrange("p t (c i) -> p c t i", i=LINE),
            )
        for block, number in ((4, 0), (5, 4)):
            late[block] = inputs_of(1, block, number)

        scaled = held([P, PACK, HALF], F32, "raw11")
        scale_steps(scaled[:, 2, :], steps[:, 2, :], 6, 0, HALF)
        quantise_h(0, 0, 8, "gates")
        for k, first, count in ((3, 0, HALF), (0, 0, HALF), (1, 0, QUARTER), (1, QUARTER, QUARTER)):
            cols = slice(first, first + count)
            scale_steps(scaled[:, k, cols], steps[:, k, cols], PACK + k, first, count)
        finish_aside(1, 0, woven, block_of(scaled, 0))
        for block in range(1, 4):
            finish(1, block, late[block], block_of(scaled, block))

        steps_aside(2, "last_negated", (7, 1), "wo_raw")

        def project(target, c, b, first, count, start, stop):
            rows = slice(b * N + c * P, b * N + (c + 1) * P)
            h_codes, h_plane, column = h_quantised[b, first]
            cols = slice(column, column + count * BLOCK)
            nc.tensor.matmul_mx(
                out=target,
                lhsT=wo_codes[:, rows].bitcast(E4M3),
                lhsT_scale=wo_plane[:, rows],
                rhs=h_codes[:, cols].bitcast(E4M3),
                rhs_scale=h_plane[:, cols],
                start=start,
                stop=stop,
            )

        out_rows = out.rearrange("(c p) s -> p c s", p=P)

        def emit(first, count, numbers, copies, slot, stores=1):
            cols = slice(first * BLOCK, (first + count) * BLOCK)
            share = (N // P) // len(numbers)
            result = held([P, N // P, count * BLOCK], F32, slot)
            banks = [bank_tile(number, [P, share, count * BLOCK]) for number in numbers]
            for b in range(2):
                for n, bank in enumerate(banks):
                    for c in range(share):
                        project(bank[:, c, :], n * share + c, b, first, count, (b, c) == (0, 0), (b, c) == (1, share - 1))
            banks_a_store = len(banks) // stores
            for n, bank in enumerate(banks):
                copies[n](result[:, n * share : (n + 1) * share, :], bank[:])
                if (n + 1) % banks_a_store == 0:
                    rows = slice((n + 1 - banks_a_store) * share, (n + 1) * share)
                    nc.sync.dma_start(out_rows[:, rows, cols], result[:, rows, :])

        tail = held([P, PACK, QUARTER], F32, "raw11")

        def scale_group(tail, first, count, column):
            for k in range(PACK):
                part = late_steps[(first - HALF) // QUARTER][:, k, first % QUARTER : first % QUARTER + count]
                scale_steps(tail[:, k, column : column + count], part, PACK + k, first, count)

        scalar_copies = (nc.scalar.copy, nc.scalar.copy)
        scale_group(tail, HALF, QUARTER, 0)
        wo_codes, wo_plane = quantise(wo_rounded[:].rearrange("p b n t -> p (b n t)"), "wo", "factors1")
        quantise_h(1, 0, 4)
        emit(0, 2, (3, 6), scalar_copies, "factors3")
        emit(2, 2, (7, 1), scalar_copies, "logs")
        for block, number in ((6, 2), (7, 5)):
            late[block] = inputs_of(1, block, number)
        for block in (4, 5):
            finish(1, block, late[block], block_of(tail, block - 4))
        tail = held([P, PACK, QUARTER], F32, "factors2")
        scale_group(tail, 6 * BLOCK, BLOCK, 0)
        quantise_h(1, 4, 2)
        emit(4, 2, (3, 6), scalar_copies, "raw00")
        finish(1, 6, late[6], block_of(tail, 0))
        scale_group(tail, 7 * BLOCK, BLOCK, BLOCK)
        quantise_h(1, 6, 1)
        emit(6, 1, (0,), scalar_copies, "early_factors")
        finish(1, 7, late[7], block_of(tail, 1))
        quantise_h(1, 7, 1)
        emit(7, 1, (4, 7, 1, 2), (nc.scalar.copy, nc.vector.tensor_copy) * 2, "rounded_wide", 2)
